import numpy as np, ml_dtypes
CORES = [40,41,42,43,44,45,46,47]
N = 8
import mx_ref
BF = ml_dtypes.bfloat16
def gcols(t, e):
    v = np.concatenate([t.reshape(8, 16, -1, 4), np.zeros((8, 16, 1, 4), BF)], axis=2)
    return np.ascontiguousarray(np.stack([v[g][:, e[g]] for g in range(8)])).reshape(128, -1)
def gpick(z, e):
    return np.concatenate([z[16 * g:16 * g + 16][:, e[g]] for g in range(8)])
def pick(q, e):
    c = np.concatenate([q[0].reshape(128, -1, 4), np.zeros((128, 1, 4), np.uint8)], axis=1); s = np.concatenate([q[1], np.ones((16, 1), np.uint8)], axis=1)
    return (np.ascontiguousarray(c[:, e].reshape(128, -1)), np.ascontiguousarray(s[:, e]))
def join(*qs):
    return (np.concatenate([q[0] for q in qs], axis=1), np.concatenate([q[1] for q in qs], axis=1))
def put(q, e, v):
    c, s = q[0].reshape(128, -1, 4).copy(), q[1].copy(); c[:, e] = v[0].reshape(128, -1, 4); s[:, e] = v[1]
    return (c.reshape(128, -1), s)
def pk(c, s):
    return (np.ascontiguousarray(c), mx_ref.live(s))
def emit(q):
    return q[0], q[1]
def packed(v, rng):
    q = [mx_ref.quantize(np.ascontiguousarray(v[r])) for r in range(N)]
    return np.stack([a for a, b in q]), np.stack([mx_ref.plane(b, rng) for a, b in q])
def values_of_codes():
    e, c = np.zeros((128, 128, 4), np.float32), np.zeros((128, 2, 4), np.uint8)
    e[np.arange(128), np.arange(128), 0] = 1
    c[:127, :, 0] = np.arange(256).reshape(2, 128).T[:127]
    return mx_ref.matmul(mx_ref.quantize(e.reshape(128, 512).astype(BF)), (c.reshape(128, 8), np.full((16, 2), 127, np.uint8))).T.reshape(-1).astype(np.float64)
CODE_VALUE, SCALE_VALUE = values_of_codes(), 2.0 ** (np.arange(256) - 127.0)
def decode(q):
    return (CODE_VALUE[q[0]].reshape(16, 8, -1, 4) * SCALE_VALUE[q[1]][:, None, :, None] + 0.0).reshape(128, -1).astype(np.float32)
def f(rng, *shape):
    return mx_ref.flush((rng.standard_normal(shape, dtype=np.float32) * np.exp2(rng.integers(-2, 3, shape[:-1] + (1,)))).astype(BF))
def wide(rng, *shape, cols=0):
    v = rng.standard_normal(shape, dtype=np.float32) * np.exp2(rng.integers(-12, 13, shape)).astype(np.float32)
    if cols: v *= np.repeat(np.exp2(rng.integers(-cols, cols + 1, shape[:-2] + (1, shape[-1] // 4))) * (rng.random(shape[:-2] + (1, shape[-1] // 4)) > 0.0625), 4, axis=-1).astype(np.float32)
    return mx_ref.flush(v.astype(BF))
C, R = 256, 3
DECIDE = np.flatnonzero(np.arange(128) % 16 < 8)
def partner(r, t):
    return r ^ (1 << t)
def parents(s):
    b = np.packbits(s.reshape(8 * N, 16, C)[:, :8] > 0, axis=1, bitorder="little")[:, 0].astype(np.int64)
    return b * np.arange(C) >> 8
def places(p):
    i, size = np.arange(len(p)), np.ones(p.shape, np.int64)
    for j in range(C - 1, 0, -1): size[i, p[:, j]] += size[:, j]
    place, free = np.zeros(p.shape, np.int64), np.ones(p.shape, np.int64)
    for j in range(1, C):
        place[:, j] = free[i, p[:, j]]
        free[i, p[:, j]] += size[:, j]
        free[:, j] = place[:, j] + 1
    return place
def highest(h, p):
    i = np.arange(len(p))
    for j in range(C - 1, 0, -1):
        k = p[:, j]
        h[i, :, k] = np.maximum(h[i, :, k], h[:, :, j])
    return h
def numbers_of(rng):
    return {"x": np.array(f(rng, N, 128, 4 * C)), "u": np.array(f(rng, N, 128, 512)), "v": np.array(f(rng, N, 128, 512))}
def weights(rng, w):
    c, p = packed(w, rng)
    return {"wc": c, "ws": p}
def setup_inputs(rng):
    return {**numbers_of(rng), **weights(rng, f(rng, N, 128, 2048))}
def setup_inputs_trees(rng):
    d = numbers_of(rng)
    x = d["x"].astype(np.float32).reshape(N, 8, 16, C, 4)
    w = np.array(f(rng, N, 128, 2048)).astype(np.float32).reshape(N, 8, 16, 4, 8, 16, 4)
    u = d["u"].reshape(N, 128, 128, 4)
    low = rng.permutation(N) < N // 2
    size, one = np.where(low, 2.0 ** -28, 1.0), np.where(low, 2.0 ** -30, 1.0)
    x[:, :, :8] = 0
    x[:, :, 8, :, 0] = 1
    w[:, :, :, :, :, :9] = 0
    for r in range(N):
        for g, k in enumerate(rng.permutation(8)):
            way = -1.0 if k == 1 or k == 3 and r % 2 else 1.0
            a = np.full((8, C), (-0.75, -0.75, 1.0, 0.0, 0.0, -4.0, 1.0, -1.0)[k])
            if k == 3: a = rng.choice([1.0, -0.75, -1.0, -4.0], (8, C))
            if k == 5: a[7] = 1
            if k == 6: a[0] = rng.choice([1.0, -4.0], C)
            x[r, g, :8, :, 0] = way * a * size[r]
            w[r, g, 8, 0, g, :8, 0] = 32 * way * size[r]
    u[:, :, DECIDE] = 0
    u[:, DECIDE, DECIDE, 0] = one.astype(np.float32).astype(BF)[:, None]
    return {"x": x.reshape(N, 128, 4 * C).astype(BF), "u": u.reshape(N, 128, 512), "v": d["v"], **weights(rng, w.reshape(N, 128, 2048).astype(BF))}
def setup_inputs_zeros(rng):
    d = numbers_of(rng)
    x = d["x"].reshape(N, 128, C, 4)
    for r in range(N):
        a = x[r][:, :5].copy()
        a[:, :2] = 0
        x[r] = a[:, rng.permutation(C) % 5]
    x[rng.integers(N)] = 0
    return {"x": x.reshape(N, 128, 4 * C), "u": d["u"], "v": d["v"], **weights(rng, f(rng, N, 128, 2048))}
def setup_inputs_huge(rng):
    d = numbers_of(rng)
    high = int(rng.integers(N))
    size = np.full(N, 0.25)
    size[high] = 1
    x = 2.0 ** 30 * (0.5 + 0.5 * rng.random((N, 8, 16, C, 4)))
    x[:, :, :8] *= size[:, None, None, None, None]
    x[high, :, 0, :, 0] = 2.0 ** 30
    c = np.stack([rng.permutation(C) % 2 * 2.0 - 1.0 for r in range(N)])
    x[:, :, :8, :, 2:] *= c[:, None, None, :, None]
    u = d["u"].reshape(N, 8, 16, 128, 4)
    a = 2.0 ** 30 * (0.75 + 0.25 * rng.random((N, 8, 8, 64, 2))) * rng.choice([-1.0, 1.0], (N, 1, 1, 64, 1))
    u[:, :, :, DECIDE] = 0
    u[:, :, :8, DECIDE, 2:] = a.astype(np.float32).astype(BF)
    w = np.zeros((N, 8, 16, 4, 8, 16, 4), np.float32)
    for g in range(8):
        for p in range(8):
            for b in range(2): w[:, g, p, b, g, p + 8, b] = -32
    return {"x": x.astype(np.float32).reshape(N, 128, 4 * C).astype(BF), "u": u.reshape(N, 128, 512), "v": d["v"], **weights(rng, w.reshape(N, 128, 2048).astype(BF))}
def setup_inputs_spread(rng):
    d = setup_inputs(rng)
    d["x"] = wide(rng, N, 128, 4 * C, cols=6)
    return d
def check_inputs(d):
    b = []
    for k in ("x", "u", "v"):
        a = np.abs(d[k].astype(np.float32))
        if not (np.isfinite(a).all() and ((a == 0) | (a >= 2.0 ** -30) & (a <= 2.0 ** 30)).all()): b.append("a value of " + k)
    if ((d["wc"] == 127) | (d["wc"] == 255)).any(): b.append("a code of wc that is no number")
    ends = np.tile(np.repeat(np.array([0.0, 2.0 ** -30, 2.0 ** 30, 0.0]), 4), (128, 1)).astype(BF)
    none, least, most = emit(mx_ref.quantize(ends))[1][0, :3]
    s = np.stack([mx_ref.live(p) for p in d["ws"]])
    if not ((s == none) | (s >= least) & (s <= most)).all(): b.append("a scale of ws")
    return b
def reference(x, u, v, wc, ws):
    qu = [mx_ref.quantize(u[r]) for r in range(N)]
    lay = [pk(wc[r], ws[r]) for r in range(N)]
    now = x
    for t in range(R):
        held = [mx_ref.quantize(now[r]) for r in range(N)]
        own = np.stack([decode(q).astype(BF) for q in held])
        p = parents(np.stack([mx_ref.matmul(qu[r], held[r]) for r in range(N)]))
        place = places(p)
        o, place = np.argsort(place, axis=1).reshape(N, 8, C), place.reshape(N, 8, C)
        sent = [mx_ref.quantize(gcols(own[r], o[r])) for r in range(N)]
        h = np.zeros((N, 128, C, 4), np.float32)
        for r in range(N):
            for b in range(4):
                z = mx_ref.matmul(pick(lay[r], np.arange(128 * b, 128 * b + 128)), sent[partner(r, t)]) * np.float32(0.03125)
                h[r, :, :, b] = gpick(z, place[r])
        m = highest(h.reshape(8 * N, 16, C, 4), p).reshape(N, 128, 4 * C)
        now = (own.astype(np.float32) + m).astype(BF)
    y, op = np.zeros((N, 128, C), np.float32), p.reshape(N, 8, C).astype(np.float32)
    oc, osc = np.zeros((N, 128, 4 * C), np.uint8), np.zeros((N, 16, C), np.uint8)
    for r in range(N):
        q = mx_ref.quantize(now[r])
        y[r] = mx_ref.matmul(mx_ref.quantize(v[r]), q)
        oc[r], osc[r] = emit(q)
    return {"y": y, "op": op, "oc": oc, "osc": osc}

@@ -1,0 +1,495 @@
+from concourse.mybir import dt, AluOpType as OP, ActivationFunctionType as AF, AxisListType
+
+C, R = 256, 3
+BIG = 1e29
+HOLD = 1024.0
+SF, PF, TOP = 1024, 2048, 3072
+
+SCRATCH = {
+    "ps": ("psum", [128, 4096], "float32"),
+    "xin": ("sbuf", [128, 1024], "bfloat16"), "uin": ("sbuf", [128, 512], "bfloat16"), "vin": ("sbuf", [128, 512], "bfloat16"),
+    "qu": ("sbuf", [128, 128], "float8_e4m3fn_x4"), "su": ("sbuf", [128, 128], "uint8"),
+    "qv": ("sbuf", [128, 128], "float8_e4m3fn_x4"), "sv": ("sbuf", [128, 128], "uint8"),
+    "qw": ("sbuf", [128, 512], "float8_e4m3fn_x4"), "sw": ("sbuf", [128, 512], "uint8"),
+    "et": ("sbuf", [128, 2048], "bfloat16"), "qe": ("sbuf", [128, 512], "float8_e4m3fn_x4"), "se": ("sbuf", [128, 512], "uint8"),
+    "ones": ("sbuf", [128, 512], "bfloat16"),
+    "xn": ("sbuf", [128, 1024], "bfloat16"), "tp": ("sbuf", [128, 1024], "bfloat16"), "bt": ("sbuf", [128, 1024], "bfloat16"),
+    "qf": ("sbuf", [128, 256], "float8_e4m3fn_x4"), "sf": ("sbuf", [128, 256], "uint8"),
+    "tab": ("sbuf", [128, 4096], "float32"), "etmp": ("sbuf", [128, 128], "float32"),
+    "m1": ("sbuf", [128, 1024], "float32"), "m2": ("sbuf", [128, 1024], "float32"),
+    "yo": ("sbuf", [128, 256], "float32"), "po": ("sbuf", [128, 256], "float32"),
+    "ci": ("sbuf", [128, 64], "int32"), "cf": ("sbuf", [128, 176], "float32"), "pw": ("sbuf", [128, 16], "float32"),
+    "posd": ("sbuf", [128, 256], "bfloat16"), "kd": ("sbuf", [128, 256], "bfloat16"), "kd2": ("sbuf", [128, 256], "bfloat16"),
+    "dmx": ("sbuf", [128, 256], "bfloat16"), "keep": ("sbuf", [128, 256], "bfloat16"), "jrow": ("sbuf", [128, 256], "bfloat16"),
+    "a0": ("sbuf", [128, 256], "float32"), "a1": ("sbuf", [128, 256], "float32"),
+    "mb": ("sbuf", [128, 256], "float32"), "exl": ("sbuf", [128, 16], "uint16"),
+    "r1": ("sbuf", [128, 256], "bfloat16"), "r2": ("sbuf", [128, 256], "bfloat16"), "r3": ("sbuf", [128, 256], "bfloat16"),
+    "z": ("sbuf", [128, 256], "bfloat16"), "j0": ("sbuf", [128, 256], "bfloat16"),
+    "ja": ("sbuf", [128, 256], "bfloat16"), "jb": ("sbuf", [128, 256], "bfloat16"),
+    "aa": ("sbuf", [128, 256], "float32"), "ab": ("sbuf", [128, 256], "float32"), "ac": ("sbuf", [128, 256], "float32"),
+    "ai": ("sbuf", [128, 256], "int32"),
+    "wa": ("sbuf", [128, 256], "bfloat16"), "wb": ("sbuf", [128, 256], "bfloat16"), "wd": ("sbuf", [128, 256], "bfloat16"),
+    "lst": ("sbuf", [128, 96], "uint16"), "rkl": ("sbuf", [128, 16], "uint16"), "pll": ("sbuf", [128, 16], "uint16"),
+    "sgl": ("sbuf", [128, 16], "uint16"), "idx": ("sbuf", [128, 64], "uint16"),
+    "p256": ("sbuf", [128, 256], "float32"), "key": ("sbuf", [128, 256], "float32"), "p1": ("sbuf", [128, 256], "float32"),
+    "junk": ("sbuf", [128, 4096], "bfloat16"),
+    "wf": ("sbuf", [128, 96], "float32"), "wi": ("sbuf", [128, 64], "int32"), "szw": ("sbuf", [128, 24], "int32"),
+    "msk": ("sbuf", [128, 1536], "int32"), "hm": ("sbuf", [128, 768], "float32"),
+    "psrt": ("sbuf", [128, 256], "float32"), "ssrt": ("sbuf", [128, 272], "bfloat16"), "cum": ("sbuf", [128, 256], "float32"),
+    "iw": ("sbuf", [128, 512], "float32"),
+}
+for _t in range(R + 1):
+    SCRATCH["qx%d" % _t] = ("sbuf", [128, 256], "float8_e4m3fn_x4")
+    SCRATCH["sx%d" % _t] = ("sbuf", [128, 256], "uint8")
+for _t in range(R):
+    SCRATCH["qp%d" % _t] = ("sbuf", [128, 256], "float8_e4m3fn_x4")
+    SCRATCH["sp%d" % _t] = ("sbuf", [128, 256], "uint8")
+    SCRATCH["ol%d" % _t] = ("sbuf", [128, 16], "uint16")
+    SCRATCH["lp%d" % _t] = ("sbuf", [128, 16], "uint16")
+
+SEMAPHORES = ["cv", "cs", "ct", "cg", "ldx", "ldu", "ldv", "ldw", "lds", "sent", "stored"] + \
+    ["aq%d" % t for t in range(R)] + ["al%d" % t for t in range(R)]
+COUNTER = {"v": "cv", "s": "cs", "t": "ct", "g": "cg"}
+
+
+def emit(g, T, ops):
+    queue = {"v": g.vector, "s": g.scalar, "t": g.tensor, "g": g, "y": g.sync}
+    touched, known, clock, waits, marked, seq = {}, {q: {} for q in queue}, [], [], set(), {}
+    for n, op in enumerate(ops):
+        q, line = op["q"], op["line"]
+        seq[line] = seq.get(line, 0) + 1
+        op["seq"] = seq[line]
+        deps = {}
+        for regs, writes in ((op["rd"], False), (op["wr"], True)):
+            for name, lo, hi in regs:
+                for a, b, m, w in touched.get(name, []):
+                    if a < hi and lo < b and (w or writes) and m != n:
+                        if ops[m]["seq"] > deps.get(ops[m]["line"], (0, 0))[0]:
+                            deps[ops[m]["line"]] = (ops[m]["seq"], m)
+        mine = []
+        if q is not None:
+            for ln, (s, m) in sorted(deps.items(), key=lambda e: -e[1][1]):
+                if known[q].get(ln, 0) < s:
+                    mine.append(m)
+                    marked.add(m)
+                    for k, val in clock[m].items():
+                        known[q][k] = max(known[q].get(k, 0), val)
+        waits.append(mine)
+        ck = dict(known[q]) if q is not None else {}
+        ck[line] = op["seq"]
+        clock.append(ck)
+        for regs, writes in ((op["rd"], False), (op["wr"], True)):
+            for name, lo, hi in regs:
+                old = touched.get(name, [])
+                if writes:
+                    old = [e for e in old if not (lo <= e[0] and e[1] <= hi)]
+                touched[name] = old + [(lo, hi, n, writes)]
+    count = {}
+    for n, op in enumerate(ops):
+        if op["token"] is None and n in marked:
+            count[op["q"]] = count.get(op["q"], 0) + 1
+            op["token"] = (COUNTER[op["q"]], count[op["q"]])
+            op["inc"] = (COUNTER[op["q"]], 1)
+    for n, op in enumerate(ops):
+        if op["q"] is None:
+            continue
+        e = queue[op["q"]]
+        for m in waits[n]:
+            e.wait_ge(T.sem[ops[m]["token"][0]], ops[m]["token"][1])
+        ins = op["fn"](e)
+        if op["inc"] is not None:
+            ins.then_inc(T.sem[op["inc"][0]], op["inc"][1])
+
+
+def rank_program(g, core, T, topo):
+    rank = T.rank_of(core)
+    if rank is None:
+        return
+    ops = []
+    totals = {"sent": 0, "stored": 0}
+
+    def A(name, lo=0, hi=None, step=1):
+        hi = T[name].shape[1] if hi is None else hi
+        if step < 0:
+            ap = T[name][:, hi - 1::-1] if lo == 0 else T[name][:, hi - 1:lo - 1:-1]
+        elif step == 1:
+            ap = T[name][:, lo:hi]
+        else:
+            ap = T[name][:, lo:hi:step]
+        if name == "ps":
+            return (ap, [], [(name, lo // 512 * 512, (hi + 511) // 512 * 512)])
+        return (ap, [(name, lo, hi)], [])
+
+    def part(view, *names):
+        return (view[0], [(k, 0, 1) for k in names], [])
+
+    def ind(win, off):
+        return (win[0].indirect(off[0]), win[1] + off[1], [])
+
+    def val(s):
+        return s[0] if isinstance(s, tuple) else s
+
+    def rec(q, fn, outs, ins, token=None, inc=None, line=None):
+        rd, wr = [], []
+        for o in outs:
+            wr += o[1] + o[2]
+        for i in ins:
+            if isinstance(i, tuple):
+                rd += i[1]
+                wr += i[2]
+        ops.append({"q": q, "fn": fn, "rd": rd, "wr": wr, "token": token, "inc": inc, "line": line or q})
+
+    def tt(o, a, b, op):
+        rec("v", lambda e: e.tensor_tensor(o[0], a[0], b[0], op), [o], [a, b])
+
+    def ts(o, a, s1, op0, s2=None, op1=None):
+        if op1 is None:
+            rec("v", lambda e: e.tensor_scalar(o[0], a[0], val(s1), None, op0), [o], [a, s1])
+        else:
+            rec("v", lambda e: e.tensor_scalar(o[0], a[0], val(s1), val(s2), op0, op1), [o], [a, s1, s2])
+
+    def cp(o, a):
+        rec("v", lambda e: e.tensor_copy(o[0], a[0]), [o], [a])
+
+    def total(o, a):
+        rec("v", lambda e: e.tensor_reduce(o[0], a[0], AxisListType.X, OP.add), [o], [a])
+
+    def scatter(win, off, a):
+        rec("v", lambda e: e.tensor_copy(win[0].indirect(off[0]), a[0]), [win], [off, a])
+
+    def fill(o, c):
+        rec("v", lambda e: e.memset(o[0], c), [o], [])
+
+    def scan(o, d0, d1, init, op0, op1):
+        rec("v", lambda e: e.tensor_tensor_scan(o[0], d0[0], d1[0], init, op0, op1), [o], [d0, d1])
+
+    def turn(o, a):
+        rec("v", lambda e: e.transpose(o[0], a[0]), [o], [a])
+
+    def quant(qn, sn, a):
+        rec("v", lambda e: e.quantize_mx(T[qn][:], T[sn][:], a[0]), [A(qn), A(sn)], [a])
+
+    def act(o, a, func, bias=None, scale=1.0, acc=None):
+        def fn(e):
+            kw = {}
+            if bias is not None:
+                kw["bias"] = val(bias)
+            if scale != 1.0:
+                kw["scale"] = scale
+            if acc is not None:
+                kw["accum_out"] = acc[0]
+            return e.activation(o[0], a[0], func, **kw)
+        rec("s", fn, [o] + ([acc] if acc is not None else []), [a, bias])
+
+    def mm(bank, wq, ws, b, xq, xs):
+        o, l, ls = A("ps", 512 * bank, 512 * bank + C), A(wq, 128 * b, 128 * b + 128), A(ws, 128 * b, 128 * b + 128)
+        rec("t", lambda e: e.matmul_mx(o[0], l[0], ls[0], T[xq][:], T[xs][:], True, True), [o], [l, ls, A(xq), A(xs)])
+
+    def iota(o, pattern, base, mult, small=False):
+        if small:
+            rec("g", lambda e: e.iota(o[0], pattern, base, mult, allow_small_or_imprecise_dtypes=True), [o], [])
+        else:
+            rec("g", lambda e: e.iota(o[0], pattern, base, mult), [o], [])
+
+    def load(q, name, dst, src, sem):
+        rec(q, lambda e: e.dma_start(dst, src), [A(name)], [], token=(sem, 16), inc=(sem, 16), line=sem)
+
+    def store(q, dst, src, name):
+        totals["stored"] += 16
+        rec(q, lambda e: e.dma_start(dst, src), [], [A(name)], token=("stored", 0), inc=("stored", 16), line="st%d" % totals["stored"])
+
+    def send(peer, dst, src, name, sem):
+        rid, pid = topo.addr(peer)[:2]
+        totals["sent"] += len(topo.engines(core, peer))
+        rec("g", lambda e: e.remote_dma(dst, src, T.sem[sem], T.sem.sent, pid, rid, topo.mask(core, peer)), [], [A(name)],
+            token=("sent", 0), line="tx%d" % totals["sent"])
+
+    def arrive(names, sem, n):
+        rec(None, None, [A(k) for k in names], [], token=(sem, n), line=sem)
+
+    def bank(b, n=C):
+        return A("ps", 512 * b, 512 * b + n)
+
+    load("y", "xin", T.xin[:], T.x[:], "ldx")
+    load("s", "uin", T.uin[:], T.u[:], "ldu")
+    load("y", "qw", T.qw[:].bitcast(dt.uint8), T.wc[:], "ldw")
+    load("y", "sw", T.sw[:], T.ws[:], "lds")
+    load("y", "vin", T.vin[:], T.v[:], "ldv")
+
+    i16, w2k, invk = A("cf", 0, 1), A("cf", 1, 2), A("cf", 2, 3)
+    jc, jw, radj, inv2m = A("cf", 16, 32), A("cf", 32, 48), A("cf", 48, 64), A("cf", 64, 70)
+    t16, u16, two, zero = A("cf", 80, 96), A("cf", 96, 112), A("cf", 112, 128), A("cf", 128, 144)
+    root, jw2 = A("cf", 144, 160), A("cf", 160, 176)
+    iota(A("ci", 16, 17), [[0, 1]], 0, 1)
+    iota(A("posd"), [[0, 16], [1, 16]], 0, 0, True)
+    iota(A("ci", 0, 16), [[32, 8], [0, 2]], 0, 0)
+    iota(A("ci", 32, 48), [[1, 16]], 0, 0)
+    iota(A("jrow"), [[1, 256]], 0, 0, True)
+    fill(two, 2.0)
+    fill(zero, 0.0)
+    fill(A("keep"), 1.0)
+    fill(A("z"), 0.0)
+    fill(A("ones"), 1.0)
+    fill(A("keep", 0, 256, 16), 0.0)
+    scan(t16, two, zero, 0.5, OP.mult, OP.add)
+    ts(A("ci", 17, 18), A("ci", 16, 17), 15, OP.bitwise_and)
+    ts(A("ci", 18, 19), A("ci", 16, 17), 31, OP.bitwise_and)
+    fill(A("cf", 88, 96), 0.0)
+    cp(i16, A("ci", 17, 18))
+    cp(A("cf", 3, 4), A("ci", 18, 19))
+    fill(two, 256.0)
+    ts(A("posd"), A("posd"), i16, OP.subtract)
+    ts(invk, i16, 15.0, OP.is_equal, 1.0 / HOLD, OP.max)
+    fill(A("cf", 112, 128, 3), 2.0 ** -15)
+    ts(A("dmx"), A("posd"), 0.0, OP.is_equal)
+    ts(A("kd"), A("posd"), 1.0, OP.is_equal, HOLD, OP.mult)
+    ts(A("kd2"), A("posd"), 2.0, OP.is_ge)
+    tt(u16, t16, A("dmx", 0, 16), OP.mult)
+    ts(jc, A("ci", 0, 16), A("cf", 3, 4), OP.add, 1.0 / 256, OP.mult)
+    scan(t16, A("keep", 1, 16 + 1), u16, 0.0, OP.mult, OP.add)
+    tt(A("kd"), A("kd"), A("kd2"), OP.add)
+    cp(w2k, A("cf", 94, 95))
+    cp(A("exl"), A("ci", 32, 48))
+    scan(A("pw"), two, zero, 2.0 ** 15, OP.mult, OP.add)
+    quant("qu", "su", A("uin"))
+    quant("qx0", "sx0", A("xin"))
+
+    def late_constants():
+        tt(A("a0"), ind(A("pw"), A("exl")), A("dmx"), OP.mult)
+        ts(jw, A("ci", 32, 48), 16.0, OP.mult, i16, OP.add)
+        fill(A("a0", 0, 1), 0.0)
+        fill(A("p256", 0, 1), 255.0)
+        ts(root, jw, 0.0, OP.is_equal)
+        ts(jw2, jw, 256.0, OP.add)
+        act(A("a1"), A("a0"), AF.Copy)
+        tt(jw2, jw2, root, OP.subtract)
+
+    def later_constants():
+        ts(radj, jw, 0.0, OP.is_equal, 256.0, OP.mult)
+        fill(two, 0.5)
+        fill(A("ssrt", 0, 16), 0.0)
+        ts(radj, radj, -1.0, OP.add)
+        scan(inv2m, A("cf", 112, 118), A("cf", 128, 134), 2.0, OP.mult, OP.add)
+        fill(A("p1", 0, 1), 255.0)
+
+    def unpackers():
+        for b in range(4):
+            o = A("et", 512 * b, 512 * b + 512)
+            rec("g", lambda e, o=o, b=b: e.affine_select(o[0], T.ones[:], [[1, 512]], OP.is_equal, 0.0, -b, -4), [o], [A("ones")])
+
+    def table_constants():
+        fill(A("mb"), BIG)
+        quant("qv", "sv", A("vin"))
+        fill(A("mb", 0, 256, 8), -BIG)
+
+    def wrap(row, *outs):
+        scan(A("r3"), A("kd"), row, 0.0, OP.mult, OP.max)
+        for o in outs:
+            ts(o, A("r3", 15, 256, 16), invk, OP.mult)
+
+    def spread(out):
+        scan(A("r2"), A("keep"), A("z"), 0.0, OP.mult, OP.add)
+        turn(out, A("r2"))
+
+    def L(k):
+        return A("lst", 16 * k, 16 * k + 16)
+
+    def sweep(name, between):
+        for a in range(32, 256, 32):
+            tt(A(name, a, a + 32), ind(A(name, 0, a), A("lst", 80 + a // 16, 82 + a // 16)), A(name, a, a + 32), OP.add)
+            if between is not None:
+                between(a)
+
+    def W(k, n=1):
+        return A("iw", 16 * k, 16 * (k + n))
+
+    for t in range(R):
+        peer = T.cores[rank ^ (1 << t)]
+        qx, sx, qp, sp, ol, lp = ["%s%d" % (k, t) for k in ("qx", "sx", "qp", "sp", "ol", "lp")]
+        engines = len(topo.engines(peer, core))
+        mm(4, "qu", "su", 0, qx, sx)
+        send(peer, T[qp][:].bitcast(dt.uint8), T[qx][:].bitcast(dt.uint8), qx, "aq%d" % t)
+        send(peer, T[sp][:], T[sx][:], sx, "aq%d" % t)
+        arrive([qp, sp], "aq%d" % t, 2 * engines)
+        if t == 0:
+            unpackers()
+            late_constants()
+        ts(A("r1"), bank(4), 0.0, OP.is_gt, w2k, OP.mult)
+        turn(A("r2"), A("r1"))
+        scan(A("r1"), A("keep"), A("r2"), 0.0, OP.mult, OP.add)
+        tt(A("wf", 0, 16), A("r1", 15, 256, 16), jc, OP.mult)
+        ts(A("wi", 0, 16), A("wf", 0, 16), -0.498046875, OP.add)
+        cp(A("z", 0, 256, 16), A("wi", 0, 16))
+        spread(A("j0"))
+        wrap(A("j0"), L(0), A("wi", 16, 32))
+        act(A("p256", 1, 256), A("j0", 1, 256), AF.Identity, bias=256.0, scale=256.0)
+        keyw, sg = A("wf", 16, 32), A("wf", 32, 48)
+        jn, an = ["j0", "ja", "jb", "ja", "jb", "ja"], ["a0", "aa", "ab", "aa", "ab", "aa"]
+        for k in range(5):
+            act(A(jn[k + 1]), ind(A(jn[k]), L(k)), AF.Copy)
+            tt(A(an[k + 1]), ind(A(an[k]), L(k)), A("ac" if k else "a1"), OP.add)
+            if k < 4:
+                act(A("ac"), A(an[k + 1]), AF.Copy)
+            wrap(A(jn[k + 1]), L(k + 1))
+            if k == 0:
+                ts(keyw, A("wi", 16, 32), 256.0, OP.mult)
+            if k == 1:
+                tt(keyw, keyw, jw2, OP.add)
+            if k == 2:
+                scan(A("key"), A("jrow"), A("p256"), 0.0, OP.min, OP.add)
+            if k == 3 and t == 0:
+                later_constants()
+        for k in range(16):
+            act(A("junk", 256 * k, 256 * k + 256), A("key"), AF.Sign, bias=A("wf", 16 + k, 17 + k), scale=-1.0, acc=A("wf", 32 + k, 33 + k))
+        sweep("aa", lambda a: cp(A("ai", a - 32, a), A("aa", a - 32, a)))
+        cp(A("ai", 224, 256), A("aa", 224, 256))
+        for m in range(7):
+            if m < 6:
+                ts(A("msk", 304 * m, 256 * m + 256), A("ai", 48 * m, 256), 0x010101 << m, OP.bitwise_and)
+            if m >= 1:
+                lo, n = 304 * (m - 1), 128 - 24 * (m - 1)
+                tt(A("hm", 128 * m - 128, 128 * m - 128 + n), A("msk", lo, lo + n), A("msk", lo + n, lo + 2 * n), OP.add)
+        for m in range(6):
+            total(A("wf", 48 + m, 49 + m), A("hm", 128 * m, 104 * m + 128))
+        tt(A("wi", 32, 38), A("wf", 48, 54), inv2m, OP.mult)
+        if t == 0:
+            quant("qe", "se", A("et"))
+        for f in range(3):
+            ts(A("szw", f, 18, 3), A("wi", 32, 38), 8 * f, OP.logical_shift_right, 255, OP.bitwise_and)
+        tt(A("z", 0, 256, 16), A("szw", 0, 16), root, OP.add)
+        spread(A("r1"))
+        wrap(A("r1"), A("z", 0, 256, 16))
+        spread(A("r1"))
+        ts(A("rkl"), sg, 255.0, OP.add, 0.5, OP.mult)
+        act(A("p1", 1, 256), A("j0", 1, 256), AF.Identity, bias=255.0, scale=256.0)
+        scatter(A("r2"), A("rkl"), A("jrow"))
+        wrap(A("r2"), A("sgl"))
+        act(A("psrt"), ind(A("p256"), A("sgl")), AF.Copy)
+        for b in range(4):
+            mm(b, "qe", "se", b, qp, sp)
+        for b in range(4):
+            act(A("tp", 256 * b, 256 * b + 256), bank(b), AF.Copy)
+        for b in range(4):
+            mm(b, "qe", "se", b, qx, sx)
+        if t == 0:
+            act(A("tab", TOP, 4096), A("junk", 0, 1024), AF.Copy)
+        if t == R - 1:
+            act(A("po"), A("j0"), AF.Copy)
+            store("y", T.op[:], T.po[0:128:16, :], "po")
+        cp(A("ssrt", 16, 272), ind(A("r1"), A("sgl")))
+        scan(A("cum"), A("ssrt", 15, 271), A("psrt"), 0.0, OP.add, OP.max)
+        tt(A("wa"), ind(A("cum"), A("rkl")), A("p1"), OP.subtract)
+        wn = ["wa", "wb"]
+        for k in range(5):
+            cp(A("wd"), A(wn[k % 2]))
+            tt(A(wn[(k + 1) % 2]), ind(A(wn[k % 2]), L(k)), A("wd"), OP.add)
+        sweep("wb", None)
+        wrap(A("wb"), A("pll"), W(0))
+        scatter(A("r1"), A("pll"), A("jrow"))
+        wrap(A("r1"), A(ol))
+        send(peer, T[lp][:], T[ol][:], ol, "al%d" % t)
+        arrive([lp], "al%d" % t, engines)
+        l, r, l8, r8 = W(0), W(1), W(2), W(3)
+        tt(W(4), A("szw", 0, 16), radj, OP.add)
+        ts(W(5), l, 1.0, OP.add)
+        tt(r, l, W(4), OP.add)
+        if t == 0:
+            table_constants()
+        ts(A("wi", 32, 64), W(0, 2), 0.125, OP.mult, -0.4375, OP.add)
+        tt(W(20), W(5), r, OP.min)
+        ts(W(6), r, -1.0, OP.add)
+        ts(W(2, 2), A("wi", 32, 64), 8.0, OP.mult)
+        tt(W(21), W(6), l, OP.max)
+        tt(W(7), r, l8, OP.subtract)
+        tt(W(8), l, r8, OP.subtract)
+        tt(W(9), l, l8, OP.subtract)
+        tt(W(10), r8, l8, OP.subtract)
+        ts(W(15), l8, float(TOP + 5), OP.add)
+        ts(W(11), W(7), 7.0, OP.is_ge, float(SF), OP.mult)
+        ts(W(12), W(8), 0.0, OP.is_le, float(PF), OP.mult)
+        ts(W(13), W(7), 4.0, OP.is_ge)
+        ts(W(14), W(9), 2.0, OP.is_le)
+        ts(W(16), W(10), 24.0, OP.is_ge, float(TOP - SF + 1), OP.mult)
+        ts(W(17), W(10), 24.0, OP.is_ge, float(TOP - SF + 1 - 8), OP.mult)
+        tt(W(15), W(15), W(20), OP.subtract)
+        tt(W(28, 2), W(0, 2), W(11, 2), OP.add)
+        tt(W(13), W(13), W(14), OP.mult)
+        tt(W(22, 2), W(2, 2), W(16, 2), OP.add)
+        for b in range(4):
+            o, win = part(A("bt", b, 1024, 4), "bt%d" % b), ind(A("tp", 256 * b, 256 * b + 256), A(lp))
+            if b % 2:
+                act(o, win, AF.Copy)
+            else:
+                cp(o, win)
+        quant("qf", "sf", part(A("bt"), "bt0", "bt1", "bt2", "bt3"))
+        ts(W(4), W(10), 40.0, OP.is_ge)
+        ts(W(5), W(10), 40.0, OP.is_ge, -15.0, OP.mult)
+        ts(W(6), W(10), 72.0, OP.is_ge)
+        ts(W(7), W(10), 72.0, OP.is_ge, -31.0, OP.mult)
+        ts(W(8), W(10), 136.0, OP.is_ge, float(SF + 8), OP.add)
+        ts(W(9), W(10), 136.0, OP.is_lt, 63.0, OP.mult)
+        tt(W(15), W(15), W(13), OP.mult)
+        tt(W(4, 2), W(4, 2), W(6, 2), OP.add)
+        tt(W(22, 2), W(22, 2), W(8, 2), OP.add)
+        ts(W(24), W(10), 16.0, OP.is_ge)
+        tt(W(20), W(20), W(15), OP.add)
+        ts(W(5), W(5), float(SF - 8 - 63), OP.add)
+        ts(W(25), W(10), 16.0, OP.is_ge)
+        tt(W(22, 2), W(22, 2), W(20, 2), OP.subtract)
+        for b in range(4):
+            mm(4 + b, "qw", "sw", b, "qf", "sf")
+        for b in range(4):
+            act(A("tab", 256 * b, 256 * b + 256), bank(4 + b), AF.Copy, scale=0.03125)
+
+        def suffix(b):
+            scan(A("tab", SF + 256 * b, SF + 256 * b + 256, -1), A("mb"), A("tab", 256 * b, 256 * b + 256, -1), -BIG, OP.min, OP.max)
+
+        def prefix(b):
+            scan(A("tab", PF + 256 * b, PF + 256 * b + 256), A("mb"), A("tab", 256 * b, 256 * b + 256), -BIG, OP.min, OP.max)
+
+        def top(k, lo, n):
+            base = SF if k == 0 else TOP + k
+            v = A("tab", base + 8 * lo, base + 8 * (lo + n - 1) + 1, 8)
+            return v if k == 0 else part(v, "top%d" % k)
+
+        tt(W(22, 2), W(22, 2), W(4, 2), OP.add)
+        suffix(0)
+        tt(W(22, 2), W(22, 2), W(24, 2), OP.mult)
+        suffix(1)
+        tt(W(30, 2), W(22, 2), W(20, 2), OP.add)
+        suffix(2)
+        cp(A("idx"), W(28, 4))
+        suffix(3)
+        prefix(0)
+        for b in range(4):
+            act(A("m1", 256 * b, 256 * b + 256), ind(A("tab", 256 * b, SF + 256 * b + 256), A("idx", 0, 16)), AF.Copy)
+        tt(top(1, 0, 127), top(0, 0, 127), top(0, 1, 127), OP.max)
+        tt(A("etmp"), A("tab", 2, 1024, 8), A("tab", 3, 1024, 8), OP.max)
+        tt(top(2, 0, 125), top(1, 0, 125), top(1, 2, 125), OP.max)
+        prefix(1)
+        tt(top(3, 0, 121), top(2, 0, 121), top(2, 4, 121), OP.max)
+        prefix(2)
+        tt(top(4, 0, 113), top(3, 0, 113), top(3, 8, 113), OP.max)
+        tt(top(5, 0, 128), A("etmp"), A("tab", 4, 1024, 8), OP.max)
+        prefix(3)
+        tops = [("top%d" % k, 0, 1) for k in range(1, 6)]
+        mn = ["m1", "m2", "m1", "m2"]
+        for s in range(1, 4):
+            for b in range(4):
+                win = A("tab", 256 * b, (PF if s == 1 else TOP) + 256 * b + 256)
+                if s > 1:
+                    win = (win[0], win[1] + tops, [])
+                tt(A(mn[s], 256 * b, 256 * b + 256), ind(win, A("idx", 16 * s, 16 * s + 16)), A(mn[s - 1], 256 * b, 256 * b + 256), OP.max)
+        for b in range(4):
+            tt(part(A("xn", b, 1024, 4), "xn%d" % b), bank(b), A("m2", 256 * b, 256 * b + 256), OP.add)
+        quant("qx%d" % (t + 1), "sx%d" % (t + 1), part(A("xn"), "xn0", "xn1", "xn2", "xn3"))
+
+    mm(4, "qv", "sv", 0, "qx3", "sx3")
+    store("y", T.oc[:], T.qx3[:].bitcast(dt.uint8), "qx3")
+    for k in range(4):
+        store("s", T.osc[4 * k:4 * k + 4, :], T.sx3[32 * k:32 * k + 4, :], "sx3")
+    cp(A("yo"), bank(4))
+    store("y", T.y[:], T.yo[:], "yo")
+    emit(g, T, ops)
+    g.sync.wait_ge(T.sem.stored, totals["stored"])
+    g.wait_ge(T.sem.sent, totals["sent"])

@@ -3,6 +3,7 @@ from concourse.mybir import dt, AluOpType as OP, ActivationFunctionType as AF, A
 C, R = 256, 3
 BIG = 1e29
 HOLD = 1024.0
+ROUND = 12582912.0
 SF, PF, TOP = 1024, 2048, 3072
 
 SCRATCH = {
@@ -21,9 +22,10 @@ SCRATCH = {
     "ci": ("sbuf", [128, 64], "int32"), "cf": ("sbuf", [128, 176], "float32"), "pw": ("sbuf", [128, 16], "float32"),
     "posd": ("sbuf", [128, 256], "bfloat16"), "kd": ("sbuf", [128, 256], "bfloat16"), "kd2": ("sbuf", [128, 256], "bfloat16"),
     "dmx": ("sbuf", [128, 256], "bfloat16"), "keep": ("sbuf", [128, 256], "bfloat16"), "jrow": ("sbuf", [128, 256], "bfloat16"),
-    "a0": ("sbuf", [128, 256], "float32"), "a1": ("sbuf", [128, 256], "float32"),
-    "mb": ("sbuf", [128, 256], "float32"), "exl": ("sbuf", [128, 16], "uint16"),
+    "a0": ("sbuf", [128, 256], "float32"), "a1": ("sbuf", [128, 256], "float32"), "dj": ("sbuf", [128, 256], "bfloat16"),
+    "mb": ("sbuf", [128, 512], "float32"), "exl": ("sbuf", [128, 16], "uint16"),
     "r1": ("sbuf", [128, 256], "bfloat16"), "r2": ("sbuf", [128, 256], "bfloat16"), "r3": ("sbuf", [128, 256], "bfloat16"),
+    "r4": ("sbuf", [128, 256], "bfloat16"), "r5": ("sbuf", [128, 256], "bfloat16"), "xs": ("sbuf", [128, 256], "float32"),
     "z": ("sbuf", [128, 256], "bfloat16"), "j0": ("sbuf", [128, 256], "bfloat16"),
     "ja": ("sbuf", [128, 256], "bfloat16"), "jb": ("sbuf", [128, 256], "bfloat16"),
     "aa": ("sbuf", [128, 256], "float32"), "ab": ("sbuf", [128, 256], "float32"), "ac": ("sbuf", [128, 256], "float32"),
@@ -166,8 +168,8 @@ def rank_program(g, core, T, topo):
     def turn(o, a):
         rec("v", lambda e: e.transpose(o[0], a[0]), [o], [a])
 
-    def quant(qn, sn, a):
-        rec("v", lambda e: e.quantize_mx(T[qn][:], T[sn][:], a[0]), [A(qn), A(sn)], [a])
+    def quant(q, s, a):
+        rec("v", lambda e: e.quantize_mx(q[0], s[0], a[0]), [q, s], [a])
 
     def act(o, a, func, bias=None, scale=1.0, acc=None):
         def fn(e):
@@ -216,61 +218,67 @@ def rank_program(g, core, T, topo):
     load("y", "sw", T.sw[:], T.ws[:], "lds")
     load("y", "vin", T.vin[:], T.v[:], "ldv")
 
-    i16, w2k, invk = A("cf", 0, 1), A("cf", 1, 2), A("cf", 2, 3)
-    jc, jw, radj, inv2m = A("cf", 16, 32), A("cf", 32, 48), A("cf", 48, 64), A("cf", 64, 70)
-    t16, u16, two, zero = A("cf", 80, 96), A("cf", 96, 112), A("cf", 112, 128), A("cf", 128, 144)
-    root, jw2 = A("cf", 144, 160), A("cf", 160, 176)
+    i16, cut8, invk = A("cf", 0, 1), A("cf", 1, 2), A("cf", 2, 3)
+    jw, radj, inv2m = A("cf", 32, 48), A("cf", 48, 64), A("cf", 64, 70)
+    two, zero, root, jw2 = A("cf", 112, 128), A("cf", 128, 144), A("cf", 144, 160), A("cf", 160, 176)
     iota(A("ci", 16, 17), [[0, 1]], 0, 1)
     iota(A("posd"), [[0, 16], [1, 16]], 0, 0, True)
     iota(A("ci", 0, 16), [[32, 8], [0, 2]], 0, 0)
     iota(A("ci", 32, 48), [[1, 16]], 0, 0)
     iota(A("jrow"), [[1, 256]], 0, 0, True)
-    fill(two, 2.0)
-    fill(zero, 0.0)
+    fill(A("dj"), 0.5)
     fill(A("keep"), 1.0)
     fill(A("z"), 0.0)
     fill(A("ones"), 1.0)
-    fill(A("keep", 0, 256, 16), 0.0)
-    scan(t16, two, zero, 0.5, OP.mult, OP.add)
     ts(A("ci", 17, 18), A("ci", 16, 17), 15, OP.bitwise_and)
     ts(A("ci", 18, 19), A("ci", 16, 17), 31, OP.bitwise_and)
-    fill(A("cf", 88, 96), 0.0)
+    fill(two, 256.0)
+    fill(zero, 0.0)
     cp(i16, A("ci", 17, 18))
     cp(A("cf", 3, 4), A("ci", 18, 19))
-    fill(two, 256.0)
-    ts(A("posd"), A("posd"), i16, OP.subtract)
-    ts(invk, i16, 15.0, OP.is_equal, 1.0 / HOLD, OP.max)
+    fill(A("keep", 0, 256, 16), 0.0)
+    fill(A("dj", 0, 256, 16), 0.0)
     fill(A("cf", 112, 128, 3), 2.0 ** -15)
-    ts(A("dmx"), A("posd"), 0.0, OP.is_equal)
+    ts(cut8, i16, -1.0, OP.mult, 8.0, OP.add)
+    fill(A("dj", 9, 256, 16), 1.0)
+    ts(A("posd"), A("posd"), i16, OP.subtract)
+    ts(cut8, cut8, 1.0, OP.min, -0.498046875, OP.max)
+    ts(A("dj", 8, 256, 16), A("ci", 0, 16), A("cf", 3, 4), OP.add, 0.5, OP.mult)
     ts(A("kd"), A("posd"), 1.0, OP.is_equal, HOLD, OP.mult)
     ts(A("kd2"), A("posd"), 2.0, OP.is_ge)
-    tt(u16, t16, A("dmx", 0, 16), OP.mult)
-    ts(jc, A("ci", 0, 16), A("cf", 3, 4), OP.add, 1.0 / 256, OP.mult)
-    scan(t16, A("keep", 1, 16 + 1), u16, 0.0, OP.mult, OP.add)
-    tt(A("kd"), A("kd"), A("kd2"), OP.add)
-    cp(w2k, A("cf", 94, 95))
-    cp(A("exl"), A("ci", 32, 48))
+    quant(A("qu"), A("su"), A("uin"))
+    quant(A("qx0"), A("sx0"), A("xin"))
+    ts(A("dmx"), A("posd"), 0.0, OP.is_equal)
     scan(A("pw"), two, zero, 2.0 ** 15, OP.mult, OP.add)
-    quant("qu", "su", A("uin"))
-    quant("qx0", "sx0", A("xin"))
+    cp(A("exl"), A("ci", 32, 48))
+    ts(invk, i16, 15.0, OP.is_equal, 1.0 / HOLD, OP.max)
 
-    def late_constants():
-        tt(A("a0"), ind(A("pw"), A("exl")), A("dmx"), OP.mult)
-        ts(jw, A("ci", 32, 48), 16.0, OP.mult, i16, OP.add)
-        fill(A("a0", 0, 1), 0.0)
-        fill(A("p256", 0, 1), 255.0)
-        ts(root, jw, 0.0, OP.is_equal)
-        ts(jw2, jw, 256.0, OP.add)
-        act(A("a1"), A("a0"), AF.Copy)
-        tt(jw2, jw2, root, OP.subtract)
+    def late_constants(step):
+        if step == 0:
+            tt(A("kd"), A("kd"), A("kd2"), OP.add)
+        if step == 1:
+            tt(A("a0"), ind(A("pw"), A("exl")), A("dmx"), OP.mult)
+        if step == 2:
+            ts(jw, A("ci", 32, 48), 16.0, OP.mult, i16, OP.add)
+            fill(A("a0", 0, 1), 0.0)
+        if step == 3:
+            fill(A("p256", 0, 1), 255.0)
+            act(A("a1"), A("a0"), AF.Copy)
+            ts(root, jw, 0.0, OP.is_equal)
+        if step == 4:
+            ts(jw2, jw, 256.0, OP.add)
+        if step == 5:
+            tt(jw2, jw2, root, OP.subtract)
 
-    def later_constants():
-        ts(radj, jw, 0.0, OP.is_equal, 256.0, OP.mult)
-        fill(two, 0.5)
-        fill(A("ssrt", 0, 16), 0.0)
-        ts(radj, radj, -1.0, OP.add)
-        scan(inv2m, A("cf", 112, 118), A("cf", 128, 134), 2.0, OP.mult, OP.add)
-        fill(A("p1", 0, 1), 255.0)
+    def later_constants(step):
+        if step == 2:
+            ts(radj, root, 256.0, OP.mult, -1.0, OP.add)
+            fill(two, 0.5)
+        if step == 3:
+            fill(A("ssrt", 0, 16), 0.0)
+            scan(inv2m, A("cf", 112, 118), A("cf", 128, 134), 2.0, OP.mult, OP.add)
+        if step == 4:
+            fill(A("p1", 0, 1), 255.0)
 
     def unpackers():
         for b in range(4):
@@ -279,26 +287,20 @@ def rank_program(g, core, T, topo):
 
     def table_constants():
         fill(A("mb"), BIG)
-        quant("qv", "sv", A("vin"))
-        fill(A("mb", 0, 256, 8), -BIG)
+        quant(A("qv"), A("sv"), A("vin"))
+        fill(A("mb", 0, 512, 8), -BIG)
 
-    def wrap(row, *outs):
+    def wrap(row, out):
         scan(A("r3"), A("kd"), row, 0.0, OP.mult, OP.max)
-        for o in outs:
-            ts(o, A("r3", 15, 256, 16), invk, OP.mult)
-
-    def spread(out):
-        scan(A("r2"), A("keep"), A("z"), 0.0, OP.mult, OP.add)
-        turn(out, A("r2"))
+        ts(out, A("r3", 15, 256, 16), invk, OP.mult)
 
     def L(k):
         return A("lst", 16 * k, 16 * k + 16)
 
-    def sweep(name, between):
+    def sweep(name, between, last):
         for a in range(32, 256, 32):
-            tt(A(name, a, a + 32), ind(A(name, 0, a), A("lst", 80 + a // 16, 82 + a // 16)), A(name, a, a + 32), OP.add)
-            if between is not None:
-                between(a)
+            tt(A(name if a < 224 else last, a, a + 32), ind(A(name, 0, a), A("lst", 80 + a // 16, 82 + a // 16)), A(name, a, a + 32), OP.add)
+            between(a)
 
     def W(k, n=1):
         return A("iw", 16 * k, 16 * (k + n))
@@ -313,15 +315,20 @@ def rank_program(g, core, T, topo):
         arrive([qp, sp], "aq%d" % t, 2 * engines)
         if t == 0:
             unpackers()
-            late_constants()
-        ts(A("r1"), bank(4), 0.0, OP.is_gt, w2k, OP.mult)
+        late = late_constants if t == 0 else (lambda step: None)
+        ts(A("r1"), bank(4), 0.0, OP.is_gt, cut8, OP.min)
+        late(0)
         turn(A("r2"), A("r1"))
-        scan(A("r1"), A("keep"), A("r2"), 0.0, OP.mult, OP.add)
-        tt(A("wf", 0, 16), A("r1", 15, 256, 16), jc, OP.mult)
-        ts(A("wi", 0, 16), A("wf", 0, 16), -0.498046875, OP.add)
-        cp(A("z", 0, 256, 16), A("wi", 0, 16))
-        spread(A("j0"))
-        wrap(A("j0"), L(0), A("wi", 16, 32))
+        late(1)
+        scan(A("xs"), A("dj"), A("r2"), 0.0, OP.mult, OP.add)
+        late(2)
+        ts(A("z", 0, 256, 16), A("xs", 9, 256, 16), ROUND, OP.add, ROUND, OP.subtract)
+        late(3)
+        scan(A("r2"), A("keep"), A("z"), 0.0, OP.mult, OP.add)
+        late(4)
+        turn(A("j0"), A("r2"))
+        late(5)
+        wrap(A("j0"), L(0))
         act(A("p256", 1, 256), A("j0", 1, 256), AF.Identity, bias=256.0, scale=256.0)
         keyw, sg = A("wf", 16, 32), A("wf", 32, 48)
         jn, an = ["j0", "ja", "jb", "ja", "jb", "ja"], ["a0", "aa", "ab", "aa", "ab", "aa"]
@@ -330,19 +337,26 @@ def rank_program(g, core, T, topo):
             tt(A(an[k + 1]), ind(A(an[k]), L(k)), A("ac" if k else "a1"), OP.add)
             if k < 4:
                 act(A("ac"), A(an[k + 1]), AF.Copy)
-            wrap(A(jn[k + 1]), L(k + 1))
+            scan(A("r3"), A("kd"), A(jn[k + 1]), 0.0, OP.mult, OP.max)
             if k == 0:
-                ts(keyw, A("wi", 16, 32), 256.0, OP.mult)
+                ts(keyw, L(0), 256.0, OP.mult)
             if k == 1:
                 tt(keyw, keyw, jw2, OP.add)
-            if k == 2:
+            if t == 0:
+                later_constants(k)
+            ts(L(k + 1), A("r3", 15, 256, 16), invk, OP.mult)
+
+        def beside_bits(a):
+            if a == 32:
                 scan(A("key"), A("jrow"), A("p256"), 0.0, OP.min, OP.add)
-            if k == 3 and t == 0:
-                later_constants()
+            if a == 96:
+                cp(A("ai", 0, 96), A("aa", 0, 96))
+            if a in (160, 224):
+                cp(A("ai", a - 64, a), A("aa", a - 64, a))
+
+        sweep("aa", beside_bits, "ai")
         for k in range(16):
             act(A("junk", 256 * k, 256 * k + 256), A("key"), AF.Sign, bias=A("wf", 16 + k, 17 + k), scale=-1.0, acc=A("wf", 32 + k, 33 + k))
-        sweep("aa", lambda a: cp(A("ai", a - 32, a), A("aa", a - 32, a)))
-        cp(A("ai", 224, 256), A("aa", 224, 256))
         for m in range(7):
             if m < 6:
                 ts(A("msk", 304 * m, 256 * m + 256), A("ai", 48 * m, 256), 0x010101 << m, OP.bitwise_and)
@@ -352,19 +366,39 @@ def rank_program(g, core, T, topo):
         for m in range(6):
             total(A("wf", 48 + m, 49 + m), A("hm", 128 * m, 104 * m + 128))
         tt(A("wi", 32, 38), A("wf", 48, 54), inv2m, OP.mult)
-        if t == 0:
-            quant("qe", "se", A("et"))
         for f in range(3):
-            ts(A("szw", f, 18, 3), A("wi", 32, 38), 8 * f, OP.logical_shift_right, 255, OP.bitwise_and)
-        tt(A("z", 0, 256, 16), A("szw", 0, 16), root, OP.add)
-        spread(A("r1"))
-        wrap(A("r1"), A("z", 0, 256, 16))
-        spread(A("r1"))
+            ts(part(A("szw", f, 18, 3), "sz%d" % f), A("wi", 32, 38), 8 * f, OP.logical_shift_right, 255, OP.bitwise_and)
+        size = part(A("szw", 0, 16), "sz0", "sz1", "sz2")
+        tt(A("z", 0, 256, 16), size, root, OP.add)
+        scan(A("r2"), A("keep"), A("z"), 0.0, OP.mult, OP.add)
+        tt(W(4), size, radj, OP.add)
+        turn(A("r1"), A("r2"))
         ts(A("rkl"), sg, 255.0, OP.add, 0.5, OP.mult)
+        scan(A("r3"), A("kd"), A("r1"), 0.0, OP.mult, OP.max)
+        scatter(A("r4"), A("rkl"), A("jrow"))
+        ts(A("z", 0, 256, 16), A("r3", 15, 256, 16), invk, OP.mult)
         act(A("p1", 1, 256), A("j0", 1, 256), AF.Identity, bias=255.0, scale=256.0)
-        scatter(A("r2"), A("rkl"), A("jrow"))
-        wrap(A("r2"), A("sgl"))
+        scan(A("r5"), A("kd"), A("r4"), 0.0, OP.mult, OP.max)
+        scan(A("r2"), A("keep"), A("z"), 0.0, OP.mult, OP.add)
+        ts(A("sgl"), A("r5", 15, 256, 16), invk, OP.mult)
+        turn(A("r1"), A("r2"))
         act(A("psrt"), ind(A("p256"), A("sgl")), AF.Copy)
+        ts(W(5), W(4), 1.0, OP.min)
+        cp(A("ssrt", 16, 272), ind(A("r1"), A("sgl")))
+        ts(W(6), W(4), 1.0, OP.min, -1.0, OP.mult)
+        scan(A("cum"), A("ssrt", 15, 271), A("psrt"), 0.0, OP.add, OP.max)
+        tt(A("wa"), ind(A("cum"), A("rkl")), A("p1"), OP.subtract)
+        wn = ["wa", "wb"]
+        for k in range(5):
+            cp(A("wd"), A(wn[k % 2]))
+            tt(A(wn[(k + 1) % 2]), ind(A(wn[k % 2]), L(k)), A("wd"), OP.add)
+
+        def beside_places(a):
+            b = a // 32 - 1
+            if t == 0 and b < 4:
+                quant(A("qe", 128 * b, 128 * b + 128), A("se", 128 * b, 128 * b + 128), A("et", 512 * b, 512 * b + 512))
+
+        sweep("wb", beside_places, "wb")
         for b in range(4):
             mm(b, "qe", "se", b, qp, sp)
         for b in range(4):
@@ -376,30 +410,20 @@ def rank_program(g, core, T, topo):
         if t == R - 1:
             act(A("po"), A("j0"), AF.Copy)
             store("y", T.op[:], T.po[0:128:16, :], "po")
-        cp(A("ssrt", 16, 272), ind(A("r1"), A("sgl")))
-        scan(A("cum"), A("ssrt", 15, 271), A("psrt"), 0.0, OP.add, OP.max)
-        tt(A("wa"), ind(A("cum"), A("rkl")), A("p1"), OP.subtract)
-        wn = ["wa", "wb"]
-        for k in range(5):
-            cp(A("wd"), A(wn[k % 2]))
-            tt(A(wn[(k + 1) % 2]), ind(A(wn[k % 2]), L(k)), A("wd"), OP.add)
-        sweep("wb", None)
-        wrap(A("wb"), A("pll"), W(0))
+        wrap(A("wb"), A("pll"))
         scatter(A("r1"), A("pll"), A("jrow"))
-        wrap(A("r1"), A(ol))
+        l, r, l8, r8 = W(0), W(1), W(2), W(3)
+        cp(l, A("pll"))
+        scan(A("r3"), A("kd"), A("r1"), 0.0, OP.mult, OP.max)
+        tt(r, l, W(4), OP.add)
+        ts(A(ol), A("r3", 15, 256, 16), invk, OP.mult)
         send(peer, T[lp][:], T[ol][:], ol, "al%d" % t)
         arrive([lp], "al%d" % t, engines)
-        l, r, l8, r8 = W(0), W(1), W(2), W(3)
-        tt(W(4), A("szw", 0, 16), radj, OP.add)
-        ts(W(5), l, 1.0, OP.add)
-        tt(r, l, W(4), OP.add)
+        ts(A("wi", 32, 64), W(0, 2), 0.125, OP.mult, -0.4375, OP.add)
+        tt(W(20, 2), W(0, 2), W(5, 2), OP.add)
         if t == 0:
             table_constants()
-        ts(A("wi", 32, 64), W(0, 2), 0.125, OP.mult, -0.4375, OP.add)
-        tt(W(20), W(5), r, OP.min)
-        ts(W(6), r, -1.0, OP.add)
         ts(W(2, 2), A("wi", 32, 64), 8.0, OP.mult)
-        tt(W(21), W(6), l, OP.max)
         tt(W(7), r, l8, OP.subtract)
         tt(W(8), l, r8, OP.subtract)
         tt(W(9), l, l8, OP.subtract)
@@ -415,63 +439,61 @@ def rank_program(g, core, T, topo):
         tt(W(28, 2), W(0, 2), W(11, 2), OP.add)
         tt(W(13), W(13), W(14), OP.mult)
         tt(W(22, 2), W(2, 2), W(16, 2), OP.add)
+        ts(W(4), W(10), 40.0, OP.is_ge)
+        ts(W(5), W(10), 40.0, OP.is_lt, 15.0, OP.mult)
+        ts(W(6), W(10), 72.0, OP.is_ge, float(SF + 8), OP.add)
         for b in range(4):
             o, win = part(A("bt", b, 1024, 4), "bt%d" % b), ind(A("tp", 256 * b, 256 * b + 256), A(lp))
             if b % 2:
                 act(o, win, AF.Copy)
             else:
                 cp(o, win)
-        quant("qf", "sf", part(A("bt"), "bt0", "bt1", "bt2", "bt3"))
-        ts(W(4), W(10), 40.0, OP.is_ge)
-        ts(W(5), W(10), 40.0, OP.is_ge, -15.0, OP.mult)
-        ts(W(6), W(10), 72.0, OP.is_ge)
-        ts(W(7), W(10), 72.0, OP.is_ge, -31.0, OP.mult)
-        ts(W(8), W(10), 136.0, OP.is_ge, float(SF + 8), OP.add)
+        quant(A("qf"), A("sf"), part(A("bt"), "bt0", "bt1", "bt2", "bt3"))
+        ts(W(7), W(10), 72.0, OP.is_lt, 31.0, OP.mult)
+        ts(W(8), W(10), 136.0, OP.is_ge)
         ts(W(9), W(10), 136.0, OP.is_lt, 63.0, OP.mult)
         tt(W(15), W(15), W(13), OP.mult)
+        ts(W(23), W(23), float(SF - 8 - 15 - 31 - 63), OP.add)
         tt(W(4, 2), W(4, 2), W(6, 2), OP.add)
-        tt(W(22, 2), W(22, 2), W(8, 2), OP.add)
         ts(W(24), W(10), 16.0, OP.is_ge)
         tt(W(20), W(20), W(15), OP.add)
-        ts(W(5), W(5), float(SF - 8 - 63), OP.add)
+        tt(W(22, 2), W(22, 2), W(8, 2), OP.add)
         ts(W(25), W(10), 16.0, OP.is_ge)
-        tt(W(22, 2), W(22, 2), W(20, 2), OP.subtract)
+        tt(W(4, 2), W(4, 2), W(20, 2), OP.subtract)
         for b in range(4):
             mm(4 + b, "qw", "sw", b, "qf", "sf")
         for b in range(4):
             act(A("tab", 256 * b, 256 * b + 256), bank(4 + b), AF.Copy, scale=0.03125)
 
         def suffix(b):
-            scan(A("tab", SF + 256 * b, SF + 256 * b + 256, -1), A("mb"), A("tab", 256 * b, 256 * b + 256, -1), -BIG, OP.min, OP.max)
+            scan(A("tab", SF + 256 * b, SF + 256 * b + 256, -1), A("mb", 0, 256), A("tab", 256 * b, 256 * b + 256, -1), -BIG, OP.min, OP.max)
 
-        def prefix(b):
-            scan(A("tab", PF + 256 * b, PF + 256 * b + 256), A("mb"), A("tab", 256 * b, 256 * b + 256), -BIG, OP.min, OP.max)
+        def prefix(h):
+            scan(A("tab", PF + 512 * h, PF + 512 * h + 512), A("mb"), A("tab", 512 * h, 512 * h + 512), -BIG, OP.min, OP.max)
 
         def top(k, lo, n):
             base = SF if k == 0 else TOP + k
             v = A("tab", base + 8 * lo, base + 8 * (lo + n - 1) + 1, 8)
             return v if k == 0 else part(v, "top%d" % k)
 
-        tt(W(22, 2), W(22, 2), W(4, 2), OP.add)
         suffix(0)
-        tt(W(22, 2), W(22, 2), W(24, 2), OP.mult)
+        tt(W(22, 2), W(22, 2), W(4, 2), OP.add)
         suffix(1)
-        tt(W(30, 2), W(22, 2), W(20, 2), OP.add)
+        tt(W(22, 2), W(22, 2), W(24, 2), OP.mult)
         suffix(2)
-        cp(A("idx"), W(28, 4))
+        tt(W(30, 2), W(22, 2), W(20, 2), OP.add)
         suffix(3)
-        prefix(0)
+        cp(A("idx"), W(28, 4))
+        tt(top(1, 0, 127), top(0, 0, 127), top(0, 1, 127), OP.max)
         for b in range(4):
             act(A("m1", 256 * b, 256 * b + 256), ind(A("tab", 256 * b, SF + 256 * b + 256), A("idx", 0, 16)), AF.Copy)
-        tt(top(1, 0, 127), top(0, 0, 127), top(0, 1, 127), OP.max)
-        tt(A("etmp"), A("tab", 2, 1024, 8), A("tab", 3, 1024, 8), OP.max)
+        prefix(0)
         tt(top(2, 0, 125), top(1, 0, 125), top(1, 2, 125), OP.max)
-        prefix(1)
+        tt(A("etmp"), A("tab", 2, 1024, 8), A("tab", 3, 1024, 8), OP.max)
         tt(top(3, 0, 121), top(2, 0, 121), top(2, 4, 121), OP.max)
-        prefix(2)
+        prefix(1)
         tt(top(4, 0, 113), top(3, 0, 113), top(3, 8, 113), OP.max)
         tt(top(5, 0, 128), A("etmp"), A("tab", 4, 1024, 8), OP.max)
-        prefix(3)
         tops = [("top%d" % k, 0, 1) for k in range(1, 6)]
         mn = ["m1", "m2", "m1", "m2"]
         for s in range(1, 4):
@@ -482,7 +504,7 @@ def rank_program(g, core, T, topo):
                 tt(A(mn[s], 256 * b, 256 * b + 256), ind(win, A("idx", 16 * s, 16 * s + 16)), A(mn[s - 1], 256 * b, 256 * b + 256), OP.max)
         for b in range(4):
             tt(part(A("xn", b, 1024, 4), "xn%d" % b), bank(b), A("m2", 256 * b, 256 * b + 256), OP.add)
-        quant("qx%d" % (t + 1), "sx%d" % (t + 1), part(A("xn"), "xn0", "xn1", "xn2", "xn3"))
+        quant(A("qx%d" % (t + 1)), A("sx%d" % (t + 1)), part(A("xn"), "xn0", "xn1", "xn2", "xn3"))
 
     mm(4, "qv", "sv", 0, "qx3", "sx3")
     store("y", T.oc[:], T.qx3[:].bitcast(dt.uint8), "qx3")

@@ -27,11 +27,10 @@ SCRATCH = {
     "r1": ("sbuf", [128, 256], "bfloat16"), "r2": ("sbuf", [128, 256], "bfloat16"), "r3": ("sbuf", [128, 256], "bfloat16"),
     "r4": ("sbuf", [128, 256], "bfloat16"), "r5": ("sbuf", [128, 256], "bfloat16"), "xs": ("sbuf", [128, 256], "float32"),
     "z": ("sbuf", [128, 256], "bfloat16"), "j0": ("sbuf", [128, 256], "bfloat16"),
-    "ja": ("sbuf", [128, 256], "bfloat16"), "jb": ("sbuf", [128, 256], "bfloat16"),
+    "ja": ("sbuf", [128, 256], "bfloat16"), "jb": ("sbuf", [128, 256], "bfloat16"), "jd": ("sbuf", [128, 256], "bfloat16"),
     "aa": ("sbuf", [128, 256], "float32"), "ab": ("sbuf", [128, 256], "float32"), "ac": ("sbuf", [128, 256], "float32"),
-    "ai": ("sbuf", [128, 256], "int32"),
-    "wa": ("sbuf", [128, 256], "bfloat16"), "wb": ("sbuf", [128, 256], "bfloat16"), "wd": ("sbuf", [128, 256], "bfloat16"),
-    "lst": ("sbuf", [128, 96], "uint16"), "rkl": ("sbuf", [128, 16], "uint16"), "pll": ("sbuf", [128, 16], "uint16"),
+    "ai": ("sbuf", [128, 256], "int32"), "wz": ("sbuf", [128, 2304], "bfloat16"),
+    "lst": ("sbuf", [128, 128], "uint16"), "rkl": ("sbuf", [128, 16], "uint16"), "pll": ("sbuf", [128, 16], "uint16"),
     "sgl": ("sbuf", [128, 16], "uint16"), "idx": ("sbuf", [128, 64], "uint16"),
     "p256": ("sbuf", [128, 256], "float32"), "key": ("sbuf", [128, 256], "float32"), "p1": ("sbuf", [128, 256], "float32"),
     "junk": ("sbuf", [128, 4096], "bfloat16"),
@@ -183,9 +182,10 @@ def rank_program(g, core, T, topo):
             return e.activation(o[0], a[0], func, **kw)
         rec("s", fn, [o] + ([acc] if acc is not None else []), [a, bias])
 
-    def mm(bank, wq, ws, b, xq, xs):
-        o, l, ls = A("ps", 512 * bank, 512 * bank + C), A(wq, 128 * b, 128 * b + 128), A(ws, 128 * b, 128 * b + 128)
-        rec("t", lambda e: e.matmul_mx(o[0], l[0], ls[0], T[xq][:], T[xs][:], True, True), [o], [l, ls, A(xq), A(xs)])
+    def mm(bank, wq, ws, b, xq, xs, lo=0, hi=C):
+        o, l, ls = A("ps", 512 * bank, 512 * bank + hi - lo), A(wq, 128 * b, 128 * b + 128), A(ws, 128 * b, 128 * b + 128)
+        r, rs = A(xq, lo, hi), A(xs, lo, hi)
+        rec("t", lambda e: e.matmul_mx(o[0], l[0], ls[0], r[0], rs[0], True, True), [o], [l, ls, r, rs])
 
     def iota(o, pattern, base, mult, small=False):
         if small:
@@ -270,14 +270,14 @@ def rank_program(g, core, T, topo):
         if step == 5:
             tt(jw2, jw2, root, OP.subtract)
 
-    def later_constants(step):
-        if step == 2:
+    def later_constants(a):
+        if a == 32:
             ts(radj, root, 256.0, OP.mult, -1.0, OP.add)
             fill(two, 0.5)
-        if step == 3:
+        if a == 64:
             fill(A("ssrt", 0, 16), 0.0)
             scan(inv2m, A("cf", 112, 118), A("cf", 128, 134), 2.0, OP.mult, OP.add)
-        if step == 4:
+        if a == 128:
             fill(A("p1", 0, 1), 255.0)
 
     def unpackers():
@@ -290,17 +290,20 @@ def rank_program(g, core, T, topo):
         quant(A("qv"), A("sv"), A("vin"))
         fill(A("mb", 0, 512, 8), -BIG)
 
-    def wrap(row, out):
-        scan(A("r3"), A("kd"), row, 0.0, OP.mult, OP.max)
-        ts(out, A("r3", 15, 256, 16), invk, OP.mult)
-
     def L(k):
         return A("lst", 16 * k, 16 * k + 16)
 
-    def sweep(name, between, last):
+    def sweep(name, base, between, last):
         for a in range(32, 256, 32):
-            tt(A(name if a < 224 else last, a, a + 32), ind(A(name, 0, a), A("lst", 80 + a // 16, 82 + a // 16)), A(name, a, a + 32), OP.add)
+            own = A(name, base + a, base + a + 32)
+            tt(own if a < 224 or last is None else last, ind(A(name, base, base + a), A("lst", 112 + a // 16, 114 + a // 16)), own, OP.add)
             between(a)
+
+    def H(name, h, first=0, step=1):
+        return A(name, 128 * h + first, 128 * h + 128, step)
+
+    def requant(t, h):
+        quant(H("qx%d" % t, h), H("sx%d" % t, h), part(A("xn", 512 * h, 512 * h + 512), *["xn%d%d" % (h, b) for b in range(4)]))
 
     def W(k, n=1):
         return A("iw", 16 * k, 16 * (k + n))
@@ -309,52 +312,55 @@ def rank_program(g, core, T, topo):
         peer = T.cores[rank ^ (1 << t)]
         qx, sx, qp, sp, ol, lp = ["%s%d" % (k, t) for k in ("qx", "sx", "qp", "sp", "ol", "lp")]
         engines = len(topo.engines(peer, core))
-        mm(4, "qu", "su", 0, qx, sx)
+        for h in range(2):
+            mm(4 + h, "qu", "su", 0, qx, sx, 128 * h, 128 * h + 128)
         send(peer, T[qp][:].bitcast(dt.uint8), T[qx][:].bitcast(dt.uint8), qx, "aq%d" % t)
         send(peer, T[sp][:], T[sx][:], sx, "aq%d" % t)
         arrive([qp, sp], "aq%d" % t, 2 * engines)
         if t == 0:
             unpackers()
-        late = late_constants if t == 0 else (lambda step: None)
-        ts(A("r1"), bank(4), 0.0, OP.is_gt, cut8, OP.min)
-        late(0)
-        turn(A("r2"), A("r1"))
-        late(1)
-        scan(A("xs"), A("dj"), A("r2"), 0.0, OP.mult, OP.add)
-        late(2)
-        ts(A("z", 0, 256, 16), A("xs", 9, 256, 16), ROUND, OP.add, ROUND, OP.subtract)
-        late(3)
-        scan(A("r2"), A("keep"), A("z"), 0.0, OP.mult, OP.add)
-        late(4)
-        turn(A("j0"), A("r2"))
-        late(5)
-        wrap(A("j0"), L(0))
+        stages = [
+            lambda h: ts(H("r1", h), bank(4 + h, 128), 0.0, OP.is_gt, cut8, OP.min),
+            lambda h: turn(H("r2", h), H("r1", h)),
+            lambda h: scan(H("xs", h), H("dj", h), H("r2", h), 0.0, OP.mult, OP.add),
+            lambda h: ts(H("z", h, 0, 16), H("xs", h, 9, 16), ROUND, OP.add, ROUND, OP.subtract),
+            lambda h: scan(H("r4", h), H("keep", h), H("z", h), 0.0, OP.mult, OP.add),
+            lambda h: turn(H("j0", h), H("r4", h)),
+            lambda h: scan(H("r3", h), H("kd", h), H("j0", h), 0.0, OP.mult, OP.max),
+            lambda h: ts(A("lst", 8 * h, 8 * h + 8), H("r3", h, 15, 16), invk, OP.mult)]
+        for n, stage in enumerate(stages):
+            stage(0)
+            stage(1)
+            if t == 0:
+                late_constants(n)
         act(A("p256", 1, 256), A("j0", 1, 256), AF.Identity, bias=256.0, scale=256.0)
         keyw, sg = A("wf", 16, 32), A("wf", 32, 48)
-        jn, an = ["j0", "ja", "jb", "ja", "jb", "ja"], ["a0", "aa", "ab", "aa", "ab", "aa"]
-        for k in range(5):
-            act(A(jn[k + 1]), ind(A(jn[k]), L(k)), AF.Copy)
-            tt(A(an[k + 1]), ind(A(an[k]), L(k)), A("ac" if k else "a1"), OP.add)
-            if k < 4:
-                act(A("ac"), A(an[k + 1]), AF.Copy)
-            scan(A("r3"), A("kd"), A(jn[k + 1]), 0.0, OP.mult, OP.max)
+        jn, an = ["j0", "ja", "jb", "jd", "ja", "jb", "jd", "ja"], ["a1", "a0", "aa", "ab", "ac", "aa", "ab", "ac", "aa"]
+        for k in range(8):
+            held = "r5" if k % 2 else "r3"
+            if k not in (0, 6):
+                scan(A(held), A("kd"), A(jn[k]), 0.0, OP.mult, OP.max)
+            if k == 6:
+                scan(A("key"), A("jrow"), A("p256"), 0.0, OP.min, OP.add)
+            if k < 7:
+                act(A(jn[k + 1]), ind(A(jn[k]), L(max(k - 1, 0))), AF.Copy)
+                tt(A(an[k + 2]), ind(A(an[k + 1]), L(max(k - 1, 0))), A(an[k]), OP.add)
             if k == 0:
                 ts(keyw, L(0), 256.0, OP.mult)
-            if k == 1:
+            if k == 6:
                 tt(keyw, keyw, jw2, OP.add)
-            if t == 0:
-                later_constants(k)
-            ts(L(k + 1), A("r3", 15, 256, 16), invk, OP.mult)
+            if k not in (0, 6):
+                ts(L(k), A(held, 15, 256, 16), invk, OP.mult)
 
         def beside_bits(a):
-            if a == 32:
-                scan(A("key"), A("jrow"), A("p256"), 0.0, OP.min, OP.add)
             if a == 96:
                 cp(A("ai", 0, 96), A("aa", 0, 96))
             if a in (160, 224):
                 cp(A("ai", a - 64, a), A("aa", a - 64, a))
+            if t == 0:
+                later_constants(a)
 
-        sweep("aa", beside_bits, "ai")
+        sweep("aa", 0, beside_bits, A("ai", 224, 256))
         for k in range(16):
             act(A("junk", 256 * k, 256 * k + 256), A("key"), AF.Sign, bias=A("wf", 16 + k, 17 + k), scale=-1.0, acc=A("wf", 32 + k, 33 + k))
         for m in range(7):
@@ -363,17 +369,20 @@ def rank_program(g, core, T, topo):
             if m >= 1:
                 lo, n = 304 * (m - 1), 128 - 24 * (m - 1)
                 tt(A("hm", 128 * m - 128, 128 * m - 128 + n), A("msk", lo, lo + n), A("msk", lo + n, lo + 2 * n), OP.add)
-        for m in range(6):
+            if m >= 5:
+                total(A("wf", 43 + m, 44 + m), A("hm", 128 * (m - 5), 104 * (m - 5) + 128))
+        for m in range(2, 6):
             total(A("wf", 48 + m, 49 + m), A("hm", 128 * m, 104 * m + 128))
         tt(A("wi", 32, 38), A("wf", 48, 54), inv2m, OP.mult)
         for f in range(3):
             ts(part(A("szw", f, 18, 3), "sz%d" % f), A("wi", 32, 38), 8 * f, OP.logical_shift_right, 255, OP.bitwise_and)
         size = part(A("szw", 0, 16), "sz0", "sz1", "sz2")
         tt(A("z", 0, 256, 16), size, root, OP.add)
-        scan(A("r2"), A("keep"), A("z"), 0.0, OP.mult, OP.add)
         tt(W(4), size, radj, OP.add)
-        turn(A("r1"), A("r2"))
+        scan(A("r2"), A("keep"), A("z"), 0.0, OP.mult, OP.add)
         ts(A("rkl"), sg, 255.0, OP.add, 0.5, OP.mult)
+        turn(A("r1"), A("r2"))
+        ts(W(5), W(4), 1.0, OP.min)
         scan(A("r3"), A("kd"), A("r1"), 0.0, OP.mult, OP.max)
         scatter(A("r4"), A("rkl"), A("jrow"))
         ts(A("z", 0, 256, 16), A("r3", 15, 256, 16), invk, OP.mult)
@@ -383,22 +392,29 @@ def rank_program(g, core, T, topo):
         ts(A("sgl"), A("r5", 15, 256, 16), invk, OP.mult)
         turn(A("r1"), A("r2"))
         act(A("psrt"), ind(A("p256"), A("sgl")), AF.Copy)
-        ts(W(5), W(4), 1.0, OP.min)
-        cp(A("ssrt", 16, 272), ind(A("r1"), A("sgl")))
         ts(W(6), W(4), 1.0, OP.min, -1.0, OP.mult)
+        cp(A("ssrt", 16, 272), ind(A("r1"), A("sgl")))
         scan(A("cum"), A("ssrt", 15, 271), A("psrt"), 0.0, OP.add, OP.max)
-        tt(A("wa"), ind(A("cum"), A("rkl")), A("p1"), OP.subtract)
-        wn = ["wa", "wb"]
-        for k in range(5):
-            cp(A("wd"), A(wn[k % 2]))
-            tt(A(wn[(k + 1) % 2]), ind(A(wn[k % 2]), L(k)), A("wd"), OP.add)
+        for h in range(2):
+            tt(A("wz", 256 + 128 * h, 384 + 128 * h), ind(A("cum"), A("rkl", 8 * h, 8 * h + 8)), H("p1", h), OP.subtract)
+        for k in range(7):
+            for h in range(2):
+                if k == 0:
+                    cp(H("wz", h), A("wz", 256 + 128 * h, 384 + 128 * h))
+            for h in range(2):
+                s0, n = 256 * k + 128 * h, 16 * max(k - 1, 0) + 8 * h
+                tt(A("wz", s0 + 512, s0 + 640), ind(A("wz", 256 * k + 256, s0 + 384), A("lst", n, n + 8)), A("wz", s0, s0 + 128), OP.add)
 
         def beside_places(a):
             b = a // 32 - 1
             if t == 0 and b < 4:
                 quant(A("qe", 128 * b, 128 * b + 128), A("se", 128 * b, 128 * b + 128), A("et", 512 * b, 512 * b + 512))
+            if a == 160:
+                scan(H("r3", 0), H("kd", 0), A("wz", 2048, 2176), 0.0, OP.mult, OP.max)
+            if a == 192:
+                ts(A("pll", 0, 8), H("r3", 0, 15, 16), invk, OP.mult)
 
-        sweep("wb", beside_places, "wb")
+        sweep("wz", 2048, beside_places, None)
         for b in range(4):
             mm(b, "qe", "se", b, qp, sp)
         for b in range(4):
@@ -410,7 +426,8 @@ def rank_program(g, core, T, topo):
         if t == R - 1:
             act(A("po"), A("j0"), AF.Copy)
             store("y", T.op[:], T.po[0:128:16, :], "po")
-        wrap(A("wb"), A("pll"))
+        scan(H("r3", 1), H("kd", 1), A("wz", 2176, 2304), 0.0, OP.mult, OP.max)
+        ts(A("pll", 8, 16), H("r3", 1, 15, 16), invk, OP.mult)
         scatter(A("r1"), A("pll"), A("jrow"))
         l, r, l8, r8 = W(0), W(1), W(2), W(3)
         cp(l, A("pll"))
@@ -442,24 +459,26 @@ def rank_program(g, core, T, topo):
         ts(W(4), W(10), 40.0, OP.is_ge)
         ts(W(5), W(10), 40.0, OP.is_lt, 15.0, OP.mult)
         ts(W(6), W(10), 72.0, OP.is_ge, float(SF + 8), OP.add)
+        ts(W(7), W(10), 72.0, OP.is_lt, 31.0, OP.mult)
+        ts(W(8), W(10), 136.0, OP.is_ge)
+        ts(W(9), W(10), 136.0, OP.is_lt, 63.0, OP.mult)
         for b in range(4):
             o, win = part(A("bt", b, 1024, 4), "bt%d" % b), ind(A("tp", 256 * b, 256 * b + 256), A(lp))
             if b % 2:
                 act(o, win, AF.Copy)
             else:
                 cp(o, win)
-        quant(A("qf"), A("sf"), part(A("bt"), "bt0", "bt1", "bt2", "bt3"))
-        ts(W(7), W(10), 72.0, OP.is_lt, 31.0, OP.mult)
-        ts(W(8), W(10), 136.0, OP.is_ge)
-        ts(W(9), W(10), 136.0, OP.is_lt, 63.0, OP.mult)
         tt(W(15), W(15), W(13), OP.mult)
         ts(W(23), W(23), float(SF - 8 - 15 - 31 - 63), OP.add)
+        quant(A("qf"), A("sf"), part(A("bt"), "bt0", "bt1", "bt2", "bt3"))
         tt(W(4, 2), W(4, 2), W(6, 2), OP.add)
         ts(W(24), W(10), 16.0, OP.is_ge)
         tt(W(20), W(20), W(15), OP.add)
         tt(W(22, 2), W(22, 2), W(8, 2), OP.add)
         ts(W(25), W(10), 16.0, OP.is_ge)
         tt(W(4, 2), W(4, 2), W(20, 2), OP.subtract)
+        tt(W(22, 2), W(22, 2), W(4, 2), OP.add)
+        tt(W(22, 2), W(22, 2), W(24, 2), OP.mult)
         for b in range(4):
             mm(4 + b, "qw", "sw", b, "qf", "sf")
         for b in range(4):
@@ -477,23 +496,21 @@ def rank_program(g, core, T, topo):
             return v if k == 0 else part(v, "top%d" % k)
 
         suffix(0)
-        tt(W(22, 2), W(22, 2), W(4, 2), OP.add)
-        suffix(1)
-        tt(W(22, 2), W(22, 2), W(24, 2), OP.mult)
-        suffix(2)
         tt(W(30, 2), W(22, 2), W(20, 2), OP.add)
-        suffix(3)
+        suffix(1)
         cp(A("idx"), W(28, 4))
-        tt(top(1, 0, 127), top(0, 0, 127), top(0, 1, 127), OP.max)
+        suffix(2)
+        suffix(3)
         for b in range(4):
             act(A("m1", 256 * b, 256 * b + 256), ind(A("tab", 256 * b, SF + 256 * b + 256), A("idx", 0, 16)), AF.Copy)
+        tt(A("etmp"), A("tab", 2, 1024, 8), A("tab", 3, 1024, 8), OP.max)
+        tt(top(1, 0, 127), top(0, 0, 127), top(0, 1, 127), OP.max)
         prefix(0)
         tt(top(2, 0, 125), top(1, 0, 125), top(1, 2, 125), OP.max)
-        tt(A("etmp"), A("tab", 2, 1024, 8), A("tab", 3, 1024, 8), OP.max)
+        tt(top(5, 0, 128), A("etmp"), A("tab", 4, 1024, 8), OP.max)
         tt(top(3, 0, 121), top(2, 0, 121), top(2, 4, 121), OP.max)
         prefix(1)
         tt(top(4, 0, 113), top(3, 0, 113), top(3, 8, 113), OP.max)
-        tt(top(5, 0, 128), A("etmp"), A("tab", 4, 1024, 8), OP.max)
         tops = [("top%d" % k, 0, 1) for k in range(1, 6)]
         mn = ["m1", "m2", "m1", "m2"]
         for s in range(1, 4):
@@ -502,9 +519,14 @@ def rank_program(g, core, T, topo):
                 if s > 1:
                     win = (win[0], win[1] + tops, [])
                 tt(A(mn[s], 256 * b, 256 * b + 256), ind(win, A("idx", 16 * s, 16 * s + 16)), A(mn[s - 1], 256 * b, 256 * b + 256), OP.max)
-        for b in range(4):
-            tt(part(A("xn", b, 1024, 4), "xn%d" % b), bank(b), A("m2", 256 * b, 256 * b + 256), OP.add)
-        quant(A("qx%d" % (t + 1)), A("sx%d" % (t + 1)), part(A("xn"), "xn0", "xn1", "xn2", "xn3"))
+        for h in range(2):
+            for b in range(4):
+                lo = 128 * h
+                tt(part(A("xn", 4 * lo + b, 4 * lo + 512, 4), "xn%d%d" % (h, b)), A("ps", 512 * b + lo, 512 * b + lo + 128),
+                   A("m2", 256 * b + lo, 256 * b + lo + 128), OP.add)
+                if (h, b) == (1, 1):
+                    requant(t + 1, 0)
+        requant(t + 1, 1)
 
     mm(4, "qv", "sv", 0, "qx3", "sx3")
     store("y", T.oc[:], T.qx3[:].bitcast(dt.uint8), "qx3")

@@ -4,7 +4,14 @@ C, R = 256, 3
 BIG = 1e29
 HOLD = 1024.0
 ROUND = 12582912.0
-SF, PF, TOP = 1024, 2048, 3072
+MID, S16, S4, RAW, P4, P16 = 0, 1024, 2048, 3072, 4096, 5120
+STEPS = 7
+BLOCK = 384
+CUT = 192
+LAST = ((128, 192), (192, 256))
+
+CYCLE, FLOOR, WAKE, GATHER, SCATTER, LOCAL, REMOTE = 0.83, 64, 220.0, 1.5, 3.5, 1200.0, 1200.0
+SOON, SPARE, LEAD = 40.0, 30.0, 1500.0
 
 SCRATCH = {
     "ps": ("psum", [128, 4096], "float32"),
@@ -16,28 +23,32 @@ SCRATCH = {
     "ones": ("sbuf", [128, 512], "bfloat16"),
     "xn": ("sbuf", [128, 1024], "bfloat16"), "tp": ("sbuf", [128, 1024], "bfloat16"), "bt": ("sbuf", [128, 1024], "bfloat16"),
     "qf": ("sbuf", [128, 256], "float8_e4m3fn_x4"), "sf": ("sbuf", [128, 256], "uint8"),
-    "tab": ("sbuf", [128, 4096], "float32"), "etmp": ("sbuf", [128, 128], "float32"),
-    "m1": ("sbuf", [128, 1024], "float32"), "m2": ("sbuf", [128, 1024], "float32"),
+    "tab": ("sbuf", [128, 6144], "float32"), "mg": ("sbuf", [128, 448], "float32"),
+    "m1": ("sbuf", [128, 1024], "float32"), "m2": ("sbuf", [128, 1024], "float32"), "m3": ("sbuf", [128, 1024], "float32"),
     "yo": ("sbuf", [128, 256], "float32"), "po": ("sbuf", [128, 256], "float32"),
-    "ci": ("sbuf", [128, 64], "int32"), "cf": ("sbuf", [128, 176], "float32"), "pw": ("sbuf", [128, 16], "float32"),
-    "posd": ("sbuf", [128, 256], "bfloat16"), "kd": ("sbuf", [128, 256], "bfloat16"), "kd2": ("sbuf", [128, 256], "bfloat16"),
-    "dmx": ("sbuf", [128, 256], "bfloat16"), "keep": ("sbuf", [128, 256], "bfloat16"), "jrow": ("sbuf", [128, 256], "bfloat16"),
-    "a0": ("sbuf", [128, 256], "float32"), "a1": ("sbuf", [128, 256], "float32"), "dj": ("sbuf", [128, 256], "bfloat16"),
-    "mb": ("sbuf", [128, 512], "float32"), "exl": ("sbuf", [128, 16], "uint16"),
+    "ci": ("sbuf", [128, 96], "int32"), "cf": ("sbuf", [128, 128], "float32"), "pw": ("sbuf", [128, 16], "float32"),
+    "posd": ("sbuf", [128, 128], "bfloat16"), "kd": ("sbuf", [128, 128], "bfloat16"), "kd2": ("sbuf", [128, 128], "bfloat16"),
+    "pos4": ("sbuf", [128, 32], "bfloat16"), "k4": ("sbuf", [128, 256], "bfloat16"), "k42": ("sbuf", [128, 32], "bfloat16"),
+    "dmx": ("sbuf", [128, 128], "bfloat16"), "keep": ("sbuf", [128, 256], "bfloat16"), "jrow": ("sbuf", [128, 256], "bfloat16"),
+    "jfr": ("sbuf", [128, 256], "bfloat16"), "dj": ("sbuf", [128, 256], "bfloat16"),
+    "mb4": ("sbuf", [128, 512], "bfloat16"), "mb16": ("sbuf", [128, 512], "bfloat16"), "mbm": ("sbuf", [128, 112], "bfloat16"),
+    "cl": ("sbuf", [128, 48], "uint16"),
     "r1": ("sbuf", [128, 256], "bfloat16"), "r2": ("sbuf", [128, 256], "bfloat16"), "r3": ("sbuf", [128, 256], "bfloat16"),
-    "r4": ("sbuf", [128, 256], "bfloat16"), "r5": ("sbuf", [128, 256], "bfloat16"), "xs": ("sbuf", [128, 256], "float32"),
-    "z": ("sbuf", [128, 256], "bfloat16"), "j0": ("sbuf", [128, 256], "bfloat16"),
-    "ja": ("sbuf", [128, 256], "bfloat16"), "jb": ("sbuf", [128, 256], "bfloat16"), "jd": ("sbuf", [128, 256], "bfloat16"),
-    "aa": ("sbuf", [128, 256], "float32"), "ab": ("sbuf", [128, 256], "float32"), "ac": ("sbuf", [128, 256], "float32"),
-    "ai": ("sbuf", [128, 256], "int32"), "wz": ("sbuf", [128, 2304], "bfloat16"),
-    "lst": ("sbuf", [128, 128], "uint16"), "rkl": ("sbuf", [128, 16], "uint16"), "pll": ("sbuf", [128, 16], "uint16"),
-    "sgl": ("sbuf", [128, 16], "uint16"), "idx": ("sbuf", [128, 64], "uint16"),
-    "p256": ("sbuf", [128, 256], "float32"), "key": ("sbuf", [128, 256], "float32"), "p1": ("sbuf", [128, 256], "float32"),
-    "junk": ("sbuf", [128, 4096], "bfloat16"),
-    "wf": ("sbuf", [128, 96], "float32"), "wi": ("sbuf", [128, 64], "int32"), "szw": ("sbuf", [128, 24], "int32"),
-    "msk": ("sbuf", [128, 1536], "int32"), "hm": ("sbuf", [128, 768], "float32"),
-    "psrt": ("sbuf", [128, 256], "float32"), "ssrt": ("sbuf", [128, 272], "bfloat16"), "cum": ("sbuf", [128, 256], "float32"),
-    "iw": ("sbuf", [128, 512], "float32"),
+    "r4": ("sbuf", [128, 256], "bfloat16"), "jr": ("sbuf", [128, 1536], "bfloat16"), "hd": ("sbuf", [128, 2304], "bfloat16"),
+    "sa": ("sbuf", [128, 1920], "float32"), "af": ("sbuf", [128, 256], "float32"), "ai": ("sbuf", [128, 256], "int32"),
+    "wz": ("sbuf", [128, 1152], "bfloat16"), "pf": ("sbuf", [128, 256], "bfloat16"),
+    "lst": ("sbuf", [128, 144], "uint16"), "rkl": ("sbuf", [128, 16], "uint16"), "pll": ("sbuf", [128, 16], "uint16"),
+    "sgl": ("sbuf", [128, 16], "uint16"), "spl": ("sbuf", [128, 24], "uint16"), "idx": ("sbuf", [128, 48], "uint16"),
+    "key": ("sbuf", [128, 256], "float32"), "junk": ("sbuf", [128, 2048], "bfloat16"),
+    "wf": ("sbuf", [128, 96], "float32"), "wi": ("sbuf", [128, 96], "int32"), "szw": ("sbuf", [128, 24], "int32"),
+    "msk": ("sbuf", [128, 1024], "int32"), "hm": ("sbuf", [128, 768], "float32"),
+    "z": ("sbuf", [128, 512], "bfloat16"), "zb": ("sbuf", [128, 512], "bfloat16"), "zt": ("sbuf", [128, 512], "bfloat16"),
+    "srow": ("sbuf", [128, 256], "bfloat16"), "shd": ("sbuf", [128, 256], "bfloat16"),
+    "psrt": ("sbuf", [128, 256], "bfloat16"), "ssrt": ("sbuf", [128, 272], "bfloat16"),
+    "step": ("sbuf", [128, 256], "bfloat16"), "same": ("sbuf", [128, 272], "bfloat16"),
+    "cum": ("sbuf", [128, 256], "bfloat16"), "szp": ("sbuf", [128, 128], "bfloat16"), "phd": ("sbuf", [128, 256], "bfloat16"),
+    "orow": ("sbuf", [128, 256], "bfloat16"), "ohd": ("sbuf", [128, 256], "bfloat16"),
+    "iv": ("sbuf", [128, 192], "int32"), "iw": ("sbuf", [128, 416], "float32"),
 }
 for _t in range(R + 1):
     SCRATCH["qx%d" % _t] = ("sbuf", [128, 256], "float8_e4m3fn_x4")
@@ -45,28 +56,90 @@ for _t in range(R + 1):
 for _t in range(R):
     SCRATCH["qp%d" % _t] = ("sbuf", [128, 256], "float8_e4m3fn_x4")
     SCRATCH["sp%d" % _t] = ("sbuf", [128, 256], "uint8")
-    SCRATCH["ol%d" % _t] = ("sbuf", [128, 16], "uint16")
-    SCRATCH["lp%d" % _t] = ("sbuf", [128, 16], "uint16")
+    SCRATCH["ol%d" % _t] = ("sbuf", [128, 64], "uint16")
+    SCRATCH["lp%d" % _t] = ("sbuf", [128, 64], "uint16")
 
-SEMAPHORES = ["cv", "cs", "ct", "cg", "ldx", "ldu", "ldv", "ldw", "lds", "sent", "stored"] + \
+SEMAPHORES = ["cv", "cs", "ct", "cg", "ldx0", "ldx1", "ldu", "ldv", "ldw", "lds", "sent", "stored"] + \
     ["aq%d" % t for t in range(R)] + ["al%d" % t for t in range(R)]
 COUNTER = {"v": "cv", "s": "cs", "t": "ct", "g": "cg"}
+PLAN = []
+
+
+def earlier(ops):
+    touched, found = {}, []
+    for n, op in enumerate(ops):
+        deps = set()
+        for regs, writes in ((op["rd"], False), (op["wr"], True)):
+            for name, lo, hi in regs:
+                deps.update(m for a, b, m, w in touched.get(name, []) if a < hi and lo < b and (w or writes))
+        found.append(deps)
+        for regs, writes in ((op["rd"], False), (op["wr"], True)):
+            for name, lo, hi in regs:
+                old = touched.get(name, [])
+                if writes:
+                    old = [e for e in old if not (lo <= e[0] and e[1] <= hi)]
+                touched[name] = old + [(lo, hi, n, writes)]
+    return found
+
+
+def arrange(ops):
+    deps = earlier(ops)
+    for n, op in enumerate(ops):
+        deps[n].update(op["after"])
+    later = [[] for op in ops]
+    for n, d in enumerate(deps):
+        for m in d:
+            later[m].append(n)
+
+    def lay(weight, before, after, back):
+        tail = [op["time"] - op["hold"] if back else 0.0 for op in ops]
+        missing, ready, free, at = [len(d) for d in before], list(tail), {}, {}
+        open_calls = [n for n in range(len(ops)) if not missing[n]]
+        while open_calls:
+            start = {n: max(ready[n], free.get(ops[n]["q"], 0.0)) for n in open_calls}
+            first = min(open_calls, key=lambda n: (start[n], -weight[n]))
+            mine = sorted([n for n in open_calls if ops[n]["q"] == ops[first]["q"]], key=lambda n: -weight[n])
+            pick, limit = None, float("inf")
+            for n in mine:
+                if start[n] <= start[first] + SOON and start[n] + ops[n]["hold"] <= limit:
+                    pick = n
+                    break
+                limit = min(limit, start[n] + SPARE + weight[mine[0]] - weight[n])
+            if pick is None:
+                pick = min([n for n in mine if start[n] > start[first] + SOON], key=lambda n: start[n])
+            open_calls.remove(pick)
+            at[pick] = start[pick]
+            if ops[pick]["q"] is not None:
+                free[ops[pick]["q"]] = at[pick] + ops[pick]["hold"]
+            for k in after[pick]:
+                ready[k] = max(ready[k], at[pick] + ops[pick]["time"] - tail[pick] + WAKE + tail[k])
+                missing[k] -= 1
+                if not missing[k]:
+                    open_calls.append(k)
+        return [at[n] + ops[n]["hold"] for n in range(len(ops))], sorted(at, key=lambda n: (at[n], n))
+
+    chain = [0.0] * len(ops)
+    for n in reversed(range(len(ops))):
+        chain[n] = ops[n]["time"] + max([WAKE + chain[k] for k in later[n]] + [0.0])
+    ends = lay([chain[n] + ops[n].get("lead", 0.0) for n in range(len(ops))], deps, later, False)[0]
+    order = lay(lay(ends, later, deps, True)[0], deps, later, False)[1]
+    return order, earlier([ops[n] for n in order])
 
 
 def emit(g, T, ops):
     queue = {"v": g.vector, "s": g.scalar, "t": g.tensor, "g": g, "y": g.sync}
-    touched, known, clock, waits, marked, seq = {}, {q: {} for q in queue}, [], [], set(), {}
-    for n, op in enumerate(ops):
+    if not PLAN:
+        PLAN.extend(arrange(ops))
+    ops = [ops[n] for n in PLAN[0]]
+    known, clock, waits, marked, seq = {q: {} for q in queue}, [], [], set(), {}
+    for n, (op, before) in enumerate(zip(ops, PLAN[1])):
         q, line = op["q"], op["line"]
         seq[line] = seq.get(line, 0) + 1
         op["seq"] = seq[line]
         deps = {}
-        for regs, writes in ((op["rd"], False), (op["wr"], True)):
-            for name, lo, hi in regs:
-                for a, b, m, w in touched.get(name, []):
-                    if a < hi and lo < b and (w or writes) and m != n:
-                        if ops[m]["seq"] > deps.get(ops[m]["line"], (0, 0))[0]:
-                            deps[ops[m]["line"]] = (ops[m]["seq"], m)
+        for m in before:
+            if ops[m]["seq"] > deps.get(ops[m]["line"], (0, 0))[0]:
+                deps[ops[m]["line"]] = (ops[m]["seq"], m)
         mine = []
         if q is not None:
             for ln, (s, m) in sorted(deps.items(), key=lambda e: -e[1][1]):
@@ -79,12 +152,6 @@ def emit(g, T, ops):
         ck = dict(known[q]) if q is not None else {}
         ck[line] = op["seq"]
         clock.append(ck)
-        for regs, writes in ((op["rd"], False), (op["wr"], True)):
-            for name, lo, hi in regs:
-                old = touched.get(name, [])
-                if writes:
-                    old = [e for e in old if not (lo <= e[0] and e[1] <= hi)]
-                touched[name] = old + [(lo, hi, n, writes)]
     count = {}
     for n, op in enumerate(ops):
         if op["token"] is None and n in marked:
@@ -117,20 +184,21 @@ def rank_program(g, core, T, topo):
             ap = T[name][:, lo:hi]
         else:
             ap = T[name][:, lo:hi:step]
+        n, narrow = len(range(lo, hi, abs(step))), SCRATCH[name][2] in ("bfloat16", "uint16")
         if name == "ps":
-            return (ap, [], [(name, lo // 512 * 512, (hi + 511) // 512 * 512)])
-        return (ap, [(name, lo, hi)], [])
+            return (ap, [], [(name, lo // 512 * 512, (hi + 511) // 512 * 512)], n, narrow)
+        return (ap, [(name, lo, hi)], [], n, narrow)
 
     def part(view, *names):
-        return (view[0], [(k, 0, 1) for k in names], [])
+        return (view[0], [(k, 0, 1) for k in names], []) + view[3:]
 
     def ind(win, off):
-        return (win[0].indirect(off[0]), win[1] + off[1], [])
+        return (win[0].indirect(off[0]), win[1] + off[1], [], 16 * off[3], None)
 
     def val(s):
         return s[0] if isinstance(s, tuple) else s
 
-    def rec(q, fn, outs, ins, token=None, inc=None, line=None):
+    def rec(q, fn, outs, ins, time, hold=None, token=None, inc=None, line=None, after=()):
         rd, wr = [], []
         for o in outs:
             wr += o[1] + o[2]
@@ -138,39 +206,47 @@ def rank_program(g, core, T, topo):
             if isinstance(i, tuple):
                 rd += i[1]
                 wr += i[2]
-        ops.append({"q": q, "fn": fn, "rd": rd, "wr": wr, "token": token, "inc": inc, "line": line or q})
+        ops.append({"q": q, "fn": fn, "rd": rd, "wr": wr, "token": token, "inc": inc, "line": line or q,
+                    "time": time, "hold": time if hold is None else hold, "after": after})
+
+    def span(a, *others, rate=None):
+        if a[4] is None:
+            return 60 + a[3] * GATHER * CYCLE
+        if rate is None:
+            rate = 0.5 if a[4] and all(o[4] for o in others) else 1.0
+        return max(FLOOR, a[3] * rate) * CYCLE
 
     def tt(o, a, b, op):
-        rec("v", lambda e: e.tensor_tensor(o[0], a[0], b[0], op), [o], [a, b])
+        rec("v", lambda e: e.tensor_tensor(o[0], a[0], b[0], op), [o], [a, b], span(a, rate=1.0 if a[2] else 2.0))
 
     def ts(o, a, s1, op0, s2=None, op1=None):
         if op1 is None:
-            rec("v", lambda e: e.tensor_scalar(o[0], a[0], val(s1), None, op0), [o], [a, s1])
+            rec("v", lambda e: e.tensor_scalar(o[0], a[0], val(s1), None, op0), [o], [a, s1], span(a, o))
         else:
-            rec("v", lambda e: e.tensor_scalar(o[0], a[0], val(s1), val(s2), op0, op1), [o], [a, s1, s2])
+            rec("v", lambda e: e.tensor_scalar(o[0], a[0], val(s1), val(s2), op0, op1), [o], [a, s1, s2], span(a, o))
 
     def cp(o, a):
-        rec("v", lambda e: e.tensor_copy(o[0], a[0]), [o], [a])
+        rec("v", lambda e: e.tensor_copy(o[0], a[0]), [o], [a], span(a, o))
 
     def total(o, a):
-        rec("v", lambda e: e.tensor_reduce(o[0], a[0], AxisListType.X, OP.add), [o], [a])
+        rec("v", lambda e: e.tensor_reduce(o[0], a[0], AxisListType.X, OP.add), [o], [a], span(a, rate=1.0))
 
     def scatter(win, off, a):
-        rec("v", lambda e: e.tensor_copy(win[0].indirect(off[0]), a[0]), [win], [off, a])
+        rec("v", lambda e: e.tensor_copy(win[0].indirect(off[0]), a[0]), [win], [off, a], 50 + a[3] * SCATTER * CYCLE)
 
     def fill(o, c):
-        rec("v", lambda e: e.memset(o[0], c), [o], [])
+        rec("v", lambda e: e.memset(o[0], c), [o], [], span(o))
 
     def scan(o, d0, d1, init, op0, op1):
-        rec("v", lambda e: e.tensor_tensor_scan(o[0], d0[0], d1[0], init, op0, op1), [o], [d0, d1])
+        rec("v", lambda e: e.tensor_tensor_scan(o[0], d0[0], d1[0], init, op0, op1), [o], [d0, d1], span(o, d0, d1))
 
     def turn(o, a):
-        rec("v", lambda e: e.transpose(o[0], a[0]), [o], [a])
+        rec("v", lambda e: e.transpose(o[0], a[0]), [o], [a], span(a, o))
 
     def quant(q, s, a):
-        rec("v", lambda e: e.quantize_mx(q[0], s[0], a[0]), [q, s], [a])
+        rec("v", lambda e: e.quantize_mx(q[0], s[0], a[0]), [q, s], [a], 12 + 0.22 * a[3])
 
-    def act(o, a, func, bias=None, scale=1.0, acc=None):
+    def act(o, a, func=AF.Copy, bias=None, scale=1.0, acc=None):
         def fn(e):
             kw = {}
             if bias is not None:
@@ -180,133 +256,171 @@ def rank_program(g, core, T, topo):
             if acc is not None:
                 kw["accum_out"] = acc[0]
             return e.activation(o[0], a[0], func, **kw)
-        rec("s", fn, [o] + ([acc] if acc is not None else []), [a, bias])
+        rec("s", fn, [o] + ([acc] if acc is not None else []), [a, bias], span(a, rate=1.0) + (20 if acc else 0))
 
     def mm(bank, wq, ws, b, xq, xs, lo=0, hi=C):
         o, l, ls = A("ps", 512 * bank, 512 * bank + hi - lo), A(wq, 128 * b, 128 * b + 128), A(ws, 128 * b, 128 * b + 128)
         r, rs = A(xq, lo, hi), A(xs, lo, hi)
-        rec("t", lambda e: e.matmul_mx(o[0], l[0], ls[0], r[0], rs[0], True, True), [o], [l, ls, r, rs])
+        rec("t", lambda e: e.matmul_mx(o[0], l[0], ls[0], r[0], rs[0], True, True), [o], [l, ls, r, rs], (hi - lo + 16) * CYCLE)
 
-    def iota(o, pattern, base, mult, small=False):
-        if small:
-            rec("g", lambda e: e.iota(o[0], pattern, base, mult, allow_small_or_imprecise_dtypes=True), [o], [])
+    def iota(o, pattern, base, mult):
+        if o[4]:
+            rec("g", lambda e: e.iota(o[0], pattern, base, mult, allow_small_or_imprecise_dtypes=True), [o], [], 130 + 2 * o[3] * CYCLE)
         else:
-            rec("g", lambda e: e.iota(o[0], pattern, base, mult), [o], [])
+            rec("g", lambda e: e.iota(o[0], pattern, base, mult), [o], [], 130 + 2 * o[3] * CYCLE)
 
-    def load(q, name, dst, src, sem):
-        rec(q, lambda e: e.dma_start(dst, src), [A(name)], [], token=(sem, 16), inc=(sem, 16), line=sem)
+    def load(q, view, dst, src, sem):
+        rec(q, lambda e: e.dma_start(dst, src), [view], [], LOCAL, 50, (sem, 16), (sem, 16), sem)
 
-    def store(q, dst, src, name):
+    def store(q, dst, src, view):
         totals["stored"] += 16
-        rec(q, lambda e: e.dma_start(dst, src), [], [A(name)], token=("stored", 0), inc=("stored", 16), line="st%d" % totals["stored"])
+        rec(q, lambda e: e.dma_start(dst, src), [], [view], LOCAL, 50, ("stored", 0), ("stored", 16), "st%d" % totals["stored"])
 
     def send(peer, dst, src, name, sem):
         rid, pid = topo.addr(peer)[:2]
         totals["sent"] += len(topo.engines(core, peer))
         rec("g", lambda e: e.remote_dma(dst, src, T.sem[sem], T.sem.sent, pid, rid, topo.mask(core, peer)), [], [A(name)],
-            token=("sent", 0), line="tx%d" % totals["sent"])
+            REMOTE, 100, ("sent", 0), None, "tx%d" % totals["sent"])
 
-    def arrive(names, sem, n):
-        rec(None, None, [A(k) for k in names], [], token=(sem, n), line=sem)
+    def arrive(names, sem, n, more=0.0):
+        rec(None, None, [A(k) for k in names], [], more, 0, (sem, n), None, sem, [len(ops) - 1])
 
-    def bank(b, n=C):
-        return A("ps", 512 * b, 512 * b + n)
+    def bank(b, lo=0, hi=C):
+        return A("ps", 512 * b + lo, 512 * b + hi)
 
-    load("y", "xin", T.xin[:], T.x[:], "ldx")
-    load("s", "uin", T.uin[:], T.u[:], "ldu")
-    load("y", "qw", T.qw[:].bitcast(dt.uint8), T.wc[:], "ldw")
-    load("y", "sw", T.sw[:], T.ws[:], "lds")
-    load("y", "vin", T.vin[:], T.v[:], "ldv")
+    def H(name, h, base=0, first=0, step=1):
+        return A(name, base + 128 * h + first, base + 128 * h + 128, step)
 
-    i16, cut8, invk = A("cf", 0, 1), A("cf", 1, 2), A("cf", 2, 3)
-    jw, radj, inv2m = A("cf", 32, 48), A("cf", 48, 64), A("cf", 64, 70)
-    two, zero, root, jw2 = A("cf", 112, 128), A("cf", 128, 144), A("cf", 144, 160), A("cf", 160, 176)
+    def F(k, n=1):
+        return A("cf", k, k + n)
+
+    def own(name, k, h, lo=0, hi=128):
+        return A(name, BLOCK * k + 256 * h + lo, BLOCK * k + 256 * h + hi)
+
+    def win(name, k, h, hi=128):
+        return A(name, BLOCK * k + 128 * h, BLOCK * k + 256 * h + hi)
+
+    for h in range(2):
+        load("y", A("xin", 512 * h, 512 * h + 512), T.xin[:, 512 * h:512 * h + 512], T.x[:, 512 * h:512 * h + 512], "ldx%d" % h)
+    load("s", A("uin"), T.uin[:], T.u[:], "ldu")
+    load("y", A("qw"), T.qw[:].bitcast(dt.uint8), T.wc[:], "ldw")
+    load("y", A("sw"), T.sw[:], T.ws[:], "lds")
+    load("y", A("vin"), T.vin[:], T.v[:], "ldv")
+    quant(A("qu"), A("su"), A("uin"))
+    quant(A("qv"), A("sv"), A("vin"))
+    for h in range(2):
+        quant(H("qx0", h), H("sx0", h), A("xin", 512 * h, 512 * h + 512))
+
+    i16, p32, cut, invk, i4, inv4, b256, ifr, odd16 = [F(k) for k in range(9)]
+    jw, root, radj, kfr, two, zero = [F(16 * k, 16) for k in range(1, 7)]
+    spread, turned, lines = A("cl", 0, 16), A("cl", 16, 24), A("cl", 24, 31)
     iota(A("ci", 16, 17), [[0, 1]], 0, 1)
-    iota(A("posd"), [[0, 16], [1, 16]], 0, 0, True)
+    iota(A("posd"), [[0, 8], [1, 16]], 0, 0)
     iota(A("ci", 0, 16), [[32, 8], [0, 2]], 0, 0)
     iota(A("ci", 32, 48), [[1, 16]], 0, 0)
-    iota(A("jrow"), [[1, 256]], 0, 0, True)
-    fill(A("dj"), 0.5)
-    fill(A("keep"), 1.0)
-    fill(A("z"), 0.0)
-    fill(A("ones"), 1.0)
+    iota(A("jrow"), [[1, 256]], 0, 0)
+    iota(A("pos4"), [[0, 8], [1, 4]], 0, 0)
     ts(A("ci", 17, 18), A("ci", 16, 17), 15, OP.bitwise_and)
     ts(A("ci", 18, 19), A("ci", 16, 17), 31, OP.bitwise_and)
-    fill(two, 256.0)
-    fill(zero, 0.0)
-    cp(i16, A("ci", 17, 18))
-    cp(A("cf", 3, 4), A("ci", 18, 19))
-    fill(A("keep", 0, 256, 16), 0.0)
-    fill(A("dj", 0, 256, 16), 0.0)
-    fill(A("cf", 112, 128, 3), 2.0 ** -15)
-    ts(cut8, i16, -1.0, OP.mult, 8.0, OP.add)
-    fill(A("dj", 9, 256, 16), 1.0)
+    ts(A("ci", 19, 20), A("ci", 16, 17), 2, OP.logical_shift_right, 3, OP.bitwise_and)
+    ts(A("ci", 20, 21), A("ci", 16, 17), 3, OP.bitwise_and)
+    cp(F(0, 2), A("ci", 17, 19))
+    cp(i4, A("ci", 19, 20))
+    ts(b256, A("ci", 20, 21), 256.0, OP.mult)
+    tt(odd16, p32, i16, OP.subtract)
+    ts(cut, i16, 8.0, OP.subtract, -2 * ROUND, OP.mult)
+    ts(cut, cut, -0.498046875, OP.add, 1.0, OP.min)
+    ts(cut, cut, -ROUND, OP.max)
+    fill(A("dj"), 0.5)
+    fill(part(A("dj", 0, 256, 16), "dj0"), 0.0)
+    fill(part(A("dj", 9, 256, 16), "dj9"), 1.0)
+    fill(part(A("dj", 10, 256, 16), "dj10"), -1.0)
+    ts(part(A("dj", 8, 256, 16), "dj8"), A("ci", 0, 16), p32, OP.add, 0.5, OP.mult)
+    for op in ops[-4:]:
+        op["rd"] = op["rd"] + [("dj", 0, 256)]
+    ts(turned, A("ci", 32, 40), 16.0, OP.mult, 10.0, OP.add)
     ts(A("posd"), A("posd"), i16, OP.subtract)
-    ts(cut8, cut8, 1.0, OP.min, -0.498046875, OP.max)
-    ts(A("dj", 8, 256, 16), A("ci", 0, 16), A("cf", 3, 4), OP.add, 0.5, OP.mult)
     ts(A("kd"), A("posd"), 1.0, OP.is_equal, HOLD, OP.mult)
     ts(A("kd2"), A("posd"), 2.0, OP.is_ge)
-    quant(A("qu"), A("su"), A("uin"))
-    quant(A("qx0"), A("sx0"), A("xin"))
-    ts(A("dmx"), A("posd"), 0.0, OP.is_equal)
-    scan(A("pw"), two, zero, 2.0 ** 15, OP.mult, OP.add)
-    cp(A("exl"), A("ci", 32, 48))
+    tt(A("kd"), A("kd"), A("kd2"), OP.add)
     ts(invk, i16, 15.0, OP.is_equal, 1.0 / HOLD, OP.max)
+    ts(A("pos4"), A("pos4"), i4, OP.subtract)
+    ts(A("k4", 0, 32), A("pos4"), 1.0, OP.is_equal, HOLD, OP.mult)
+    ts(A("k42"), A("pos4"), 2.0, OP.is_ge)
+    tt(A("k4", 0, 32), A("k4", 0, 32), A("k42"), OP.add)
+    for n in (32, 64, 128):
+        act(A("k4", n, 2 * n), A("k4", 0, n))
+    ts(inv4, i4, 3.0, OP.is_equal, 1.0 / HOLD, OP.max)
+    fill(two, 256.0)
+    fill(A("cf", 80, 96, 3), 2.0 ** -15)
+    fill(zero, 0.0)
+    scan(A("pw"), two, zero, 2.0 ** 15, OP.mult, OP.add)
+    cp(spread, A("ci", 32, 48))
+    ts(A("dmx"), A("posd"), 0.0, OP.is_equal)
+    for h in range(2):
+        tt(own("sa", 0, h), ind(A("pw"), A("cl", 8 * h, 8 * h + 8)), A("dmx"), OP.mult)
+    fill(A("sa", 0, 1), 0.0)
+    for h in range(2):
+        act(own("sa", 1, h), own("sa", 0, h))
+    for name, blocks in (("jr", 4), ("sa", 5), ("wz", 3)):
+        for k in range(blocks):
+            act(A(name, BLOCK * k + 128, BLOCK * k + 256), A("jrow", 0, 128), scale=float(name == "jr"))
+    act(A("jfr"), A("jrow"), scale=1.0 / C)
+    ts(ifr, i16, 1.0 / C, OP.mult)
+    ts(kfr, A("ci", 32, 48), 16.0 / C, OP.mult)
+    ts(jw, A("ci", 32, 48), 16.0, OP.mult, i16, OP.add)
+    ts(root, jw, 0.0, OP.is_equal)
+    ts(radj, root, float(C), OP.mult)
+    fill(A("ones"), 1.0)
+    fill(A("keep"), 1.0)
+    fill(A("keep", 0, 256, 32), 0.0)
+    act(A("z"), A("ones"), scale=0.0)
+    fill(A("wf", 52, 54), 0.0)
+    fill(A("ssrt", 0, 16), 0.0)
+    fill(A("same", 0, 1), 1.0)
+    fill(A("same", 1, 257, 255), 0.0)
+    for b in range(4):
+        o = A("et", 512 * b, 512 * b + 512)
+        rec("g", lambda e, o=o, b=b: e.affine_select(o[0], T.ones[:], [[1, 512]], OP.is_equal, 0.0, -b, -4), [o], [A("ones")], 170 + 1024 * CYCLE)
+        quant(A("qe", 128 * b, 128 * b + 128), A("se", 128 * b, 128 * b + 128), o)
+    for name, n in (("mb4", 4), ("mb16", 16)):
+        act(A(name), A("ones"), scale=BIG)
+        fill(A(name, 0, 512, n), -BIG)
+    fill(A("mbm"), BIG)
+    fill(A("mbm", 0, 112, 16), -BIG)
+    fill(A("mbm", 1, 112, 17), -BIG)
+    for h in range(2):
+        act(A("tab", MID + 512 * h, MID + 512 * h + 512), A("ones"), scale=-BIG)
+    ts(F(112, 7), A("ci", 33, 40), i16, OP.is_gt)
+    ts(F(120, 7), A("ci", 33, 40), -1.0, OP.mult, 15.0, OP.add)
+    tt(F(112, 7), F(112, 7), F(120, 7), OP.mult)
+    ts(lines, F(112, 7), i16, OP.add, 16.0, OP.mult)
 
-    def late_constants(step):
-        if step == 0:
-            tt(A("kd"), A("kd"), A("kd2"), OP.add)
-        if step == 1:
-            tt(A("a0"), ind(A("pw"), A("exl")), A("dmx"), OP.mult)
-        if step == 2:
-            ts(jw, A("ci", 32, 48), 16.0, OP.mult, i16, OP.add)
-            fill(A("a0", 0, 1), 0.0)
-        if step == 3:
-            fill(A("p256", 0, 1), 255.0)
-            act(A("a1"), A("a0"), AF.Copy)
-            ts(root, jw, 0.0, OP.is_equal)
-        if step == 4:
-            ts(jw2, jw, 256.0, OP.add)
-        if step == 5:
-            tt(jw2, jw2, root, OP.subtract)
+    def L(k, h, lo=0, hi=128):
+        return A("lst", 16 * k + 8 * h + lo // 16, 16 * k + 8 * h + hi // 16)
 
-    def later_constants(a):
-        if a == 32:
-            ts(radj, root, 256.0, OP.mult, -1.0, OP.add)
-            fill(two, 0.5)
-        if a == 64:
-            fill(A("ssrt", 0, 16), 0.0)
-            scan(inv2m, A("cf", 112, 118), A("cf", 128, 134), 2.0, OP.mult, OP.add)
-        if a == 128:
-            fill(A("p1", 0, 1), 255.0)
+    def wrap(out, held, row):
+        name, lo, hi = held[1][0]
+        scan(held, A("kd", 0, hi - lo), row, 0.0, OP.mult, OP.max)
+        ts(out, A(name, lo + 15, hi, 16), invk, OP.mult)
 
-    def unpackers():
-        for b in range(4):
-            o = A("et", 512 * b, 512 * b + 512)
-            rec("g", lambda e, o=o, b=b: e.affine_select(o[0], T.ones[:], [[1, 512]], OP.is_equal, 0.0, -b, -4), [o], [A("ones")])
+    def path_sums(name, blocks, h, out):
+        for k in range(STEPS):
+            tt(out if k == STEPS - 1 else own(name, blocks[k + 2], h), ind(win(name, blocks[k + 1], h), L(max(k - 1, 0), h)), own(name, blocks[k], h), OP.add)
 
-    def table_constants():
-        fill(A("mb"), BIG)
-        quant(A("qv"), A("sv"), A("vin"))
-        fill(A("mb", 0, 512, 8), -BIG)
-
-    def L(k):
-        return A("lst", 16 * k, 16 * k + 16)
-
-    def sweep(name, base, between, last):
-        for a in range(32, 256, 32):
-            own = A(name, base + a, base + a + 32)
-            tt(own if a < 224 or last is None else last, ind(A(name, base, base + a), A("lst", 112 + a // 16, 114 + a // 16)), own, OP.add)
-            between(a)
-
-    def H(name, h, first=0, step=1):
-        return A(name, 128 * h + first, 128 * h + 128, step)
-
-    def requant(t, h):
-        quant(H("qx%d" % t, h), H("sx%d" % t, h), part(A("xn", 512 * h, 512 * h + 512), *["xn%d%d" % (h, b) for b in range(4)]))
+    def sweep(name, base, first, last, out=None):
+        for a in range(first, last, 32):
+            run = A(name, base + a, base + a + 32)
+            tt(out if out and a + 32 == last else run, ind(A(name, base, base + a), L(STEPS, 0, a, a + 32)), run, OP.add)
 
     def W(k, n=1):
         return A("iw", 16 * k, 16 * (k + n))
+
+    def V(k, n=1):
+        return A("iv", 16 * k, 16 * (k + n))
+
+    def tab(region, lo, hi, step=1):
+        return A("tab", region + lo, region + hi, step)
 
     for t in range(R):
         peer = T.cores[rank ^ (1 << t)]
@@ -314,226 +428,170 @@ def rank_program(g, core, T, topo):
         engines = len(topo.engines(peer, core))
         for h in range(2):
             mm(4 + h, "qu", "su", 0, qx, sx, 128 * h, 128 * h + 128)
+            ts(H("r1", h), bank(4 + h, 0, 128), 0.0, OP.is_gt, cut, OP.min)
+            turn(H("r2", h), H("r1", h))
+            dj = H("dj", h)
+            scan(H("r3", h), (dj[0], dj[1] + [(k, 0, 1) for k in ("dj0", "dj8", "dj9", "dj10")]) + dj[2:], H("r2", h), 0.0, OP.mult, OP.add)
+            act(H("r4", h), ind(H("r3", h), turned), scale=-1.0)
+            turn(own("jr", 0, h), H("r4", h))
+            wrap(L(0, h), H("hd", h), own("jr", 0, h))
+            for op in ops[-8:]:
+                op["lead"] = LEAD * (1 - h)
         send(peer, T[qp][:].bitcast(dt.uint8), T[qx][:].bitcast(dt.uint8), qx, "aq%d" % t)
         send(peer, T[sp][:], T[sx][:], sx, "aq%d" % t)
-        arrive([qp, sp], "aq%d" % t, 2 * engines)
-        if t == 0:
-            unpackers()
-        stages = [
-            lambda h: ts(H("r1", h), bank(4 + h, 128), 0.0, OP.is_gt, cut8, OP.min),
-            lambda h: turn(H("r2", h), H("r1", h)),
-            lambda h: scan(H("xs", h), H("dj", h), H("r2", h), 0.0, OP.mult, OP.add),
-            lambda h: ts(H("z", h, 0, 16), H("xs", h, 9, 16), ROUND, OP.add, ROUND, OP.subtract),
-            lambda h: scan(H("r4", h), H("keep", h), H("z", h), 0.0, OP.mult, OP.add),
-            lambda h: turn(H("j0", h), H("r4", h)),
-            lambda h: scan(H("r3", h), H("kd", h), H("j0", h), 0.0, OP.mult, OP.max),
-            lambda h: ts(A("lst", 8 * h, 8 * h + 8), H("r3", h, 15, 16), invk, OP.mult)]
-        for n, stage in enumerate(stages):
-            stage(0)
-            stage(1)
-            if t == 0:
-                late_constants(n)
-        act(A("p256", 1, 256), A("j0", 1, 256), AF.Identity, bias=256.0, scale=256.0)
-        keyw, sg = A("wf", 16, 32), A("wf", 32, 48)
-        jn, an = ["j0", "ja", "jb", "jd", "ja", "jb", "jd", "ja"], ["a1", "a0", "aa", "ab", "ac", "aa", "ab", "ac", "aa"]
-        for k in range(8):
-            held = "r5" if k % 2 else "r3"
-            if k not in (0, 6):
-                scan(A(held), A("kd"), A(jn[k]), 0.0, OP.mult, OP.max)
-            if k == 6:
-                scan(A("key"), A("jrow"), A("p256"), 0.0, OP.min, OP.add)
-            if k < 7:
-                act(A(jn[k + 1]), ind(A(jn[k]), L(max(k - 1, 0))), AF.Copy)
-                tt(A(an[k + 2]), ind(A(an[k + 1]), L(max(k - 1, 0))), A(an[k]), OP.add)
-            if k == 0:
-                ts(keyw, L(0), 256.0, OP.mult)
-            if k == 6:
-                tt(keyw, keyw, jw2, OP.add)
-            if k not in (0, 6):
-                ts(L(k), A(held, 15, 256, 16), invk, OP.mult)
-
-        def beside_bits(a):
-            if a == 96:
-                cp(A("ai", 0, 96), A("aa", 0, 96))
-            if a in (160, 224):
-                cp(A("ai", a - 64, a), A("aa", a - 64, a))
-            if t == 0:
-                later_constants(a)
-
-        sweep("aa", 0, beside_bits, A("ai", 224, 256))
-        for k in range(16):
-            act(A("junk", 256 * k, 256 * k + 256), A("key"), AF.Sign, bias=A("wf", 16 + k, 17 + k), scale=-1.0, acc=A("wf", 32 + k, 33 + k))
-        for m in range(7):
-            if m < 6:
-                ts(A("msk", 304 * m, 256 * m + 256), A("ai", 48 * m, 256), 0x010101 << m, OP.bitwise_and)
-            if m >= 1:
-                lo, n = 304 * (m - 1), 128 - 24 * (m - 1)
-                tt(A("hm", 128 * m - 128, 128 * m - 128 + n), A("msk", lo, lo + n), A("msk", lo + n, lo + 2 * n), OP.add)
-            if m >= 5:
-                total(A("wf", 43 + m, 44 + m), A("hm", 128 * (m - 5), 104 * (m - 5) + 128))
-        for m in range(2, 6):
-            total(A("wf", 48 + m, 49 + m), A("hm", 128 * m, 104 * m + 128))
-        tt(A("wi", 32, 38), A("wf", 48, 54), inv2m, OP.mult)
+        arrive([qp, sp], "aq%d" % t, 2 * engines, 2000.0)
+        ring = [0] + [1 + k % 3 for k in range(STEPS)]
+        for h in range(2):
+            for k in range(STEPS):
+                act(own("jr", ring[k + 1], h), ind(win("jr", ring[k], h), L(max(k - 1, 0), h)))
+                if k != STEPS - 2:
+                    wrap(L(k + 1, h), H("hd", h, 256 * k + 256), own("jr", ring[k + 1], h))
+            path_sums("sa", [0, 1] + [2 + k % 3 for k in range(STEPS)], h, H("af", h))
+        sweep("af", 0, 32, C, A("ai", 224, C))
+        for lo, hi in ((0, 128), (128, CUT), (CUT, 224)):
+            cp(A("ai", lo, hi), A("af", lo, hi))
+        for a in range(32, 128, 32):
+            act(own("jr", ring[-1], 1, a, a + 32), ind(win("jr", ring[-1], 1, a), L(STEPS, 1, a, a + 32)))
+        wrap(L(STEPS + 1, 1), H("hd", 1, 256 * STEPS + 256), own("jr", ring[-1], 1))
+        for h in range(2):
+            name, lo, hi = own("jr", 0, h)[1][0]
+            scan(A("key", 128 * h, 128 * h + 128, -1), A("jfr", 128 * h, 128 * h + 128, -1), A(name, lo, hi, -1), 1.0, OP.min, OP.add)
+            keyw = A("wf", 16 + 8 * h, 24 + 8 * h)
+            ts(keyw, L(0, h), ifr, OP.add)
+            tt(keyw, keyw, F(64 + 8 * h, 8), OP.add)
+            for k in range(8 * h, 8 * h + 8):
+                act(A("junk", 128 * k, 128 * k + 128), H("key", h), AF.Sign, A("wf", 16 + k, 17 + k), -1.0, A("wf", 32 + k, 33 + k))
+            ts(A("rkl", 8 * h, 8 * h + 8), A("wf", 32 + 8 * h, 40 + 8 * h), 127.0, OP.add, 0.5, OP.mult)
+            scatter(H("srow", h), A("rkl", 8 * h, 8 * h + 8), A("jrow", 0, 128))
+            wrap(A("sgl", 8 * h, 8 * h + 8), H("shd", h), H("srow", h))
+            act(H("psrt", h), ind(own("jr", 0, h), A("sgl", 8 * h, 8 * h + 8)))
+            lo, hi = 2 + 127 * h, 128 * h + 128
+            scan(A("step", lo, hi), A("psrt", lo - 1, hi - 1), A("psrt", lo, hi), 0.0, OP.max, OP.subtract)
+            ts(A("same", lo, hi), A("step", lo, hi), 0.0, OP.is_equal)
+        for lo, lists in ((0, [A("sgl", 0, 8), L(0, 1)]), (16, [A("sgl", 8, 16)])):
+            hi = lo + 8 * len(lists)
+            for k, names in enumerate(lists):
+                cp(A("wi", lo + 8 * k, lo + 8 * k + 8), names)
+            ts(A("wi", 64 + lo, 64 + hi), A("wi", lo, hi), 240, OP.bitwise_and)
+            tt(A("wf", 64 + lo, 64 + hi), A("wi", 64 + lo, 64 + hi), A("wi", lo, hi), OP.add)
+            ts(A("spl", lo, hi), A("wf", 64 + lo, 64 + hi), odd16, OP.add)
+        at, rest = 0, C - CUT
+        for m in range(CUT // 48):
+            first = at
+            for lo, hi in ((48 * m, 128), (max(48 * m, 128), CUT)):
+                n = hi - lo
+                if n > 0:
+                    ts(A("msk", at, at + n), A("ai", lo, hi), m, OP.logical_shift_right, 0x010101, OP.bitwise_and)
+                    tt(A("hm", at // 2, (at + n) // 2), A("msk", at, at + n // 2), A("msk", at + n // 2, at + n), OP.add)
+                    at += n
+            total(A("wf", 48 + m, 49 + m), A("hm", first // 2, at // 2))
+        for m in range(6):
+            ts(A("msk", at + rest * m, at + rest * m + rest), A("ai", CUT, C), m, OP.logical_shift_right, 0x010101, OP.bitwise_and)
+        for lo in range(0, 6 * rest, 3 * rest):
+            tt(A("hm", (at + lo) // 2, (at + lo + 3 * rest) // 2), A("msk", at + lo, at + lo + 3 * rest, 2), A("msk", at + lo + 1, at + lo + 3 * rest, 2), OP.add)
+        scan(A("hm", 512, 512 + 3 * rest), A("keep", 0, 3 * rest), A("hm", at // 2, at // 2 + 3 * rest), 0.0, OP.mult, OP.add)
+        tt(A("wi", 32, 38), A("wf", 48, 54), A("hm", 512 + 31, 512 + 3 * rest, 32), OP.add)
         for f in range(3):
             ts(part(A("szw", f, 18, 3), "sz%d" % f), A("wi", 32, 38), 8 * f, OP.logical_shift_right, 255, OP.bitwise_and)
         size = part(A("szw", 0, 16), "sz0", "sz1", "sz2")
-        tt(A("z", 0, 256, 16), size, root, OP.add)
-        tt(W(4), size, radj, OP.add)
-        scan(A("r2"), A("keep"), A("z"), 0.0, OP.mult, OP.add)
-        ts(A("rkl"), sg, 255.0, OP.add, 0.5, OP.mult)
-        turn(A("r1"), A("r2"))
-        ts(W(5), W(4), 1.0, OP.min)
-        scan(A("r3"), A("kd"), A("r1"), 0.0, OP.mult, OP.max)
-        scatter(A("r4"), A("rkl"), A("jrow"))
-        ts(A("z", 0, 256, 16), A("r3", 15, 256, 16), invk, OP.mult)
-        act(A("p1", 1, 256), A("j0", 1, 256), AF.Identity, bias=255.0, scale=256.0)
-        scan(A("r5"), A("kd"), A("r4"), 0.0, OP.mult, OP.max)
-        scan(A("r2"), A("keep"), A("z"), 0.0, OP.mult, OP.add)
-        ts(A("sgl"), A("r5", 15, 256, 16), invk, OP.mult)
-        turn(A("r1"), A("r2"))
-        act(A("psrt"), ind(A("p256"), A("sgl")), AF.Copy)
-        ts(W(6), W(4), 1.0, OP.min, -1.0, OP.mult)
-        cp(A("ssrt", 16, 272), ind(A("r1"), A("sgl")))
-        scan(A("cum"), A("ssrt", 15, 271), A("psrt"), 0.0, OP.add, OP.max)
-        for h in range(2):
-            tt(A("wz", 256 + 128 * h, 384 + 128 * h), ind(A("cum"), A("rkl", 8 * h, 8 * h + 8)), H("p1", h), OP.subtract)
-        for k in range(7):
-            for h in range(2):
-                if k == 0:
-                    cp(H("wz", h), A("wz", 256 + 128 * h, 384 + 128 * h))
-            for h in range(2):
-                s0, n = 256 * k + 128 * h, 16 * max(k - 1, 0) + 8 * h
-                tt(A("wz", s0 + 512, s0 + 640), ind(A("wz", 256 * k + 256, s0 + 384), A("lst", n, n + 8)), A("wz", s0, s0 + 128), OP.add)
-
-        def beside_places(a):
-            b = a // 32 - 1
-            if t == 0 and b < 4:
-                quant(A("qe", 128 * b, 128 * b + 128), A("se", 128 * b, 128 * b + 128), A("et", 512 * b, 512 * b + 512))
-            if a == 160:
-                scan(H("r3", 0), H("kd", 0), A("wz", 2048, 2176), 0.0, OP.mult, OP.max)
-            if a == 192:
-                ts(A("pll", 0, 8), H("r3", 0, 15, 16), invk, OP.mult)
-
-        sweep("wz", 2048, beside_places, None)
-        for b in range(4):
-            mm(b, "qe", "se", b, qp, sp)
-        for b in range(4):
-            act(A("tp", 256 * b, 256 * b + 256), bank(b), AF.Copy)
-        for b in range(4):
-            mm(b, "qe", "se", b, qx, sx)
-        if t == 0:
-            act(A("tab", TOP, 4096), A("junk", 0, 1024), AF.Copy)
-        if t == R - 1:
-            act(A("po"), A("j0"), AF.Copy)
-            store("y", T.op[:], T.po[0:128:16, :], "po")
-        scan(H("r3", 1), H("kd", 1), A("wz", 2176, 2304), 0.0, OP.mult, OP.max)
-        ts(A("pll", 8, 16), H("r3", 1, 15, 16), invk, OP.mult)
-        scatter(A("r1"), A("pll"), A("jrow"))
-        l, r, l8, r8 = W(0), W(1), W(2), W(3)
-        cp(l, A("pll"))
-        scan(A("r3"), A("kd"), A("r1"), 0.0, OP.mult, OP.max)
-        tt(r, l, W(4), OP.add)
-        ts(A(ol), A("r3", 15, 256, 16), invk, OP.mult)
+        tt(A("z", 0, 512, 32), size, radj, OP.add)
+        for lo in (256, 0):
+            scan(A("zb", lo, lo + 256), A("keep"), A("z", lo, lo + 256), 0.0, OP.mult, OP.add)
+            turn(A("zt", lo, lo + 256), A("zb", lo, lo + 256))
+        cp(A("ssrt", 144, 272), ind(A("zt", 256, 512), A("spl", 16, 24)))
+        cp(A("ssrt", 16, 144), ind(A("zt", 0, 256), A("spl", 0, 8)))
+        act(A("szp"), ind(A("zt"), A("spl", 8, 16)))
+        scan(H("cum", 0), A("ssrt", 15, 143), H("same", 0), -1.0, OP.add, OP.mult)
+        scan(A("cum", 128, 256, -1), A("same", 129, 257, -1), A("ssrt", 144, 272, -1), 0.0, OP.mult, OP.subtract)
+        for k in range(2):
+            act(own("wz", k, 0), ind(H("cum", 0), A("rkl", 0, 8)), AF.Identity, 1.0)
+            tt(own("wz", k, 1), ind(H("cum", 1), A("rkl", 8, 16)), A("szp"), OP.add)
+        ring = [k % 3 for k in range(STEPS + 2)]
+        path_sums("wz", ring, 0, H("pf", 0))
+        path_sums("wz", ring, 1, own("wz", ring[-1], 1))
+        sweep("pf", 0, 32, 128)
+        sweep("wz", BLOCK * ring[-1] + 128, 160, C)
+        for lo, hi in ((0, 128),) + LAST:
+            if lo:
+                tt(A("pf", lo, hi), ind(H("pf", 0), L(STEPS + 1, 0, lo, hi)), own("wz", ring[-1], 1, lo - 128, hi - 128), OP.add)
+            wrap(A("pll", lo // 16, hi // 16), A("phd", lo, hi), A("pf", lo, hi))
+            scatter(A("orow"), A("pll", lo // 16, hi // 16), A("jrow", lo, hi))
+        scan(A("ohd"), A("k4"), A("orow"), 0.0, OP.mult, OP.max)
+        ts(A(ol), A("ohd", 3, C, 4), inv4, OP.mult, b256, OP.add)
         send(peer, T[lp][:], T[ol][:], ol, "al%d" % t)
         arrive([lp], "al%d" % t, engines)
-        ts(A("wi", 32, 64), W(0, 2), 0.125, OP.mult, -0.4375, OP.add)
-        tt(W(20, 2), W(0, 2), W(5, 2), OP.add)
-        if t == 0:
-            table_constants()
-        ts(W(2, 2), A("wi", 32, 64), 8.0, OP.mult)
-        tt(W(7), r, l8, OP.subtract)
-        tt(W(8), l, r8, OP.subtract)
-        tt(W(9), l, l8, OP.subtract)
-        tt(W(10), r8, l8, OP.subtract)
-        ts(W(15), l8, float(TOP + 5), OP.add)
-        ts(W(11), W(7), 7.0, OP.is_ge, float(SF), OP.mult)
-        ts(W(12), W(8), 0.0, OP.is_le, float(PF), OP.mult)
-        ts(W(13), W(7), 4.0, OP.is_ge)
-        ts(W(14), W(9), 2.0, OP.is_le)
-        ts(W(16), W(10), 24.0, OP.is_ge, float(TOP - SF + 1), OP.mult)
-        ts(W(17), W(10), 24.0, OP.is_ge, float(TOP - SF + 1 - 8), OP.mult)
-        tt(W(15), W(15), W(20), OP.subtract)
-        tt(W(28, 2), W(0, 2), W(11, 2), OP.add)
-        tt(W(13), W(13), W(14), OP.mult)
-        tt(W(22, 2), W(2, 2), W(16, 2), OP.add)
-        ts(W(4), W(10), 40.0, OP.is_ge)
-        ts(W(5), W(10), 40.0, OP.is_lt, 15.0, OP.mult)
-        ts(W(6), W(10), 72.0, OP.is_ge, float(SF + 8), OP.add)
-        ts(W(7), W(10), 72.0, OP.is_lt, 31.0, OP.mult)
-        ts(W(8), W(10), 136.0, OP.is_ge)
-        ts(W(9), W(10), 136.0, OP.is_lt, 63.0, OP.mult)
         for b in range(4):
-            o, win = part(A("bt", b, 1024, 4), "bt%d" % b), ind(A("tp", 256 * b, 256 * b + 256), A(lp))
-            if b % 2:
-                act(o, win, AF.Copy)
-            else:
-                cp(o, win)
-        tt(W(15), W(15), W(13), OP.mult)
-        ts(W(23), W(23), float(SF - 8 - 15 - 31 - 63), OP.add)
-        quant(A("qf"), A("sf"), part(A("bt"), "bt0", "bt1", "bt2", "bt3"))
-        tt(W(4, 2), W(4, 2), W(6, 2), OP.add)
-        ts(W(24), W(10), 16.0, OP.is_ge)
-        tt(W(20), W(20), W(15), OP.add)
-        tt(W(22, 2), W(22, 2), W(8, 2), OP.add)
-        ts(W(25), W(10), 16.0, OP.is_ge)
-        tt(W(4, 2), W(4, 2), W(20, 2), OP.subtract)
-        tt(W(22, 2), W(22, 2), W(4, 2), OP.add)
-        tt(W(22, 2), W(22, 2), W(24, 2), OP.mult)
-        for b in range(4):
-            mm(4 + b, "qw", "sw", b, "qf", "sf")
-        for b in range(4):
-            act(A("tab", 256 * b, 256 * b + 256), bank(4 + b), AF.Copy, scale=0.03125)
-
-        def suffix(b):
-            scan(A("tab", SF + 256 * b, SF + 256 * b + 256, -1), A("mb", 0, 256), A("tab", 256 * b, 256 * b + 256, -1), -BIG, OP.min, OP.max)
-
-        def prefix(h):
-            scan(A("tab", PF + 512 * h, PF + 512 * h + 512), A("mb"), A("tab", 512 * h, 512 * h + 512), -BIG, OP.min, OP.max)
-
-        def top(k, lo, n):
-            base = SF if k == 0 else TOP + k
-            v = A("tab", base + 8 * lo, base + 8 * (lo + n - 1) + 1, 8)
-            return v if k == 0 else part(v, "top%d" % k)
-
-        suffix(0)
-        tt(W(30, 2), W(22, 2), W(20, 2), OP.add)
-        suffix(1)
-        cp(A("idx"), W(28, 4))
-        suffix(2)
-        suffix(3)
-        for b in range(4):
-            act(A("m1", 256 * b, 256 * b + 256), ind(A("tab", 256 * b, SF + 256 * b + 256), A("idx", 0, 16)), AF.Copy)
-        tt(A("etmp"), A("tab", 2, 1024, 8), A("tab", 3, 1024, 8), OP.max)
-        tt(top(1, 0, 127), top(0, 0, 127), top(0, 1, 127), OP.max)
-        prefix(0)
-        tt(top(2, 0, 125), top(1, 0, 125), top(1, 2, 125), OP.max)
-        tt(top(5, 0, 128), A("etmp"), A("tab", 4, 1024, 8), OP.max)
-        tt(top(3, 0, 121), top(2, 0, 121), top(2, 4, 121), OP.max)
-        prefix(1)
-        tt(top(4, 0, 113), top(3, 0, 113), top(3, 8, 113), OP.max)
-        tops = [("top%d" % k, 0, 1) for k in range(1, 6)]
-        mn = ["m1", "m2", "m1", "m2"]
-        for s in range(1, 4):
+            mm(b, "qe", "se", b, qp, sp)
+            act(A("tp", 256 * b, 256 * b + 256), bank(b))
+            mm(b, "qe", "se", b, qx, sx)
+        if t == R - 1:
+            for h in range(2):
+                act(H("po", h), own("jr", 0, h))
+            store("y", T.op[:], T.po[0:128:16, :], A("po"))
+        for k in range(2):
+            tt(W(k), size, radj, OP.add)
+            ts(V(k), A("pll"), -float(k), OP.add)
+        tt(V(2, 2), V(0, 2), W(0, 2), OP.add)
+        ts(V(4, 4), V(0, 4), 2, OP.arith_shift_right)
+        ts(V(8, 4), V(0, 4), 4, OP.arith_shift_right)
+        tt(W(2, 2), V(6, 2), V(4, 2), OP.is_gt)
+        tt(W(4, 2), V(10, 2), V(8, 2), OP.is_gt)
+        tt(W(6), V(7), V(4), OP.subtract)
+        tt(W(7), V(11), V(8), OP.subtract)
+        tt(W(8, 2), W(2, 2), W(4, 2), OP.add)
+        ts(W(10), W(8), float(S4 - RAW), OP.mult, float(RAW - S16), OP.add)
+        ts(W(11), W(9), float(P4 - RAW), OP.mult)
+        tt(W(22), W(10), V(0), OP.add)
+        tt(W(23), W(11), V(3), OP.add)
+        ts(W(12), W(6), 2.0, OP.is_equal)
+        ts(W(18), W(7), 16.0, OP.mult, 3.0, OP.add)
+        tt(W(13), W(6), W(18), OP.is_equal)
+        ts(W(14), W(7), 2.0, OP.is_ge)
+        ts(W(15), V(4), 4.0, OP.mult, float(S4 - MID + 4), OP.add)
+        ts(W(16), V(8), 16.0, OP.mult, 15.0, OP.add)
+        ts(W(19), V(8), -17.0, OP.mult, 222.0, OP.add)
+        tt(W(20), W(16), W(19), OP.min)
+        tt(W(17), W(20), V(11), OP.add)
+        tt(W(12, 3), W(12, 3), W(15, 3), OP.mult)
+        tt(W(21), W(12), W(13), OP.add)
+        tt(W(24), W(21), W(14), OP.add)
+        cp(A("idx", 0, 32), W(22, 2))
+        cp(A("idx", 32, 48), W(24))
+        for h in range(2):
+            for q in (2 * h, 2 * h + 1):
+                (act if q % 2 else cp)(A("bt", 256 * q, 256 * q + 256), ind(A("tp"), A(lp, 16 * q, 16 * q + 16)))
+            quant(H("qf", h), H("sf", h), A("bt", 512 * h, 512 * h + 512))
             for b in range(4):
-                win = A("tab", 256 * b, (PF if s == 1 else TOP) + 256 * b + 256)
-                if s > 1:
-                    win = (win[0], win[1] + tops, [])
-                tt(A(mn[s], 256 * b, 256 * b + 256), ind(win, A("idx", 16 * s, 16 * s + 16)), A(mn[s - 1], 256 * b, 256 * b + 256), OP.max)
+                mm(4 + b, "qw", "sw", b, "qf", "sf", 128 * h, 128 * h + 128)
+                lo = 256 * b + 128 * h
+                act(tab(RAW, lo, lo + 128), bank(4 + b, 0, 128), scale=0.03125)
+                scan(tab(S16, lo, lo + 128, -1), A("mb16", 0, 128), tab(RAW, lo, lo + 128, -1), -BIG, OP.min, OP.max)
+        for region, mask, step in ((S4, "mb4", -1), (P4, "mb4", 1), (P16, "mb16", 1)):
+            for lo in (0, 512):
+                scan(tab(region, lo, lo + 512, step), A(mask), tab(RAW, lo, lo + 512, step), -BIG, OP.min, OP.max)
+        for b in range(4):
+            act(A("mg", 112 * b, 112 * b + 112), ind(tab(S16, 256 * b, 256 * b + 256), lines))
+            scan(tab(MID, 256 * b + 16, 256 * b + 128), A("mbm"), A("mg", 112 * b, 112 * b + 112), -BIG, OP.min, OP.max)
+        tt(tab(MID, 15, 1024, 16), tab(S4, 4, 1024, 16), tab(S4, 8, 1024, 16), OP.max)
+        for b in range(4):
+            lo, hi = 256 * b, 256 * b + 256
+            act(A("m1", lo, hi), ind(A("tab", S16 + lo, RAW + hi), A("idx", 0, 16)))
+            tt(A("m2", lo, hi), ind(A("tab", RAW + lo, P16 + hi), A("idx", 16, 32)), A("m1", lo, hi), OP.max)
         for h in range(2):
             for b in range(4):
-                lo = 128 * h
-                tt(part(A("xn", 4 * lo + b, 4 * lo + 512, 4), "xn%d%d" % (h, b)), A("ps", 512 * b + lo, 512 * b + lo + 128),
-                   A("m2", 256 * b + lo, 256 * b + lo + 128), OP.add)
-                if (h, b) == (1, 1):
-                    requant(t + 1, 0)
-        requant(t + 1, 1)
+                lo = 256 * b
+                tt(H("m3", h, lo), ind(A("tab", MID + lo, S4 + lo + 256), A("idx", 32 + 8 * h, 40 + 8 * h)), H("m2", h, lo), OP.max)
+                tt(part(A("xn", 512 * h + b, 512 * h + 512, 4), "xn%d%d" % (h, b)), bank(b, 128 * h, 128 * h + 128), H("m3", h, lo), OP.add)
+            quant(H("qx%d" % (t + 1), h), H("sx%d" % (t + 1), h), part(A("xn", 512 * h, 512 * h + 512), *["xn%d%d" % (h, b) for b in range(4)]))
 
-    mm(4, "qv", "sv", 0, "qx3", "sx3")
-    store("y", T.oc[:], T.qx3[:].bitcast(dt.uint8), "qx3")
+    for h in range(2):
+        lo, hi = 128 * h, 128 * h + 128
+        mm(4 + h, "qv", "sv", 0, "qx3", "sx3", lo, hi)
+        store("y", T.oc[:, 4 * lo:4 * hi], T.qx3[:, lo:hi].bitcast(dt.uint8), H("qx3", h))
+        act(H("yo", h), bank(4 + h, 0, 128))
+        store("y", T.y[:, lo:hi], T.yo[:, lo:hi], H("yo", h))
     for k in range(4):
-        store("s", T.osc[4 * k:4 * k + 4, :], T.sx3[32 * k:32 * k + 4, :], "sx3")
-    cp(A("yo"), bank(4))
-    store("y", T.y[:], T.yo[:], "yo")
+        store("s", T.osc[4 * k:4 * k + 4, :], T.sx3[32 * k:32 * k + 4, :], A("sx3"))
     emit(g, T, ops)
     g.sync.wait_ge(T.sem.stored, totals["stored"])
     g.wait_ge(T.sem.sent, totals["sent"])

@@ -7,10 +7,9 @@ ROUND = 12582912.0
 MID, S16, S4, RAW, P4, P16 = 0, 1024, 2048, 3072, 4096, 5120
 STEPS = 7
 BLOCK = 384
-CUT = 192
-LAST = ((128, 192), (192, 256))
+LAST = ((128, 256),)
 
-CYCLE, FLOOR, WAKE, GATHER, SCATTER, LOCAL, REMOTE = 0.83, 64, 220.0, 1.5, 3.5, 1200.0, 1200.0
+CYCLE, FLOOR, WAKE, GATHER, SCATTER, LOCAL, REMOTE = 0.95, 64, 220.0, 1.5, 3.5, 1200.0, 1200.0
 SOON, SPARE, LEAD = 40.0, 30.0, 1500.0
 
 SCRATCH = {
@@ -35,15 +34,18 @@ SCRATCH = {
     "cl": ("sbuf", [128, 48], "uint16"),
     "r1": ("sbuf", [128, 256], "bfloat16"), "r2": ("sbuf", [128, 256], "bfloat16"), "r3": ("sbuf", [128, 256], "bfloat16"),
     "r4": ("sbuf", [128, 256], "bfloat16"), "jr": ("sbuf", [128, 1536], "bfloat16"), "hd": ("sbuf", [128, 2304], "bfloat16"),
-    "sa": ("sbuf", [128, 1920], "float32"), "af": ("sbuf", [128, 256], "float32"), "ai": ("sbuf", [128, 256], "int32"),
+    "sa": ("sbuf", [128, 1920], "float32"), "af": ("sbuf", [128, 512], "float32"), "ai": ("sbuf", [128, 128], "int32"),
+    "four": ("sbuf", [128, 512], "float32"), "kp4": ("sbuf", [128, 128], "bfloat16"), "kp16": ("sbuf", [128, 128], "bfloat16"),
+    "kp32": ("sbuf", [128, 128], "bfloat16"),
     "wz": ("sbuf", [128, 1152], "bfloat16"), "pf": ("sbuf", [128, 256], "bfloat16"),
     "lst": ("sbuf", [128, 144], "uint16"), "rkl": ("sbuf", [128, 16], "uint16"), "pll": ("sbuf", [128, 16], "uint16"),
-    "sgl": ("sbuf", [128, 16], "uint16"), "spl": ("sbuf", [128, 24], "uint16"), "idx": ("sbuf", [128, 48], "uint16"),
+    "spl": ("sbuf", [128, 24], "uint16"), "idx": ("sbuf", [128, 48], "uint16"),
     "key": ("sbuf", [128, 256], "float32"), "junk": ("sbuf", [128, 2048], "bfloat16"),
     "wf": ("sbuf", [128, 96], "float32"), "wi": ("sbuf", [128, 96], "int32"), "szw": ("sbuf", [128, 24], "int32"),
     "msk": ("sbuf", [128, 1024], "int32"), "hm": ("sbuf", [128, 768], "float32"),
     "z": ("sbuf", [128, 512], "bfloat16"), "zb": ("sbuf", [128, 512], "bfloat16"), "zt": ("sbuf", [128, 512], "bfloat16"),
-    "srow": ("sbuf", [128, 256], "bfloat16"), "shd": ("sbuf", [128, 256], "bfloat16"),
+    "srow": ("sbuf", [128, 384], "float32"), "shd": ("sbuf", [128, 384], "float32"),
+    "wide": ("sbuf", [128, 256], "float32"), "pwd": ("sbuf", [128, 512], "bfloat16"),
     "psrt": ("sbuf", [128, 256], "bfloat16"), "ssrt": ("sbuf", [128, 272], "bfloat16"),
     "step": ("sbuf", [128, 256], "bfloat16"), "same": ("sbuf", [128, 272], "bfloat16"),
     "cum": ("sbuf", [128, 256], "bfloat16"), "szp": ("sbuf", [128, 128], "bfloat16"), "phd": ("sbuf", [128, 256], "bfloat16"),
@@ -238,7 +240,7 @@ def rank_program(g, core, T, topo):
         rec("v", lambda e: e.memset(o[0], c), [o], [], span(o))
 
     def scan(o, d0, d1, init, op0, op1):
-        rec("v", lambda e: e.tensor_tensor_scan(o[0], d0[0], d1[0], init, op0, op1), [o], [d0, d1], span(o, d0, d1))
+        rec("v", lambda e: e.tensor_tensor_scan(o[0], d0[0], d1[0], val(init), op0, op1), [o], [d0, d1, init], span(o, d0, d1))
 
     def turn(o, a):
         rec("v", lambda e: e.transpose(o[0], a[0]), [o], [a], span(a, o))
@@ -264,7 +266,7 @@ def rank_program(g, core, T, topo):
         rec("t", lambda e: e.matmul_mx(o[0], l[0], ls[0], r[0], rs[0], True, True), [o], [l, ls, r, rs], (hi - lo + 16) * CYCLE)
 
     def iota(o, pattern, base, mult):
-        if o[4]:
+        if o[1][0][0] != "ci":
             rec("g", lambda e: e.iota(o[0], pattern, base, mult, allow_small_or_imprecise_dtypes=True), [o], [], 130 + 2 * o[3] * CYCLE)
         else:
             rec("g", lambda e: e.iota(o[0], pattern, base, mult), [o], [], 130 + 2 * o[3] * CYCLE)
@@ -312,8 +314,8 @@ def rank_program(g, core, T, topo):
         quant(H("qx0", h), H("sx0", h), A("xin", 512 * h, 512 * h + 512))
 
     i16, p32, cut, invk, i4, inv4, b256, ifr, odd16 = [F(k) for k in range(9)]
-    jw, root, radj, kfr, two, zero = [F(16 * k, 16) for k in range(1, 7)]
-    spread, turned, lines = A("cl", 0, 16), A("cl", 16, 24), A("cl", 24, 31)
+    whole, kfr, two, zero = F(10), F(64, 16), F(80, 16), F(96, 16)
+    spread, turned, lines, twice = A("cl", 0, 16), A("cl", 16, 24), A("cl", 24, 31), A("cl", 32, 48)
     iota(A("ci", 16, 17), [[0, 1]], 0, 1)
     iota(A("posd"), [[0, 8], [1, 16]], 0, 0)
     iota(A("ci", 0, 16), [[32, 8], [0, 2]], 0, 0)
@@ -328,6 +330,10 @@ def rank_program(g, core, T, topo):
     cp(i4, A("ci", 19, 20))
     ts(b256, A("ci", 20, 21), 256.0, OP.mult)
     tt(odd16, p32, i16, OP.subtract)
+    iota(A("wide"), [[32, 16], [1, 16]], 0, 0)
+    act(A("wide"), A("wide"), AF.Identity, odd16)
+    iota(A("ci", 48, 64), [[16, 8], [0, 2]], 0, 0)
+    ts(twice, A("ci", 48, 64), i16, OP.add)
     ts(cut, i16, 8.0, OP.subtract, -2 * ROUND, OP.mult)
     ts(cut, cut, -0.498046875, OP.add, 1.0, OP.min)
     ts(cut, cut, -ROUND, OP.max)
@@ -351,31 +357,31 @@ def rank_program(g, core, T, topo):
     for n in (32, 64, 128):
         act(A("k4", n, 2 * n), A("k4", 0, n))
     ts(inv4, i4, 3.0, OP.is_equal, 1.0 / HOLD, OP.max)
-    fill(two, 256.0)
-    fill(A("cf", 80, 96, 3), 2.0 ** -15)
+    fill(part(A("cf", 81, 96, 2), "odd"), 4096.0)
+    fill(part(A("cf", 80, 96, 2), "even"), 2.0 ** -9)
     fill(zero, 0.0)
-    scan(A("pw"), two, zero, 2.0 ** 15, OP.mult, OP.add)
+    scan(A("pw"), part(two, "odd", "even"), zero, 2.0 ** 9, OP.mult, OP.add)
     cp(spread, A("ci", 32, 48))
     ts(A("dmx"), A("posd"), 0.0, OP.is_equal)
-    for h in range(2):
-        tt(own("sa", 0, h), ind(A("pw"), A("cl", 8 * h, 8 * h + 8)), A("dmx"), OP.mult)
-    fill(A("sa", 0, 1), 0.0)
-    for h in range(2):
-        act(own("sa", 1, h), own("sa", 0, h))
+    tt(own("sa", 0, 1), ind(A("pw"), A("cl", 0, 8)), A("dmx"), OP.mult)
+    for k, h in ((0, 0), (1, 0), (1, 1)):
+        act(own("sa", k, h), own("sa", 0, 1))
+    fill(A("sa", 0, BLOCK + 1, BLOCK), 0.0)
+    act(A("af", 256, 384), A("jrow", 0, 128), scale=0.0)
+    for name, n in (("kp4", 4), ("kp16", 16), ("kp32", 32)):
+        fill(A(name), 1.0)
+        fill(A(name, 0 if n < 32 else n, 128, n), 0.0)
+    ts(whole, A("ci", 17, 18), 0.0, OP.is_equal, float(C), OP.mult)
     for name, blocks in (("jr", 4), ("sa", 5), ("wz", 3)):
         for k in range(blocks):
             act(A(name, BLOCK * k + 128, BLOCK * k + 256), A("jrow", 0, 128), scale=float(name == "jr"))
     act(A("jfr"), A("jrow"), scale=1.0 / C)
     ts(ifr, i16, 1.0 / C, OP.mult)
     ts(kfr, A("ci", 32, 48), 16.0 / C, OP.mult)
-    ts(jw, A("ci", 32, 48), 16.0, OP.mult, i16, OP.add)
-    ts(root, jw, 0.0, OP.is_equal)
-    ts(radj, root, float(C), OP.mult)
     fill(A("ones"), 1.0)
     fill(A("keep"), 1.0)
     fill(A("keep", 0, 256, 32), 0.0)
-    act(A("z"), A("ones"), scale=0.0)
-    fill(A("wf", 52, 54), 0.0)
+    act(part(A("z"), "z", "z00", "z10", "z01", "z11"), A("ones"), scale=0.0)
     fill(A("ssrt", 0, 16), 0.0)
     fill(A("same", 0, 1), 1.0)
     fill(A("same", 1, 257, 255), 0.0)
@@ -389,12 +395,18 @@ def rank_program(g, core, T, topo):
     fill(A("mbm"), BIG)
     fill(A("mbm", 0, 112, 16), -BIG)
     fill(A("mbm", 1, 112, 17), -BIG)
+    fill(A("mbm", 15, 112, 16), -BIG)
     for h in range(2):
         act(A("tab", MID + 512 * h, MID + 512 * h + 512), A("ones"), scale=-BIG)
     ts(F(112, 7), A("ci", 33, 40), i16, OP.is_gt)
     ts(F(120, 7), A("ci", 33, 40), -1.0, OP.mult, 15.0, OP.add)
     tt(F(112, 7), F(112, 7), F(120, 7), OP.mult)
-    ts(lines, F(112, 7), i16, OP.add, 16.0, OP.mult)
+    ts(F(112, 7), F(112, 7), i16, OP.add, 16.0, OP.mult)
+    ts(F(120, 7), A("ci", 33, 40), 16.0, OP.mult, float(15 - 240 - S16 + MID), OP.add)
+    ts(F(9), i16, 15.0, OP.is_equal)
+    ts(F(120, 7), F(120, 7), F(9), OP.mult, float(S16 - MID), OP.add)
+    tt(F(112, 7), F(112, 7), F(120, 7), OP.add)
+    cp(lines, F(112, 7))
 
     def L(k, h, lo=0, hi=128):
         return A("lst", 16 * k + 8 * h + lo // 16, 16 * k + 8 * h + hi // 16)
@@ -446,15 +458,16 @@ def rank_program(g, core, T, topo):
                 act(own("jr", ring[k + 1], h), ind(win("jr", ring[k], h), L(max(k - 1, 0), h)))
                 if k != STEPS - 2:
                     wrap(L(k + 1, h), H("hd", h, 256 * k + 256), own("jr", ring[k + 1], h))
-            path_sums("sa", [0, 1] + [2 + k % 3 for k in range(STEPS)], h, H("af", h))
-        sweep("af", 0, 32, C, A("ai", 224, C))
-        for lo, hi in ((0, 128), (128, CUT), (CUT, 224)):
-            cp(A("ai", lo, hi), A("af", lo, hi))
+            path_sums("sa", [0, 1] + [2 + k % 3 for k in range(STEPS)], h, A("af", 384 * h, 384 * h + 128))
+            sweep("af", 256 * h, 128 * h + 32, 128 * h + 128)
+        for a in range(128, C, 32):
+            act(A("af", a, a + 32), ind(A("af", 0, a), L(STEPS, 0, a, a + 32)))
         for a in range(32, 128, 32):
             act(own("jr", ring[-1], 1, a, a + 32), ind(win("jr", ring[-1], 1, a), L(STEPS, 1, a, a + 32)))
         wrap(L(STEPS + 1, 1), H("hd", 1, 256 * STEPS + 256), own("jr", ring[-1], 1))
         for h in range(2):
             name, lo, hi = own("jr", 0, h)[1][0]
+            begin = len(ops)
             scan(A("key", 128 * h, 128 * h + 128, -1), A("jfr", 128 * h, 128 * h + 128, -1), A(name, lo, hi, -1), 1.0, OP.min, OP.add)
             keyw = A("wf", 16 + 8 * h, 24 + 8 * h)
             ts(keyw, L(0, h), ifr, OP.add)
@@ -462,45 +475,36 @@ def rank_program(g, core, T, topo):
             for k in range(8 * h, 8 * h + 8):
                 act(A("junk", 128 * k, 128 * k + 128), H("key", h), AF.Sign, A("wf", 16 + k, 17 + k), -1.0, A("wf", 32 + k, 33 + k))
             ts(A("rkl", 8 * h, 8 * h + 8), A("wf", 32 + 8 * h, 40 + 8 * h), 127.0, OP.add, 0.5, OP.mult)
-            scatter(H("srow", h), A("rkl", 8 * h, 8 * h + 8), A("jrow", 0, 128))
-            wrap(A("sgl", 8 * h, 8 * h + 8), H("shd", h), H("srow", h))
-            act(H("psrt", h), ind(own("jr", 0, h), A("sgl", 8 * h, 8 * h + 8)))
+            scatter(H("srow", h), A("rkl", 8 * h, 8 * h + 8), A("wide", 0, 128))
+            wrap(A("spl", 8 * h, 8 * h + 8), H("shd", h), H("srow", h))
+            act(A("pwd", 256 * h, 256 * h + 256), ind(own("jr", 0, h), twice))
+            act(H("psrt", h), ind(A("pwd", 256 * h, 256 * h + 256), A("spl", 8 * h, 8 * h + 8)))
             lo, hi = 2 + 127 * h, 128 * h + 128
             scan(A("step", lo, hi), A("psrt", lo - 1, hi - 1), A("psrt", lo, hi), 0.0, OP.max, OP.subtract)
             ts(A("same", lo, hi), A("step", lo, hi), 0.0, OP.is_equal)
-        for lo, lists in ((0, [A("sgl", 0, 8), L(0, 1)]), (16, [A("sgl", 8, 16)])):
-            hi = lo + 8 * len(lists)
-            for k, names in enumerate(lists):
-                cp(A("wi", lo + 8 * k, lo + 8 * k + 8), names)
-            ts(A("wi", 64 + lo, 64 + hi), A("wi", lo, hi), 240, OP.bitwise_and)
-            tt(A("wf", 64 + lo, 64 + hi), A("wi", 64 + lo, 64 + hi), A("wi", lo, hi), OP.add)
-            ts(A("spl", lo, hi), A("wf", 64 + lo, 64 + hi), odd16, OP.add)
-        at, rest = 0, C - CUT
-        for m in range(CUT // 48):
-            first = at
-            for lo, hi in ((48 * m, 128), (max(48 * m, 128), CUT)):
-                n = hi - lo
-                if n > 0:
-                    ts(A("msk", at, at + n), A("ai", lo, hi), m, OP.logical_shift_right, 0x010101, OP.bitwise_and)
-                    tt(A("hm", at // 2, (at + n) // 2), A("msk", at, at + n // 2), A("msk", at + n // 2, at + n), OP.add)
-                    at += n
-            total(A("wf", 48 + m, 49 + m), A("hm", first // 2, at // 2))
-        for m in range(6):
-            ts(A("msk", at + rest * m, at + rest * m + rest), A("ai", CUT, C), m, OP.logical_shift_right, 0x010101, OP.bitwise_and)
-        for lo in range(0, 6 * rest, 3 * rest):
-            tt(A("hm", (at + lo) // 2, (at + lo + 3 * rest) // 2), A("msk", at + lo, at + lo + 3 * rest, 2), A("msk", at + lo + 1, at + lo + 3 * rest, 2), OP.add)
-        scan(A("hm", 512, 512 + 3 * rest), A("keep", 0, 3 * rest), A("hm", at // 2, at // 2 + 3 * rest), 0.0, OP.mult, OP.add)
-        tt(A("wi", 32, 38), A("wf", 48, 54), A("hm", 512 + 31, 512 + 3 * rest, 32), OP.add)
-        for f in range(3):
-            ts(part(A("szw", f, 18, 3), "sz%d" % f), A("wi", 32, 38), 8 * f, OP.logical_shift_right, 255, OP.bitwise_and)
-        size = part(A("szw", 0, 16), "sz0", "sz1", "sz2")
-        tt(A("z", 0, 512, 32), size, radj, OP.add)
-        for lo in (256, 0):
-            scan(A("zb", lo, lo + 256), A("keep"), A("z", lo, lo + 256), 0.0, OP.mult, OP.add)
+            for op in ops[begin:]:
+                op["lead"] = LEAD
+        act(H("srow", 2), ind(A("wide"), L(0, 1)))
+        wrap(A("spl", 16, 24), H("shd", 2), H("srow", 2))
+        for lo in (384, 0, 128):
+            scan(A("four", lo, lo + 128), A("kp4"), A("af", lo, lo + 128), 0.0, OP.mult, OP.add)
+            cp(A("ai", lo // 4, lo // 4 + 32), A("four", lo + 3, lo + 128, 4))
+        for h in (1, 0):
+            n, lo = 64 - 32 * h, 256 * h
+            for m in range(4):
+                ts(A("msk", lo + n * m, lo + n * m + n), A("ai", 96 * h, 96 * h + n), 3 * m, OP.logical_shift_right, 0x7007, OP.bitwise_and)
+            tt(A("hm", lo, lo + 2 * n), A("msk", lo, lo + 4 * n, 2), A("msk", lo + 1, lo + 4 * n, 2), OP.add)
+            scan(A("hm", lo + 128, lo + 128 + 2 * n), A("kp16" if h else "kp32", 0, 2 * n), A("hm", lo, lo + 2 * n), 0.0 if h else whole, OP.mult, OP.add)
+            both, high = A("hm", lo + 128 + n // 2 - 1, lo + 128 + 2 * n, n // 2), A("wf", 48 + 4 * h, 52 + 4 * h)
+            ts(high, both, 4096 * ROUND, OP.add, 4096 * ROUND, OP.subtract)
+            tt(part(A("z", lo, lo + 256, 64), "z0%d" % h), both, high, OP.subtract)
+            ts(part(A("z", lo + 32, lo + 256, 64), "z1%d" % h), high, 1.0 / 4096, OP.mult)
+            scan(A("zb", lo, lo + 256), A("keep"), part(A("z", lo, lo + 256), "z", "z0%d" % h, "z1%d" % h), 0.0, OP.mult, OP.add)
             turn(A("zt", lo, lo + 256), A("zb", lo, lo + 256))
-        cp(A("ssrt", 144, 272), ind(A("zt", 256, 512), A("spl", 16, 24)))
+        size = part(A("z", 0, 512, 32), "z00", "z10", "z01", "z11")
+        cp(A("ssrt", 144, 272), ind(A("zt", 256, 512), A("spl", 8, 16)))
         cp(A("ssrt", 16, 144), ind(A("zt", 0, 256), A("spl", 0, 8)))
-        act(A("szp"), ind(A("zt"), A("spl", 8, 16)))
+        act(A("szp"), ind(A("zt"), A("spl", 16, 24)))
         scan(H("cum", 0), A("ssrt", 15, 143), H("same", 0), -1.0, OP.add, OP.mult)
         scan(A("cum", 128, 256, -1), A("same", 129, 257, -1), A("ssrt", 144, 272, -1), 0.0, OP.mult, OP.subtract)
         for k in range(2):
@@ -523,15 +527,13 @@ def rank_program(g, core, T, topo):
         for b in range(4):
             mm(b, "qe", "se", b, qp, sp)
             act(A("tp", 256 * b, 256 * b + 256), bank(b))
-            mm(b, "qe", "se", b, qx, sx)
         if t == R - 1:
             for h in range(2):
                 act(H("po", h), own("jr", 0, h))
             store("y", T.op[:], T.po[0:128:16, :], A("po"))
         for k in range(2):
-            tt(W(k), size, radj, OP.add)
             ts(V(k), A("pll"), -float(k), OP.add)
-        tt(V(2, 2), V(0, 2), W(0, 2), OP.add)
+            tt(V(2 + k), V(k), size, OP.add)
         ts(V(4, 4), V(0, 4), 2, OP.arith_shift_right)
         ts(V(8, 4), V(0, 4), 4, OP.arith_shift_right)
         tt(W(2, 2), V(6, 2), V(4, 2), OP.is_gt)
@@ -562,17 +564,22 @@ def rank_program(g, core, T, topo):
                 (act if q % 2 else cp)(A("bt", 256 * q, 256 * q + 256), ind(A("tp"), A(lp, 16 * q, 16 * q + 16)))
             quant(H("qf", h), H("sf", h), A("bt", 512 * h, 512 * h + 512))
             for b in range(4):
-                mm(4 + b, "qw", "sw", b, "qf", "sf", 128 * h, 128 * h + 128)
+                mm(4 * h + b, "qw", "sw", b, "qf", "sf", 128 * h, 128 * h + 128)
                 lo = 256 * b + 128 * h
-                act(tab(RAW, lo, lo + 128), bank(4 + b, 0, 128), scale=0.03125)
+                act(tab(RAW, lo, lo + 128), bank(4 * h + b, 0, 128), scale=0.03125)
                 scan(tab(S16, lo, lo + 128, -1), A("mb16", 0, 128), tab(RAW, lo, lo + 128, -1), -BIG, OP.min, OP.max)
+        for b in range(4):
+            mm(b, "qe", "se", b, qx, sx)
         for region, mask, step in ((S4, "mb4", -1), (P4, "mb4", 1), (P16, "mb16", 1)):
             for lo in (0, 512):
                 scan(tab(region, lo, lo + 512, step), A(mask), tab(RAW, lo, lo + 512, step), -BIG, OP.min, OP.max)
-        for b in range(4):
-            act(A("mg", 112 * b, 112 * b + 112), ind(tab(S16, 256 * b, 256 * b + 256), lines))
-            scan(tab(MID, 256 * b + 16, 256 * b + 128), A("mbm"), A("mg", 112 * b, 112 * b + 112), -BIG, OP.min, OP.max)
         tt(tab(MID, 15, 1024, 16), tab(S4, 4, 1024, 16), tab(S4, 8, 1024, 16), OP.max)
+        for b in range(4):
+            act(A("mg", 112 * b, 112 * b + 112), ind(A("tab", MID + 256 * b, S16 + 256 * b + 256), lines))
+        for b in range(4):
+            scan(tab(MID, 256 * b + 16, 256 * b + 128), A("mbm"), A("mg", 112 * b, 112 * b + 112), -BIG, OP.min, OP.max)
+        for op in ops[-9:]:
+            op["lead"] = LEAD / 3
         for b in range(4):
             lo, hi = 256 * b, 256 * b + 256
             act(A("m1", lo, hi), ind(A("tab", S16 + lo, RAW + hi), A("idx", 0, 16)))
@@ -588,7 +595,7 @@ def rank_program(g, core, T, topo):
         lo, hi = 128 * h, 128 * h + 128
         mm(4 + h, "qv", "sv", 0, "qx3", "sx3", lo, hi)
         store("y", T.oc[:, 4 * lo:4 * hi], T.qx3[:, lo:hi].bitcast(dt.uint8), H("qx3", h))
-        act(H("yo", h), bank(4 + h, 0, 128))
+        cp(H("yo", h), bank(4 + h, 0, 128))
         store("y", T.y[:, lo:hi], T.yo[:, lo:hi], H("yo", h))
     for k in range(4):
         store("s", T.osc[4 * k:4 * k + 4, :], T.sx3[32 * k:32 * k + 4, :], A("sx3"))

@@ -4,13 +4,13 @@ C, R = 256, 3
 BIG = 1e29
 HOLD = 1024.0
 ROUND = 12582912.0
-MID, S16, S4, RAW, P4, P16 = 0, 1024, 2048, 3072, 4096, 5120
+MID, PAIR, S16, S4, RAW, P4, P16 = 0, 1024, 2048, 3072, 4096, 5120, 6144
 STEPS = 7
 BLOCK = 384
-LAST = ((128, 256),)
 
-CYCLE, FLOOR, WAKE, GATHER, SCATTER, LOCAL, REMOTE = 0.95, 64, 220.0, 1.5, 3.5, 1200.0, 1200.0
-SOON, SPARE, LEAD = 40.0, 30.0, 1500.0
+CYCLE, CALL, WAKE, GATHER, SCATTER, LOCAL, REMOTE = 0.85, 26.0, 235.0, 1.4, 3.0, 1200.0, 1400.0
+SOON, SPARE, LEAD, LAYS, MOVES = 40.0, (0.0, 30.0, 60.0, 100.0, 150.0), 1500.0, 450, 16000
+PACES = ((235.0, 0.95), (270.0, 1.3), (215.0, 1.1))
 
 SCRATCH = {
     "ps": ("psum", [128, 4096], "float32"),
@@ -22,21 +22,21 @@ SCRATCH = {
     "ones": ("sbuf", [128, 512], "bfloat16"),
     "xn": ("sbuf", [128, 1024], "bfloat16"), "tp": ("sbuf", [128, 1024], "bfloat16"), "bt": ("sbuf", [128, 1024], "bfloat16"),
     "qf": ("sbuf", [128, 256], "float8_e4m3fn_x4"), "sf": ("sbuf", [128, 256], "uint8"),
-    "tab": ("sbuf", [128, 6144], "float32"), "mg": ("sbuf", [128, 448], "float32"),
+    "tab": ("sbuf", [128, 7168], "float32"), "mg": ("sbuf", [128, 448], "float32"),
     "m1": ("sbuf", [128, 1024], "float32"), "m2": ("sbuf", [128, 1024], "float32"), "m3": ("sbuf", [128, 1024], "float32"),
     "yo": ("sbuf", [128, 256], "float32"), "po": ("sbuf", [128, 256], "float32"),
     "ci": ("sbuf", [128, 96], "int32"), "cf": ("sbuf", [128, 128], "float32"), "pw": ("sbuf", [128, 16], "float32"),
     "posd": ("sbuf", [128, 128], "bfloat16"), "kd": ("sbuf", [128, 128], "bfloat16"), "kd2": ("sbuf", [128, 128], "bfloat16"),
     "pos4": ("sbuf", [128, 32], "bfloat16"), "k4": ("sbuf", [128, 256], "bfloat16"), "k42": ("sbuf", [128, 32], "bfloat16"),
     "dmx": ("sbuf", [128, 128], "bfloat16"), "keep": ("sbuf", [128, 256], "bfloat16"), "jrow": ("sbuf", [128, 256], "bfloat16"),
-    "jfr": ("sbuf", [128, 256], "bfloat16"), "dj": ("sbuf", [128, 256], "bfloat16"),
+    "jfr": ("sbuf", [128, 256], "bfloat16"), "dj": ("sbuf", [128, 512], "bfloat16"),
     "mb4": ("sbuf", [128, 512], "bfloat16"), "mb16": ("sbuf", [128, 512], "bfloat16"), "mbm": ("sbuf", [128, 112], "bfloat16"),
-    "cl": ("sbuf", [128, 48], "uint16"),
-    "r1": ("sbuf", [128, 256], "bfloat16"), "r2": ("sbuf", [128, 256], "bfloat16"), "r3": ("sbuf", [128, 256], "bfloat16"),
+    "cl": ("sbuf", [128, 64], "uint16"), "par": ("sbuf", [128, 32], "uint16"),
+    "r1": ("sbuf", [128, 288], "bfloat16"), "r2": ("sbuf", [128, 512], "bfloat16"), "r3": ("sbuf", [128, 512], "bfloat16"),
     "r4": ("sbuf", [128, 256], "bfloat16"), "jr": ("sbuf", [128, 1536], "bfloat16"), "hd": ("sbuf", [128, 2304], "bfloat16"),
     "sa": ("sbuf", [128, 1920], "float32"), "af": ("sbuf", [128, 512], "float32"), "ai": ("sbuf", [128, 128], "int32"),
-    "four": ("sbuf", [128, 512], "float32"), "kp4": ("sbuf", [128, 128], "bfloat16"), "kp16": ("sbuf", [128, 128], "bfloat16"),
-    "kp32": ("sbuf", [128, 128], "bfloat16"),
+    "seven": ("sbuf", [128, 512], "float32"), "kp7": ("sbuf", [128, 128], "bfloat16"), "kp10": ("sbuf", [128, 40], "bfloat16"),
+    "kp19": ("sbuf", [128, 76], "bfloat16"),
     "wz": ("sbuf", [128, 1152], "bfloat16"), "pf": ("sbuf", [128, 256], "bfloat16"),
     "lst": ("sbuf", [128, 144], "uint16"), "rkl": ("sbuf", [128, 16], "uint16"), "pll": ("sbuf", [128, 16], "uint16"),
     "spl": ("sbuf", [128, 24], "uint16"), "idx": ("sbuf", [128, 48], "uint16"),
@@ -44,7 +44,8 @@ SCRATCH = {
     "wf": ("sbuf", [128, 96], "float32"), "wi": ("sbuf", [128, 96], "int32"), "szw": ("sbuf", [128, 24], "int32"),
     "msk": ("sbuf", [128, 1024], "int32"), "hm": ("sbuf", [128, 768], "float32"),
     "z": ("sbuf", [128, 512], "bfloat16"), "zb": ("sbuf", [128, 512], "bfloat16"), "zt": ("sbuf", [128, 512], "bfloat16"),
-    "srow": ("sbuf", [128, 384], "float32"), "shd": ("sbuf", [128, 384], "float32"),
+    "srow": ("sbuf", [128, 256], "bfloat16"), "shd": ("sbuf", [128, 256], "bfloat16"),
+    "prow": ("sbuf", [128, 128], "float32"), "prh": ("sbuf", [128, 128], "float32"),
     "wide": ("sbuf", [128, 256], "float32"), "pwd": ("sbuf", [128, 512], "bfloat16"),
     "psrt": ("sbuf", [128, 256], "bfloat16"), "ssrt": ("sbuf", [128, 272], "bfloat16"),
     "step": ("sbuf", [128, 256], "bfloat16"), "same": ("sbuf", [128, 272], "bfloat16"),
@@ -73,12 +74,13 @@ def earlier(ops):
         deps = set()
         for regs, writes in ((op["rd"], False), (op["wr"], True)):
             for name, lo, hi in regs:
-                deps.update(m for a, b, m, w in touched.get(name, []) if a < hi and lo < b and (w or writes))
+                deps.update(m for a, b, m, w in touched.get(name, []) if a < hi and lo < b and (w or writes)
+                            and not (name == "ps" and ops[m]["q"] == op["q"] != "t"))
         found.append(deps)
         for regs, writes in ((op["rd"], False), (op["wr"], True)):
             for name, lo, hi in regs:
                 old = touched.get(name, [])
-                if writes:
+                if writes and (name != "ps" or op["q"] == "t"):
                     old = [e for e in old if not (lo <= e[0] and e[1] <= hi)]
                 touched[name] = old + [(lo, hi, n, writes)]
     return found
@@ -93,39 +95,110 @@ def arrange(ops):
         for m in d:
             later[m].append(n)
 
-    def lay(weight, before, after, back):
-        tail = [op["time"] - op["hold"] if back else 0.0 for op in ops]
-        missing, ready, free, at = [len(d) for d in before], list(tail), {}, {}
-        open_calls = [n for n in range(len(ops)) if not missing[n]]
-        while open_calls:
-            start = {n: max(ready[n], free.get(ops[n]["q"], 0.0)) for n in open_calls}
-            first = min(open_calls, key=lambda n: (start[n], -weight[n]))
-            mine = sorted([n for n in open_calls if ops[n]["q"] == ops[first]["q"]], key=lambda n: -weight[n])
+    calls = range(len(ops))
+    queue, time, hold = [[op[k] for op in ops] for k in ("q", "time", "hold")]
+
+    def lay(weight, back, wake, spare):
+        before, after = (later, deps) if back else (deps, later)
+        tail = [time[n] - hold[n] if back else 0.0 for n in calls]
+        missing, ready, at = [len(d) for d in before], list(tail), [0.0 for n in calls]
+        free = {q: 0.0 for q in queue}
+        open_calls = {q: [n for n in calls if queue[n] == q and not missing[n]] for q in free}
+        for count in calls:
+            first, q = min([(max(free[q], min(ready[n] for n in mine)), q) for q, mine in open_calls.items() if mine], key=lambda e: e[0])
+            mine = sorted(open_calls[q], key=lambda n: -weight[n])
             pick, limit = None, float("inf")
             for n in mine:
-                if start[n] <= start[first] + SOON and start[n] + ops[n]["hold"] <= limit:
+                start = max(ready[n], free[q])
+                if start <= first + SOON and start + hold[n] <= limit:
                     pick = n
                     break
-                limit = min(limit, start[n] + SPARE + weight[mine[0]] - weight[n])
+                limit = min(limit, start + spare + weight[mine[0]] - weight[n])
             if pick is None:
-                pick = min([n for n in mine if start[n] > start[first] + SOON], key=lambda n: start[n])
-            open_calls.remove(pick)
-            at[pick] = start[pick]
-            if ops[pick]["q"] is not None:
-                free[ops[pick]["q"]] = at[pick] + ops[pick]["hold"]
+                pick = min([n for n in mine if max(ready[n], free[q]) > first + SOON], key=lambda n: ready[n])
+            open_calls[q].remove(pick)
+            at[pick] = max(ready[pick], free[q])
+            if q is not None:
+                free[q] = at[pick] + hold[pick]
             for k in after[pick]:
-                ready[k] = max(ready[k], at[pick] + ops[pick]["time"] - tail[pick] + WAKE + tail[k])
+                ready[k] = max(ready[k], at[pick] + time[pick] - tail[pick] + wake + tail[k])
                 missing[k] -= 1
                 if not missing[k]:
-                    open_calls.append(k)
-        return [at[n] + ops[n]["hold"] for n in range(len(ops))], sorted(at, key=lambda n: (at[n], n))
+                    open_calls[queue[k]].append(k)
+        return [at[n] + hold[n] for n in calls], sorted(calls, key=lambda n: (at[n], n))
 
-    chain = [0.0] * len(ops)
-    for n in reversed(range(len(ops))):
-        chain[n] = ops[n]["time"] + max([WAKE + chain[k] for k in later[n]] + [0.0])
-    ends = lay([chain[n] + ops[n].get("lead", 0.0) for n in range(len(ops))], deps, later, False)[0]
-    order = lay(lay(ends, later, deps, True)[0], deps, later, False)[1]
-    return order, earlier([ops[n] for n in order])
+    paced = [([time[n] * (pace if hold[n] == time[n] else 1.0) + wake for n in calls],
+              [hold[n] * (pace if hold[n] == time[n] else 1.0) for n in calls]) for wake, pace in PACES]
+
+    lists = [n for n in calls if ops[n]["line"].startswith("al")]
+    kept = [([0.0 for n in calls], {q: (0.0, None) for q in "vstgy"}) for pace in PACES]
+
+    def run(order, k, keep=False):
+        (took, held), done, free, cause = paced[k], kept[k][0], kept[k][1] if keep else dict(kept[k][1]), {}
+        for n in order:
+            q = queue[n]
+            start, first = free[q] if q else (0.0, None)
+            for m in deps[n]:
+                if done[m] > start:
+                    start, first = done[m], m
+            done[n], cause[n], free[q] = start + took[n], first, (start + held[n], n)
+        last = [n for n in order[-40:] if n in lists or not later[n]]
+        return max([(done[n], n) for n in last] + [free["v"], free["s"]]) + (cause,)
+
+    def length(order):
+        return sum(run(order, k)[0] for k in range(len(PACES)))
+
+    state = [1]
+
+    def some(n):
+        state[0] = (state[0] * 1103515245 + 12345) % 2 ** 31
+        return (state[0] >> 8) % n
+
+    chain = [0.0 for n in calls]
+    for n in reversed(calls):
+        chain[n] = time[n] + max([WAKE + chain[k] for k in later[n]] + [0.0])
+    best, laid = (float("inf"), None, None), []
+    for trial in range(LAYS):
+        wake, spare = WAKE + 20 * (some(3) - 1), SPARE[some(len(SPARE))]
+        if trial < 20:
+            share = 0.5 * (1 + some(3))
+            weight = [chain[n] + share * ops[n].get("lead", 0.0) for n in calls]
+        else:
+            width = (100, 300, 600)[some(3)]
+            weight = [best[2][n] + some(width) for n in calls]
+        for turn in range(2):
+            ends, order = lay(weight, False, wake, spare)
+            laid.append(order)
+            best = min(best, (length(order), order, weight))
+            weight = lay(ends, True, wake, spare)[0] if turn == 0 else None
+    cuts = [0] + [k + 1 for k, n in enumerate(best[1]) if n in lists] + [len(ops)]
+    whole = []
+    for lo, hi in zip(cuts, cuts[1:]):
+        mine = set(best[1][lo:hi])
+        total, order = min((length(o), o) for o in [[n for n in other if n in mine] for other in laid])
+        for trial in range(MOVES):
+            if trial % 30 == 0:
+                end, n, cause = run(order, some(len(PACES)))
+                path = []
+                while n in mine:
+                    path.append(n)
+                    n = cause[n]
+            n = path[some(len(path))]
+            n = cause[n] if some(2) and cause[n] in mine else n
+            at, step, places = order.index(n), 2 * some(2) - 1, 1 + some(5)
+            to, fixed = at, later[n] if step > 0 else deps[n]
+            while places and 0 <= to + step < len(order) and order[to + step] not in fixed:
+                to += step
+                places -= queue[order[to]] == queue[n]
+            other = order[:at] + order[at + 1:]
+            other.insert(to, n)
+            now = length(other) if to != at else total + 1
+            if now <= total:
+                total, order = now, other
+        for k in range(len(PACES)):
+            run(order, k, True)
+        whole += order
+    return whole, earlier([ops[n] for n in whole])
 
 
 def emit(g, T, ops):
@@ -213,10 +286,10 @@ def rank_program(g, core, T, topo):
 
     def span(a, *others, rate=None):
         if a[4] is None:
-            return 60 + a[3] * GATHER * CYCLE
+            return 52 + a[3] * GATHER * CYCLE
         if rate is None:
             rate = 0.5 if a[4] and all(o[4] for o in others) else 1.0
-        return max(FLOOR, a[3] * rate) * CYCLE
+        return CALL + a[3] * rate * CYCLE
 
     def tt(o, a, b, op):
         rec("v", lambda e: e.tensor_tensor(o[0], a[0], b[0], op), [o], [a, b], span(a, rate=1.0 if a[2] else 2.0))
@@ -258,7 +331,7 @@ def rank_program(g, core, T, topo):
             if acc is not None:
                 kw["accum_out"] = acc[0]
             return e.activation(o[0], a[0], func, **kw)
-        rec("s", fn, [o] + ([acc] if acc is not None else []), [a, bias], span(a, rate=1.0) + (20 if acc else 0))
+        rec("s", fn, [o] + ([acc] if acc is not None else []), [a, bias], span(a, rate=1.0) + (32 if acc else 12))
 
     def mm(bank, wq, ws, b, xq, xs, lo=0, hi=C):
         o, l, ls = A("ps", 512 * bank, 512 * bank + hi - lo), A(wq, 128 * b, 128 * b + 128), A(ws, 128 * b, 128 * b + 128)
@@ -308,6 +381,8 @@ def rank_program(g, core, T, topo):
     load("y", A("qw"), T.qw[:].bitcast(dt.uint8), T.wc[:], "ldw")
     load("y", A("sw"), T.sw[:], T.ws[:], "lds")
     load("y", A("vin"), T.vin[:], T.v[:], "ldv")
+    for op in ops[-3:]:
+        op["rd"] = A("xin")[1] + A("uin")[1]
     quant(A("qu"), A("su"), A("uin"))
     quant(A("qv"), A("sv"), A("vin"))
     for h in range(2):
@@ -315,10 +390,10 @@ def rank_program(g, core, T, topo):
 
     i16, p32, cut, invk, i4, inv4, b256, ifr, odd16 = [F(k) for k in range(9)]
     whole, kfr, two, zero = F(10), F(64, 16), F(80, 16), F(96, 16)
-    spread, turned, lines, twice = A("cl", 0, 16), A("cl", 16, 24), A("cl", 24, 31), A("cl", 32, 48)
+    spread, turned, lines, twice, columns = A("cl", 0, 16), A("cl", 16, 24), A("cl", 24, 31), A("cl", 32, 48), A("cl", 48, 49)
     iota(A("ci", 16, 17), [[0, 1]], 0, 1)
     iota(A("posd"), [[0, 8], [1, 16]], 0, 0)
-    iota(A("ci", 0, 16), [[32, 8], [0, 2]], 0, 0)
+    iota(A("ci", 0, 16), [[16, 2], [32, 4], [0, 2]], 0, 0)
     iota(A("ci", 32, 48), [[1, 16]], 0, 0)
     iota(A("jrow"), [[1, 256]], 0, 0)
     iota(A("pos4"), [[0, 8], [1, 4]], 0, 0)
@@ -337,13 +412,27 @@ def rank_program(g, core, T, topo):
     ts(cut, i16, 8.0, OP.subtract, -2 * ROUND, OP.mult)
     ts(cut, cut, -0.498046875, OP.add, 1.0, OP.min)
     ts(cut, cut, -ROUND, OP.max)
+    ts(A("ci", 0, 16), A("ci", 0, 16), p32, OP.add)
+    ts(A("ci", 0, 16), A("ci", 0, 16), 127, OP.bitwise_and)
     fill(A("dj"), 0.5)
-    fill(part(A("dj", 0, 256, 16), "dj0"), 0.0)
-    fill(part(A("dj", 9, 256, 16), "dj9"), 1.0)
-    fill(part(A("dj", 10, 256, 16), "dj10"), -1.0)
-    ts(part(A("dj", 8, 256, 16), "dj8"), A("ci", 0, 16), p32, OP.add, 0.5, OP.mult)
-    for op in ops[-4:]:
-        op["rd"] = op["rd"] + [("dj", 0, 256)]
+    fill(part(A("dj", 0, 512, 16), "dj0"), 0.0)
+    fill(part(A("dj", 9, 512, 16), "dj9"), 1.0)
+    fill(part(A("dj", 10, 512, 16), "dj10"), -1.0)
+    for h in range(2):
+        ts(part(A("dj", 256 * h + 8, 256 * h + 256, 16), "dj8%d" % h), A("ci", 0, 16), 128.0 * h, OP.add, 0.5, OP.mult)
+    for op in ops[-5:]:
+        op["rd"] = op["rd"] + [("dj", 0, 512)]
+    ts(A("ci", 64, 65), A("ci", 16, 17), 4, OP.logical_shift_right, 1, OP.bitwise_and)
+    ts(A("ci", 65, 66), A("ci", 16, 17), 1, OP.bitwise_and)
+    ts(A("ci", 66, 67), A("ci", 16, 17), 1, OP.logical_shift_right, 3, OP.bitwise_and)
+    cp(F(13), A("ci", 66, 67))
+    tt(F(11), A("ci", 64, 65), A("ci", 65, 66), OP.not_equal)
+    tt(F(12), A("ci", 64, 65), A("ci", 65, 66), OP.is_gt)
+    ts(A("ci", 67, 68), F(12), 3.0, OP.mult, A("cf", 13, 14), OP.add)
+    ts(A("ci", 67, 68), A("ci", 67, 68), 3, OP.bitwise_and)
+    ts(F(11), F(11), 128.0, OP.mult, odd16, OP.add)
+    ts(F(12), A("ci", 67, 68), 32.0, OP.mult, 10.0, OP.add)
+    ts(columns, F(12), F(11), OP.add)
     ts(turned, A("ci", 32, 40), 16.0, OP.mult, 10.0, OP.add)
     ts(A("posd"), A("posd"), i16, OP.subtract)
     ts(A("kd"), A("posd"), 1.0, OP.is_equal, HOLD, OP.mult)
@@ -368,9 +457,10 @@ def rank_program(g, core, T, topo):
         act(own("sa", k, h), own("sa", 0, 1))
     fill(A("sa", 0, BLOCK + 1, BLOCK), 0.0)
     act(A("af", 256, 384), A("jrow", 0, 128), scale=0.0)
-    for name, n in (("kp4", 4), ("kp16", 16), ("kp32", 32)):
+    for name, first, n in (("kp7", 2, 7), ("kp10", 10, 10), ("kp19", 19, 19)):
         fill(A(name), 1.0)
-        fill(A(name, 0 if n < 32 else n, 128, n), 0.0)
+        fill(A(name, first, None, n), 0.0)
+    fill(A("ai", 57, 58), 0)
     ts(whole, A("ci", 17, 18), 0.0, OP.is_equal, float(C), OP.mult)
     for name, blocks in (("jr", 4), ("sa", 5), ("wz", 3)):
         for k in range(blocks):
@@ -395,20 +485,16 @@ def rank_program(g, core, T, topo):
     fill(A("mbm"), BIG)
     fill(A("mbm", 0, 112, 16), -BIG)
     fill(A("mbm", 1, 112, 17), -BIG)
-    fill(A("mbm", 15, 112, 16), -BIG)
-    for h in range(2):
+    for h in range(4):
         act(A("tab", MID + 512 * h, MID + 512 * h + 512), A("ones"), scale=-BIG)
     ts(F(112, 7), A("ci", 33, 40), i16, OP.is_gt)
     ts(F(120, 7), A("ci", 33, 40), -1.0, OP.mult, 15.0, OP.add)
     tt(F(112, 7), F(112, 7), F(120, 7), OP.mult)
-    ts(F(112, 7), F(112, 7), i16, OP.add, 16.0, OP.mult)
-    ts(F(120, 7), A("ci", 33, 40), 16.0, OP.mult, float(15 - 240 - S16 + MID), OP.add)
-    ts(F(9), i16, 15.0, OP.is_equal)
-    ts(F(120, 7), F(120, 7), F(9), OP.mult, float(S16 - MID), OP.add)
-    tt(F(112, 7), F(112, 7), F(120, 7), OP.add)
-    cp(lines, F(112, 7))
+    ts(lines, F(112, 7), i16, OP.add, 16.0, OP.mult)
 
     def L(k, h, lo=0, hi=128):
+        if k == 0:
+            return A("par", 16 * h, 16 * h + 8)
         return A("lst", 16 * k + 8 * h + lo // 16, 16 * k + 8 * h + hi // 16)
 
     def wrap(out, held, row):
@@ -438,17 +524,18 @@ def rank_program(g, core, T, topo):
         peer = T.cores[rank ^ (1 << t)]
         qx, sx, qp, sp, ol, lp = ["%s%d" % (k, t) for k in ("qx", "sx", "qp", "sp", "ol", "lp")]
         engines = len(topo.engines(peer, core))
-        for h in range(2):
+        for h in (1, 0):
             mm(4 + h, "qu", "su", 0, qx, sx, 128 * h, 128 * h + 128)
-            ts(H("r1", h), bank(4 + h, 0, 128), 0.0, OP.is_gt, cut, OP.min)
-            turn(H("r2", h), H("r1", h))
-            dj = H("dj", h)
-            scan(H("r3", h), (dj[0], dj[1] + [(k, 0, 1) for k in ("dj0", "dj8", "dj9", "dj10")]) + dj[2:], H("r2", h), 0.0, OP.mult, OP.add)
-            act(H("r4", h), ind(H("r3", h), turned), scale=-1.0)
+            for lo, n in ((0, 128), (128, 16)):
+                ts(A("r1", 144 * h + lo, 144 * h + lo + n), bank(4 + h, 0, n), 0.0, OP.is_gt, cut, OP.min)
+            for k in range(2):
+                turn(H("r2", 2 * h + k), A("r1", 144 * h + 16 * k, 144 * h + 16 * k + 128))
+                scan(H("r3", 2 * h + k), part(H("dj", 2 * h + k), "dj0", "dj80", "dj81", "dj9", "dj10"), H("r2", 2 * h + k), 0.0, OP.mult, OP.add)
+            ts(A("par", 16 * h, 16 * h + 16), ind(A("r3", 256 * h, 256 * h + 256), columns), -1.0, OP.mult)
+            act(H("r4", h), ind(H("r3", 2 * h), turned), scale=-1.0)
             turn(own("jr", 0, h), H("r4", h))
-            wrap(L(0, h), H("hd", h), own("jr", 0, h))
-            for op in ops[-8:]:
-                op["lead"] = LEAD * (1 - h)
+            for op in ops[-10:]:
+                op["lead"] = LEAD * h
         send(peer, T[qp][:].bitcast(dt.uint8), T[qx][:].bitcast(dt.uint8), qx, "aq%d" % t)
         send(peer, T[sp][:], T[sx][:], sx, "aq%d" % t)
         arrive([qp, sp], "aq%d" % t, 2 * engines, 2000.0)
@@ -457,14 +544,14 @@ def rank_program(g, core, T, topo):
             for k in range(STEPS):
                 act(own("jr", ring[k + 1], h), ind(win("jr", ring[k], h), L(max(k - 1, 0), h)))
                 if k != STEPS - 2:
-                    wrap(L(k + 1, h), H("hd", h, 256 * k + 256), own("jr", ring[k + 1], h))
+                    lo = 32 * (k == STEPS - 1)
+                    wrap(L(k + 1, h, lo), H("hd", h, 256 * k + 256, lo), own("jr", ring[k + 1], h, lo))
             path_sums("sa", [0, 1] + [2 + k % 3 for k in range(STEPS)], h, A("af", 384 * h, 384 * h + 128))
             sweep("af", 256 * h, 128 * h + 32, 128 * h + 128)
-        for a in range(128, C, 32):
-            act(A("af", a, a + 32), ind(A("af", 0, a), L(STEPS, 0, a, a + 32)))
         for a in range(32, 128, 32):
             act(own("jr", ring[-1], 1, a, a + 32), ind(win("jr", ring[-1], 1, a), L(STEPS, 1, a, a + 32)))
         wrap(L(STEPS + 1, 1), H("hd", 1, 256 * STEPS + 256), own("jr", ring[-1], 1))
+        act(A("af", 128, C), ind(A("af", 0, 128), L(STEPS + 1, 1)))
         for h in range(2):
             name, lo, hi = own("jr", 0, h)[1][0]
             begin = len(ops)
@@ -481,42 +568,43 @@ def rank_program(g, core, T, topo):
             act(H("psrt", h), ind(A("pwd", 256 * h, 256 * h + 256), A("spl", 8 * h, 8 * h + 8)))
             lo, hi = 2 + 127 * h, 128 * h + 128
             scan(A("step", lo, hi), A("psrt", lo - 1, hi - 1), A("psrt", lo, hi), 0.0, OP.max, OP.subtract)
-            ts(A("same", lo, hi), A("step", lo, hi), 0.0, OP.is_equal)
+            act(A("same", lo, hi), A("step", lo, hi), AF.Relu, 1.0)
             for op in ops[begin:]:
                 op["lead"] = LEAD
-        act(H("srow", 2), ind(A("wide"), L(0, 1)))
-        wrap(A("spl", 16, 24), H("shd", 2), H("srow", 2))
-        for lo in (384, 0, 128):
-            scan(A("four", lo, lo + 128), A("kp4"), A("af", lo, lo + 128), 0.0, OP.mult, OP.add)
-            cp(A("ai", lo // 4, lo // 4 + 32), A("four", lo + 3, lo + 128, 4))
+        act(A("prow"), ind(A("wide"), L(0, 1)))
+        wrap(A("spl", 16, 24), A("prh"), A("prow"))
+        for k, lo in enumerate((0, 128, 384)):
+            scan(A("seven", lo, lo + 128), A("kp7"), A("af", lo, lo + 128), 0.0, OP.mult, OP.add)
+            cp(A("ai", 19 * k, 19 * k + 19), A("seven", lo + 1, lo + 128, 7))
         for h in (1, 0):
-            n, lo = 64 - 32 * h, 256 * h
+            n, lo = 38 - 18 * h, 256 * h
             for m in range(4):
-                ts(A("msk", lo + n * m, lo + n * m + n), A("ai", 96 * h, 96 * h + n), 3 * m, OP.logical_shift_right, 0x7007, OP.bitwise_and)
+                ts(A("msk", lo + n * m, lo + n * m + n), A("ai", 38 * h, 38 * h + n), 3 * m, OP.logical_shift_right, 0x7007, OP.bitwise_and)
             tt(A("hm", lo, lo + 2 * n), A("msk", lo, lo + 4 * n, 2), A("msk", lo + 1, lo + 4 * n, 2), OP.add)
-            scan(A("hm", lo + 128, lo + 128 + 2 * n), A("kp16" if h else "kp32", 0, 2 * n), A("hm", lo, lo + 2 * n), 0.0 if h else whole, OP.mult, OP.add)
+            scan(A("hm", lo + 128, lo + 128 + 2 * n), A("kp10" if h else "kp19"), A("hm", lo, lo + 2 * n), 0.0 if h else whole, OP.mult, OP.add)
             both, high = A("hm", lo + 128 + n // 2 - 1, lo + 128 + 2 * n, n // 2), A("wf", 48 + 4 * h, 52 + 4 * h)
             ts(high, both, 4096 * ROUND, OP.add, 4096 * ROUND, OP.subtract)
             tt(part(A("z", lo, lo + 256, 64), "z0%d" % h), both, high, OP.subtract)
-            ts(part(A("z", lo + 32, lo + 256, 64), "z1%d" % h), high, 1.0 / 4096, OP.mult)
+            act(part(A("z", lo + 32, lo + 256, 64), "z1%d" % h), high, scale=1.0 / 4096)
             scan(A("zb", lo, lo + 256), A("keep"), part(A("z", lo, lo + 256), "z", "z0%d" % h, "z1%d" % h), 0.0, OP.mult, OP.add)
             turn(A("zt", lo, lo + 256), A("zb", lo, lo + 256))
         size = part(A("z", 0, 512, 32), "z00", "z10", "z01", "z11")
-        cp(A("ssrt", 144, 272), ind(A("zt", 256, 512), A("spl", 8, 16)))
+        act(A("ssrt", 144, 272), ind(A("zt", 256, 512), A("spl", 8, 16)))
         cp(A("ssrt", 16, 144), ind(A("zt", 0, 256), A("spl", 0, 8)))
         act(A("szp"), ind(A("zt"), A("spl", 16, 24)))
         scan(H("cum", 0), A("ssrt", 15, 143), H("same", 0), -1.0, OP.add, OP.mult)
         scan(A("cum", 128, 256, -1), A("same", 129, 257, -1), A("ssrt", 144, 272, -1), 0.0, OP.mult, OP.subtract)
-        for k in range(2):
-            act(own("wz", k, 0), ind(H("cum", 0), A("rkl", 0, 8)), AF.Identity, 1.0)
-            tt(own("wz", k, 1), ind(H("cum", 1), A("rkl", 8, 16)), A("szp"), OP.add)
+        ts(own("wz", 0, 0), ind(H("cum", 0), A("rkl", 0, 8)), 1.0, OP.add)
+        act(own("wz", 1, 0), ind(H("cum", 0), A("rkl", 0, 8)), AF.Identity, 1.0)
+        tt(own("wz", 0, 1), ind(H("cum", 1), A("rkl", 8, 16)), A("szp"), OP.add)
+        act(own("wz", 1, 1), own("wz", 0, 1))
         ring = [k % 3 for k in range(STEPS + 2)]
         path_sums("wz", ring, 0, H("pf", 0))
         path_sums("wz", ring, 1, own("wz", ring[-1], 1))
         sweep("pf", 0, 32, 128)
         sweep("wz", BLOCK * ring[-1] + 128, 160, C)
-        for lo, hi in ((0, 128),) + LAST:
-            if lo:
+        for lo, hi in ((0, 64), (64, 128), (128, C)):
+            if hi == C:
                 tt(A("pf", lo, hi), ind(H("pf", 0), L(STEPS + 1, 0, lo, hi)), own("wz", ring[-1], 1, lo - 128, hi - 128), OP.add)
             wrap(A("pll", lo // 16, hi // 16), A("phd", lo, hi), A("pf", lo, hi))
             scatter(A("orow"), A("pll", lo // 16, hi // 16), A("jrow", lo, hi))
@@ -550,9 +638,10 @@ def rank_program(g, core, T, topo):
         tt(W(13), W(6), W(18), OP.is_equal)
         ts(W(14), W(7), 2.0, OP.is_ge)
         ts(W(15), V(4), 4.0, OP.mult, float(S4 - MID + 4), OP.add)
-        ts(W(16), V(8), 16.0, OP.mult, 15.0, OP.add)
+        ts(W(16), V(8), 16.0, OP.mult, float(PAIR - MID), OP.add)
+        ts(W(20), V(8), 16.0, OP.mult, 15.0, OP.add)
         ts(W(19), V(8), -17.0, OP.mult, 222.0, OP.add)
-        tt(W(20), W(16), W(19), OP.min)
+        tt(W(20), W(20), W(19), OP.min)
         tt(W(17), W(20), V(11), OP.add)
         tt(W(12, 3), W(12, 3), W(15, 3), OP.mult)
         tt(W(21), W(12), W(13), OP.add)
@@ -571,11 +660,12 @@ def rank_program(g, core, T, topo):
         for b in range(4):
             mm(b, "qe", "se", b, qx, sx)
         for region, mask, step in ((S4, "mb4", -1), (P4, "mb4", 1), (P16, "mb16", 1)):
-            for lo in (0, 512):
-                scan(tab(region, lo, lo + 512, step), A(mask), tab(RAW, lo, lo + 512, step), -BIG, OP.min, OP.max)
-        tt(tab(MID, 15, 1024, 16), tab(S4, 4, 1024, 16), tab(S4, 8, 1024, 16), OP.max)
+            n = 128 if region == S4 else 512
+            for lo in range(0, 1024, n):
+                scan(tab(region, lo, lo + n, step), A(mask, 0, n), tab(RAW, lo, lo + n, step), -BIG, OP.min, OP.max)
+        tt(tab(PAIR, 0, 1024, 16), tab(S4, 4, 1024, 16), tab(S4, 8, 1024, 16), OP.max)
         for b in range(4):
-            act(A("mg", 112 * b, 112 * b + 112), ind(A("tab", MID + 256 * b, S16 + 256 * b + 256), lines))
+            act(A("mg", 112 * b, 112 * b + 112), ind(tab(S16, 256 * b, 256 * b + 256), lines))
         for b in range(4):
             scan(tab(MID, 256 * b + 16, 256 * b + 128), A("mbm"), A("mg", 112 * b, 112 * b + 112), -BIG, OP.min, OP.max)
         for op in ops[-9:]:
@@ -584,10 +674,13 @@ def rank_program(g, core, T, topo):
             lo, hi = 256 * b, 256 * b + 256
             act(A("m1", lo, hi), ind(A("tab", S16 + lo, RAW + hi), A("idx", 0, 16)))
             tt(A("m2", lo, hi), ind(A("tab", RAW + lo, P16 + hi), A("idx", 16, 32)), A("m1", lo, hi), OP.max)
-        for h in range(2):
+        for h in (1, 0):
             for b in range(4):
                 lo = 256 * b
-                tt(H("m3", h, lo), ind(A("tab", MID + lo, S4 + lo + 256), A("idx", 32 + 8 * h, 40 + 8 * h)), H("m2", h, lo), OP.max)
+                if t < R - 1:
+                    tt(H("m3", h, lo), ind(A("tab", MID + lo, S4 + lo + 256), A("idx", 32 + 8 * h, 40 + 8 * h)), H("m2", h, lo), OP.max)
+                elif h == 1:
+                    tt(A("m3", lo, lo + 256), ind(A("tab", MID + lo, S4 + lo + 256), A("idx", 32, 48)), A("m2", lo, lo + 256), OP.max)
                 tt(part(A("xn", 512 * h + b, 512 * h + 512, 4), "xn%d%d" % (h, b)), bank(b, 128 * h, 128 * h + 128), H("m3", h, lo), OP.add)
             quant(H("qx%d" % (t + 1), h), H("sx%d" % (t + 1), h), part(A("xn", 512 * h, 512 * h + 512), *["xn%d%d" % (h, b) for b in range(4)]))
 

from concourse.mybir import dt, AluOpType as OP, ActivationFunctionType as AF, AxisListType

C, R = 256, 3
BIG = 1e29
HOLD = 1024.0
ROUND = 12582912.0
MID, PAIR, S16, S4, RAW, P4, P16 = 0, 1024, 2048, 3072, 4096, 5120, 6144
STEPS = 7
BLOCK = 384

CYCLE, CALL, WAKE, GATHER, SCATTER, LOCAL, REMOTE = 0.85, 26.0, 235.0, 1.4, 3.0, 1200.0, 1400.0
SOON, SPARE, LEAD, LAYS, MOVES = 40.0, (0.0, 30.0, 60.0, 100.0, 150.0), 1500.0, 450, 16000
PACES = ((235.0, 0.95), (270.0, 1.3), (215.0, 1.1))

SCRATCH = {
    "ps": ("psum", [128, 4096], "float32"),
    "xin": ("sbuf", [128, 1024], "bfloat16"), "uin": ("sbuf", [128, 512], "bfloat16"), "vin": ("sbuf", [128, 512], "bfloat16"),
    "qu": ("sbuf", [128, 128], "float8_e4m3fn_x4"), "su": ("sbuf", [128, 128], "uint8"),
    "qv": ("sbuf", [128, 128], "float8_e4m3fn_x4"), "sv": ("sbuf", [128, 128], "uint8"),
    "qw": ("sbuf", [128, 512], "float8_e4m3fn_x4"), "sw": ("sbuf", [128, 512], "uint8"),
    "et": ("sbuf", [128, 2048], "bfloat16"), "qe": ("sbuf", [128, 512], "float8_e4m3fn_x4"), "se": ("sbuf", [128, 512], "uint8"),
    "ones": ("sbuf", [128, 512], "bfloat16"),
    "xn": ("sbuf", [128, 1024], "bfloat16"), "tp": ("sbuf", [128, 1024], "bfloat16"), "bt": ("sbuf", [128, 1024], "bfloat16"),
    "qf": ("sbuf", [128, 256], "float8_e4m3fn_x4"), "sf": ("sbuf", [128, 256], "uint8"),
    "tab": ("sbuf", [128, 7168], "float32"), "mg": ("sbuf", [128, 448], "float32"),
    "m1": ("sbuf", [128, 1024], "float32"), "m2": ("sbuf", [128, 1024], "float32"), "m3": ("sbuf", [128, 1024], "float32"),
    "yo": ("sbuf", [128, 256], "float32"), "po": ("sbuf", [128, 256], "float32"),
    "ci": ("sbuf", [128, 96], "int32"), "cf": ("sbuf", [128, 128], "float32"), "pw": ("sbuf", [128, 16], "float32"),
    "posd": ("sbuf", [128, 128], "bfloat16"), "kd": ("sbuf", [128, 128], "bfloat16"), "kd2": ("sbuf", [128, 128], "bfloat16"),
    "pos4": ("sbuf", [128, 32], "bfloat16"), "k4": ("sbuf", [128, 256], "bfloat16"), "k42": ("sbuf", [128, 32], "bfloat16"),
    "dmx": ("sbuf", [128, 128], "bfloat16"), "keep": ("sbuf", [128, 256], "bfloat16"), "jrow": ("sbuf", [128, 256], "bfloat16"),
    "jfr": ("sbuf", [128, 256], "bfloat16"), "dj": ("sbuf", [128, 512], "bfloat16"),
    "mb4": ("sbuf", [128, 512], "bfloat16"), "mb16": ("sbuf", [128, 512], "bfloat16"), "mbm": ("sbuf", [128, 112], "bfloat16"),
    "cl": ("sbuf", [128, 64], "uint16"), "par": ("sbuf", [128, 32], "uint16"),
    "r1": ("sbuf", [128, 288], "bfloat16"), "r2": ("sbuf", [128, 512], "bfloat16"), "r3": ("sbuf", [128, 512], "bfloat16"),
    "r4": ("sbuf", [128, 256], "bfloat16"), "jr": ("sbuf", [128, 1536], "bfloat16"), "hd": ("sbuf", [128, 2304], "bfloat16"),
    "sa": ("sbuf", [128, 1920], "float32"), "af": ("sbuf", [128, 512], "float32"), "ai": ("sbuf", [128, 128], "int32"),
    "seven": ("sbuf", [128, 512], "float32"), "kp7": ("sbuf", [128, 128], "bfloat16"), "kp10": ("sbuf", [128, 40], "bfloat16"),
    "kp19": ("sbuf", [128, 76], "bfloat16"),
    "wz": ("sbuf", [128, 1152], "bfloat16"), "pf": ("sbuf", [128, 256], "bfloat16"),
    "lst": ("sbuf", [128, 144], "uint16"), "rkl": ("sbuf", [128, 16], "uint16"), "pll": ("sbuf", [128, 16], "uint16"),
    "spl": ("sbuf", [128, 24], "uint16"), "idx": ("sbuf", [128, 48], "uint16"),
    "key": ("sbuf", [128, 256], "float32"), "junk": ("sbuf", [128, 2048], "bfloat16"),
    "wf": ("sbuf", [128, 96], "float32"), "wi": ("sbuf", [128, 96], "int32"), "szw": ("sbuf", [128, 24], "int32"),
    "msk": ("sbuf", [128, 1024], "int32"), "hm": ("sbuf", [128, 768], "float32"),
    "z": ("sbuf", [128, 512], "bfloat16"), "zb": ("sbuf", [128, 512], "bfloat16"), "zt": ("sbuf", [128, 512], "bfloat16"),
    "srow": ("sbuf", [128, 256], "bfloat16"), "shd": ("sbuf", [128, 256], "bfloat16"),
    "prow": ("sbuf", [128, 128], "float32"), "prh": ("sbuf", [128, 128], "float32"),
    "wide": ("sbuf", [128, 256], "float32"), "pwd": ("sbuf", [128, 512], "bfloat16"),
    "psrt": ("sbuf", [128, 256], "bfloat16"), "ssrt": ("sbuf", [128, 272], "bfloat16"),
    "step": ("sbuf", [128, 256], "bfloat16"), "same": ("sbuf", [128, 272], "bfloat16"),
    "cum": ("sbuf", [128, 256], "bfloat16"), "szp": ("sbuf", [128, 128], "bfloat16"), "phd": ("sbuf", [128, 256], "bfloat16"),
    "orow": ("sbuf", [128, 256], "bfloat16"), "ohd": ("sbuf", [128, 256], "bfloat16"),
    "iv": ("sbuf", [128, 192], "int32"), "iw": ("sbuf", [128, 416], "float32"),
}
for _t in range(R + 1):
    SCRATCH["qx%d" % _t] = ("sbuf", [128, 256], "float8_e4m3fn_x4")
    SCRATCH["sx%d" % _t] = ("sbuf", [128, 256], "uint8")
for _t in range(R):
    SCRATCH["qp%d" % _t] = ("sbuf", [128, 256], "float8_e4m3fn_x4")
    SCRATCH["sp%d" % _t] = ("sbuf", [128, 256], "uint8")
    SCRATCH["ol%d" % _t] = ("sbuf", [128, 64], "uint16")
    SCRATCH["lp%d" % _t] = ("sbuf", [128, 64], "uint16")

SEMAPHORES = ["cv", "cs", "ct", "cg", "ldx0", "ldx1", "ldu", "ldv", "ldw", "lds", "sent", "stored"] + \
    ["aq%d" % t for t in range(R)] + ["al%d" % t for t in range(R)]
COUNTER = {"v": "cv", "s": "cs", "t": "ct", "g": "cg"}
PLAN = []


def earlier(ops):
    touched, found = {}, []
    for n, op in enumerate(ops):
        deps = set()
        for regs, writes in ((op["rd"], False), (op["wr"], True)):
            for name, lo, hi in regs:
                deps.update(m for a, b, m, w in touched.get(name, []) if a < hi and lo < b and (w or writes)
                            and not (name == "ps" and ops[m]["q"] == op["q"] != "t"))
        found.append(deps)
        for regs, writes in ((op["rd"], False), (op["wr"], True)):
            for name, lo, hi in regs:
                old = touched.get(name, [])
                if writes and (name != "ps" or op["q"] == "t"):
                    old = [e for e in old if not (lo <= e[0] and e[1] <= hi)]
                touched[name] = old + [(lo, hi, n, writes)]
    return found


def arrange(ops):
    deps = earlier(ops)
    for n, op in enumerate(ops):
        deps[n].update(op["after"])
    later = [[] for op in ops]
    for n, d in enumerate(deps):
        for m in d:
            later[m].append(n)

    calls = range(len(ops))
    queue, time, hold = [[op[k] for op in ops] for k in ("q", "time", "hold")]

    def lay(weight, back, wake, spare):
        before, after = (later, deps) if back else (deps, later)
        tail = [time[n] - hold[n] if back else 0.0 for n in calls]
        missing, ready, at = [len(d) for d in before], list(tail), [0.0 for n in calls]
        free = {q: 0.0 for q in queue}
        open_calls = {q: [n for n in calls if queue[n] == q and not missing[n]] for q in free}
        for count in calls:
            first, q = min([(max(free[q], min(ready[n] for n in mine)), q) for q, mine in open_calls.items() if mine], key=lambda e: e[0])
            mine = sorted(open_calls[q], key=lambda n: -weight[n])
            pick, limit = None, float("inf")
            for n in mine:
                start = max(ready[n], free[q])
                if start <= first + SOON and start + hold[n] <= limit:
                    pick = n
                    break
                limit = min(limit, start + spare + weight[mine[0]] - weight[n])
            if pick is None:
                pick = min([n for n in mine if max(ready[n], free[q]) > first + SOON], key=lambda n: ready[n])
            open_calls[q].remove(pick)
            at[pick] = max(ready[pick], free[q])
            if q is not None:
                free[q] = at[pick] + hold[pick]
            for k in after[pick]:
                ready[k] = max(ready[k], at[pick] + time[pick] - tail[pick] + wake + tail[k])
                missing[k] -= 1
                if not missing[k]:
                    open_calls[queue[k]].append(k)
        return [at[n] + hold[n] for n in calls], sorted(calls, key=lambda n: (at[n], n))

    paced = [([time[n] * (pace if hold[n] == time[n] else 1.0) + wake for n in calls],
              [hold[n] * (pace if hold[n] == time[n] else 1.0) for n in calls]) for wake, pace in PACES]

    lists = [n for n in calls if ops[n]["line"].startswith("al")]
    kept = [([0.0 for n in calls], {q: (0.0, None) for q in "vstgy"}) for pace in PACES]

    def run(order, k, keep=False):
        (took, held), done, free, cause = paced[k], kept[k][0], kept[k][1] if keep else dict(kept[k][1]), {}
        for n in order:
            q = queue[n]
            start, first = free[q] if q else (0.0, None)
            for m in deps[n]:
                if done[m] > start:
                    start, first = done[m], m
            done[n], cause[n], free[q] = start + took[n], first, (start + held[n], n)
        last = [n for n in order[-40:] if n in lists or not later[n]]
        return max([(done[n], n) for n in last] + [free["v"], free["s"]]) + (cause,)

    def length(order):
        return sum(run(order, k)[0] for k in range(len(PACES)))

    state = [1]

    def some(n):
        state[0] = (state[0] * 1103515245 + 12345) % 2 ** 31
        return (state[0] >> 8) % n

    chain = [0.0 for n in calls]
    for n in reversed(calls):
        chain[n] = time[n] + max([WAKE + chain[k] for k in later[n]] + [0.0])
    best, laid = (float("inf"), None, None), []
    for trial in range(LAYS):
        wake, spare = WAKE + 20 * (some(3) - 1), SPARE[some(len(SPARE))]
        if trial < 20:
            share = 0.5 * (1 + some(3))
            weight = [chain[n] + share * ops[n].get("lead", 0.0) for n in calls]
        else:
            width = (100, 300, 600)[some(3)]
            weight = [best[2][n] + some(width) for n in calls]
        for turn in range(2):
            ends, order = lay(weight, False, wake, spare)
            laid.append(order)
            best = min(best, (length(order), order, weight))
            weight = lay(ends, True, wake, spare)[0] if turn == 0 else None
    cuts = [0] + [k + 1 for k, n in enumerate(best[1]) if n in lists] + [len(ops)]
    whole = []
    for lo, hi in zip(cuts, cuts[1:]):
        mine = set(best[1][lo:hi])
        total, order = min((length(o), o) for o in [[n for n in other if n in mine] for other in laid])
        for trial in range(MOVES):
            if trial % 30 == 0:
                end, n, cause = run(order, some(len(PACES)))
                path = []
                while n in mine:
                    path.append(n)
                    n = cause[n]
            n = path[some(len(path))]
            n = cause[n] if some(2) and cause[n] in mine else n
            at, step, places = order.index(n), 2 * some(2) - 1, 1 + some(5)
            to, fixed = at, later[n] if step > 0 else deps[n]
            while places and 0 <= to + step < len(order) and order[to + step] not in fixed:
                to += step
                places -= queue[order[to]] == queue[n]
            other = order[:at] + order[at + 1:]
            other.insert(to, n)
            now = length(other) if to != at else total + 1
            if now <= total:
                total, order = now, other
        for k in range(len(PACES)):
            run(order, k, True)
        whole += order
    return whole, earlier([ops[n] for n in whole])


def emit(g, T, ops):
    queue = {"v": g.vector, "s": g.scalar, "t": g.tensor, "g": g, "y": g.sync}
    if not PLAN:
        PLAN.extend(arrange(ops))
    ops = [ops[n] for n in PLAN[0]]
    known, clock, waits, marked, seq = {q: {} for q in queue}, [], [], set(), {}
    for n, (op, before) in enumerate(zip(ops, PLAN[1])):
        q, line = op["q"], op["line"]
        seq[line] = seq.get(line, 0) + 1
        op["seq"] = seq[line]
        deps = {}
        for m in before:
            if ops[m]["seq"] > deps.get(ops[m]["line"], (0, 0))[0]:
                deps[ops[m]["line"]] = (ops[m]["seq"], m)
        mine = []
        if q is not None:
            for ln, (s, m) in sorted(deps.items(), key=lambda e: -e[1][1]):
                if known[q].get(ln, 0) < s:
                    mine.append(m)
                    marked.add(m)
                    for k, val in clock[m].items():
                        known[q][k] = max(known[q].get(k, 0), val)
        waits.append(mine)
        ck = dict(known[q]) if q is not None else {}
        ck[line] = op["seq"]
        clock.append(ck)
    count = {}
    for n, op in enumerate(ops):
        if op["token"] is None and n in marked:
            count[op["q"]] = count.get(op["q"], 0) + 1
            op["token"] = (COUNTER[op["q"]], count[op["q"]])
            op["inc"] = (COUNTER[op["q"]], 1)
    for n, op in enumerate(ops):
        if op["q"] is None:
            continue
        e = queue[op["q"]]
        for m in waits[n]:
            e.wait_ge(T.sem[ops[m]["token"][0]], ops[m]["token"][1])
        ins = op["fn"](e)
        if op["inc"] is not None:
            ins.then_inc(T.sem[op["inc"][0]], op["inc"][1])


def rank_program(g, core, T, topo):
    rank = T.rank_of(core)
    if rank is None:
        return
    ops = []
    totals = {"sent": 0, "stored": 0}

    def A(name, lo=0, hi=None, step=1):
        hi = T[name].shape[1] if hi is None else hi
        if step < 0:
            ap = T[name][:, hi - 1::-1] if lo == 0 else T[name][:, hi - 1:lo - 1:-1]
        elif step == 1:
            ap = T[name][:, lo:hi]
        else:
            ap = T[name][:, lo:hi:step]
        n, narrow = len(range(lo, hi, abs(step))), SCRATCH[name][2] in ("bfloat16", "uint16")
        if name == "ps":
            return (ap, [], [(name, lo // 512 * 512, (hi + 511) // 512 * 512)], n, narrow)
        return (ap, [(name, lo, hi)], [], n, narrow)

    def part(view, *names):
        return (view[0], [(k, 0, 1) for k in names], []) + view[3:]

    def ind(win, off):
        return (win[0].indirect(off[0]), win[1] + off[1], [], 16 * off[3], None)

    def val(s):
        return s[0] if isinstance(s, tuple) else s

    def rec(q, fn, outs, ins, time, hold=None, token=None, inc=None, line=None, after=()):
        rd, wr = [], []
        for o in outs:
            wr += o[1] + o[2]
        for i in ins:
            if isinstance(i, tuple):
                rd += i[1]
                wr += i[2]
        ops.append({"q": q, "fn": fn, "rd": rd, "wr": wr, "token": token, "inc": inc, "line": line or q,
                    "time": time, "hold": time if hold is None else hold, "after": after})

    def span(a, *others, rate=None):
        if a[4] is None:
            return 52 + a[3] * GATHER * CYCLE
        if rate is None:
            rate = 0.5 if a[4] and all(o[4] for o in others) else 1.0
        return CALL + a[3] * rate * CYCLE

    def tt(o, a, b, op):
        rec("v", lambda e: e.tensor_tensor(o[0], a[0], b[0], op), [o], [a, b], span(a, rate=1.0 if a[2] else 2.0))

    def ts(o, a, s1, op0, s2=None, op1=None):
        if op1 is None:
            rec("v", lambda e: e.tensor_scalar(o[0], a[0], val(s1), None, op0), [o], [a, s1], span(a, o))
        else:
            rec("v", lambda e: e.tensor_scalar(o[0], a[0], val(s1), val(s2), op0, op1), [o], [a, s1, s2], span(a, o))

    def cp(o, a):
        rec("v", lambda e: e.tensor_copy(o[0], a[0]), [o], [a], span(a, o))

    def total(o, a):
        rec("v", lambda e: e.tensor_reduce(o[0], a[0], AxisListType.X, OP.add), [o], [a], span(a, rate=1.0))

    def scatter(win, off, a):
        rec("v", lambda e: e.tensor_copy(win[0].indirect(off[0]), a[0]), [win], [off, a], 50 + a[3] * SCATTER * CYCLE)

    def fill(o, c):
        rec("v", lambda e: e.memset(o[0], c), [o], [], span(o))

    def scan(o, d0, d1, init, op0, op1):
        rec("v", lambda e: e.tensor_tensor_scan(o[0], d0[0], d1[0], val(init), op0, op1), [o], [d0, d1, init], span(o, d0, d1))

    def turn(o, a):
        rec("v", lambda e: e.transpose(o[0], a[0]), [o], [a], span(a, o))

    def quant(q, s, a):
        rec("v", lambda e: e.quantize_mx(q[0], s[0], a[0]), [q, s], [a], 12 + 0.22 * a[3])

    def act(o, a, func=AF.Copy, bias=None, scale=1.0, acc=None):
        def fn(e):
            kw = {}
            if bias is not None:
                kw["bias"] = val(bias)
            if scale != 1.0:
                kw["scale"] = scale
            if acc is not None:
                kw["accum_out"] = acc[0]
            return e.activation(o[0], a[0], func, **kw)
        rec("s", fn, [o] + ([acc] if acc is not None else []), [a, bias], span(a, rate=1.0) + (32 if acc else 12))

    def mm(bank, wq, ws, b, xq, xs, lo=0, hi=C):
        o, l, ls = A("ps", 512 * bank, 512 * bank + hi - lo), A(wq, 128 * b, 128 * b + 128), A(ws, 128 * b, 128 * b + 128)
        r, rs = A(xq, lo, hi), A(xs, lo, hi)
        rec("t", lambda e: e.matmul_mx(o[0], l[0], ls[0], r[0], rs[0], True, True), [o], [l, ls, r, rs], (hi - lo + 16) * CYCLE)

    def iota(o, pattern, base, mult):
        if o[1][0][0] != "ci":
            rec("g", lambda e: e.iota(o[0], pattern, base, mult, allow_small_or_imprecise_dtypes=True), [o], [], 130 + 2 * o[3] * CYCLE)
        else:
            rec("g", lambda e: e.iota(o[0], pattern, base, mult), [o], [], 130 + 2 * o[3] * CYCLE)

    def load(q, view, dst, src, sem):
        rec(q, lambda e: e.dma_start(dst, src), [view], [], LOCAL, 50, (sem, 16), (sem, 16), sem)

    def store(q, dst, src, view):
        totals["stored"] += 16
        rec(q, lambda e: e.dma_start(dst, src), [], [view], LOCAL, 50, ("stored", 0), ("stored", 16), "st%d" % totals["stored"])

    def send(peer, dst, src, name, sem):
        rid, pid = topo.addr(peer)[:2]
        totals["sent"] += len(topo.engines(core, peer))
        rec("g", lambda e: e.remote_dma(dst, src, T.sem[sem], T.sem.sent, pid, rid, topo.mask(core, peer)), [], [A(name)],
            REMOTE, 100, ("sent", 0), None, "tx%d" % totals["sent"])

    def arrive(names, sem, n, more=0.0):
        rec(None, None, [A(k) for k in names], [], more, 0, (sem, n), None, sem, [len(ops) - 1])

    def bank(b, lo=0, hi=C):
        return A("ps", 512 * b + lo, 512 * b + hi)

    def H(name, h, base=0, first=0, step=1):
        return A(name, base + 128 * h + first, base + 128 * h + 128, step)

    def F(k, n=1):
        return A("cf", k, k + n)

    def own(name, k, h, lo=0, hi=128):
        return A(name, BLOCK * k + 256 * h + lo, BLOCK * k + 256 * h + hi)

    def win(name, k, h, hi=128):
        return A(name, BLOCK * k + 128 * h, BLOCK * k + 256 * h + hi)

    for h in range(2):
        load("y", A("xin", 512 * h, 512 * h + 512), T.xin[:, 512 * h:512 * h + 512], T.x[:, 512 * h:512 * h + 512], "ldx%d" % h)
    load("s", A("uin"), T.uin[:], T.u[:], "ldu")
    load("y", A("qw"), T.qw[:].bitcast(dt.uint8), T.wc[:], "ldw")
    load("y", A("sw"), T.sw[:], T.ws[:], "lds")
    load("y", A("vin"), T.vin[:], T.v[:], "ldv")
    for op in ops[-3:]:
        op["rd"] = A("xin")[1] + A("uin")[1]
    quant(A("qu"), A("su"), A("uin"))
    quant(A("qv"), A("sv"), A("vin"))
    for h in range(2):
        quant(H("qx0", h), H("sx0", h), A("xin", 512 * h, 512 * h + 512))

    i16, p32, cut, invk, i4, inv4, b256, ifr, odd16 = [F(k) for k in range(9)]
    whole, kfr, two, zero = F(10), F(64, 16), F(80, 16), F(96, 16)
    spread, turned, lines, twice, columns = A("cl", 0, 16), A("cl", 16, 24), A("cl", 24, 31), A("cl", 32, 48), A("cl", 48, 49)
    iota(A("ci", 16, 17), [[0, 1]], 0, 1)
    iota(A("posd"), [[0, 8], [1, 16]], 0, 0)
    iota(A("ci", 0, 16), [[16, 2], [32, 4], [0, 2]], 0, 0)
    iota(A("ci", 32, 48), [[1, 16]], 0, 0)
    iota(A("jrow"), [[1, 256]], 0, 0)
    iota(A("pos4"), [[0, 8], [1, 4]], 0, 0)
    ts(A("ci", 17, 18), A("ci", 16, 17), 15, OP.bitwise_and)
    ts(A("ci", 18, 19), A("ci", 16, 17), 31, OP.bitwise_and)
    ts(A("ci", 19, 20), A("ci", 16, 17), 2, OP.logical_shift_right, 3, OP.bitwise_and)
    ts(A("ci", 20, 21), A("ci", 16, 17), 3, OP.bitwise_and)
    cp(F(0, 2), A("ci", 17, 19))
    cp(i4, A("ci", 19, 20))
    ts(b256, A("ci", 20, 21), 256.0, OP.mult)
    tt(odd16, p32, i16, OP.subtract)
    iota(A("wide"), [[32, 16], [1, 16]], 0, 0)
    act(A("wide"), A("wide"), AF.Identity, odd16)
    iota(A("ci", 48, 64), [[16, 8], [0, 2]], 0, 0)
    ts(twice, A("ci", 48, 64), i16, OP.add)
    ts(cut, i16, 8.0, OP.subtract, -2 * ROUND, OP.mult)
    ts(cut, cut, -0.498046875, OP.add, 1.0, OP.min)
    ts(cut, cut, -ROUND, OP.max)
    ts(A("ci", 0, 16), A("ci", 0, 16), p32, OP.add)
    ts(A("ci", 0, 16), A("ci", 0, 16), 127, OP.bitwise_and)
    fill(A("dj"), 0.5)
    fill(part(A("dj", 0, 512, 16), "dj0"), 0.0)
    fill(part(A("dj", 9, 512, 16), "dj9"), 1.0)
    fill(part(A("dj", 10, 512, 16), "dj10"), -1.0)
    for h in range(2):
        ts(part(A("dj", 256 * h + 8, 256 * h + 256, 16), "dj8%d" % h), A("ci", 0, 16), 128.0 * h, OP.add, 0.5, OP.mult)
    for op in ops[-5:]:
        op["rd"] = op["rd"] + [("dj", 0, 512)]
    ts(A("ci", 64, 65), A("ci", 16, 17), 4, OP.logical_shift_right, 1, OP.bitwise_and)
    ts(A("ci", 65, 66), A("ci", 16, 17), 1, OP.bitwise_and)
    ts(A("ci", 66, 67), A("ci", 16, 17), 1, OP.logical_shift_right, 3, OP.bitwise_and)
    cp(F(13), A("ci", 66, 67))
    tt(F(11), A("ci", 64, 65), A("ci", 65, 66), OP.not_equal)
    tt(F(12), A("ci", 64, 65), A("ci", 65, 66), OP.is_gt)
    ts(A("ci", 67, 68), F(12), 3.0, OP.mult, A("cf", 13, 14), OP.add)
    ts(A("ci", 67, 68), A("ci", 67, 68), 3, OP.bitwise_and)
    ts(F(11), F(11), 128.0, OP.mult, odd16, OP.add)
    ts(F(12), A("ci", 67, 68), 32.0, OP.mult, 10.0, OP.add)
    ts(columns, F(12), F(11), OP.add)
    ts(turned, A("ci", 32, 40), 16.0, OP.mult, 10.0, OP.add)
    ts(A("posd"), A("posd"), i16, OP.subtract)
    ts(A("kd"), A("posd"), 1.0, OP.is_equal, HOLD, OP.mult)
    ts(A("kd2"), A("posd"), 2.0, OP.is_ge)
    tt(A("kd"), A("kd"), A("kd2"), OP.add)
    ts(invk, i16, 15.0, OP.is_equal, 1.0 / HOLD, OP.max)
    ts(A("pos4"), A("pos4"), i4, OP.subtract)
    ts(A("k4", 0, 32), A("pos4"), 1.0, OP.is_equal, HOLD, OP.mult)
    ts(A("k42"), A("pos4"), 2.0, OP.is_ge)
    tt(A("k4", 0, 32), A("k4", 0, 32), A("k42"), OP.add)
    for n in (32, 64, 128):
        act(A("k4", n, 2 * n), A("k4", 0, n))
    ts(inv4, i4, 3.0, OP.is_equal, 1.0 / HOLD, OP.max)
    fill(part(A("cf", 81, 96, 2), "odd"), 4096.0)
    fill(part(A("cf", 80, 96, 2), "even"), 2.0 ** -9)
    fill(zero, 0.0)
    scan(A("pw"), part(two, "odd", "even"), zero, 2.0 ** 9, OP.mult, OP.add)
    cp(spread, A("ci", 32, 48))
    ts(A("dmx"), A("posd"), 0.0, OP.is_equal)
    tt(own("sa", 0, 1), ind(A("pw"), A("cl", 0, 8)), A("dmx"), OP.mult)
    for k, h in ((0, 0), (1, 0), (1, 1)):
        act(own("sa", k, h), own("sa", 0, 1))
    fill(A("sa", 0, BLOCK + 1, BLOCK), 0.0)
    act(A("af", 256, 384), A("jrow", 0, 128), scale=0.0)
    for name, first, n in (("kp7", 2, 7), ("kp10", 10, 10), ("kp19", 19, 19)):
        fill(A(name), 1.0)
        fill(A(name, first, None, n), 0.0)
    fill(A("ai", 57, 58), 0)
    ts(whole, A("ci", 17, 18), 0.0, OP.is_equal, float(C), OP.mult)
    for name, blocks in (("jr", 4), ("sa", 5), ("wz", 3)):
        for k in range(blocks):
            act(A(name, BLOCK * k + 128, BLOCK * k + 256), A("jrow", 0, 128), scale=float(name == "jr"))
    act(A("jfr"), A("jrow"), scale=1.0 / C)
    ts(ifr, i16, 1.0 / C, OP.mult)
    ts(kfr, A("ci", 32, 48), 16.0 / C, OP.mult)
    fill(A("ones"), 1.0)
    fill(A("keep"), 1.0)
    fill(A("keep", 0, 256, 32), 0.0)
    act(part(A("z"), "z", "z00", "z10", "z01", "z11"), A("ones"), scale=0.0)
    fill(A("ssrt", 0, 16), 0.0)
    fill(A("same", 0, 1), 1.0)
    fill(A("same", 1, 257, 255), 0.0)
    for b in range(4):
        o = A("et", 512 * b, 512 * b + 512)
        rec("g", lambda e, o=o, b=b: e.affine_select(o[0], T.ones[:], [[1, 512]], OP.is_equal, 0.0, -b, -4), [o], [A("ones")], 170 + 1024 * CYCLE)
        quant(A("qe", 128 * b, 128 * b + 128), A("se", 128 * b, 128 * b + 128), o)
    for name, n in (("mb4", 4), ("mb16", 16)):
        act(A(name), A("ones"), scale=BIG)
        fill(A(name, 0, 512, n), -BIG)
    fill(A("mbm"), BIG)
    fill(A("mbm", 0, 112, 16), -BIG)
    fill(A("mbm", 1, 112, 17), -BIG)
    for h in range(4):
        act(A("tab", MID + 512 * h, MID + 512 * h + 512), A("ones"), scale=-BIG)
    ts(F(112, 7), A("ci", 33, 40), i16, OP.is_gt)
    ts(F(120, 7), A("ci", 33, 40), -1.0, OP.mult, 15.0, OP.add)
    tt(F(112, 7), F(112, 7), F(120, 7), OP.mult)
    ts(lines, F(112, 7), i16, OP.add, 16.0, OP.mult)

    def L(k, h, lo=0, hi=128):
        if k == 0:
            return A("par", 16 * h, 16 * h + 8)
        return A("lst", 16 * k + 8 * h + lo // 16, 16 * k + 8 * h + hi // 16)

    def wrap(out, held, row):
        name, lo, hi = held[1][0]
        scan(held, A("kd", 0, hi - lo), row, 0.0, OP.mult, OP.max)
        ts(out, A(name, lo + 15, hi, 16), invk, OP.mult)

    def path_sums(name, blocks, h, out):
        for k in range(STEPS):
            tt(out if k == STEPS - 1 else own(name, blocks[k + 2], h), ind(win(name, blocks[k + 1], h), L(max(k - 1, 0), h)), own(name, blocks[k], h), OP.add)

    def sweep(name, base, first, last, out=None):
        for a in range(first, last, 32):
            run = A(name, base + a, base + a + 32)
            tt(out if out and a + 32 == last else run, ind(A(name, base, base + a), L(STEPS, 0, a, a + 32)), run, OP.add)

    def W(k, n=1):
        return A("iw", 16 * k, 16 * (k + n))

    def V(k, n=1):
        return A("iv", 16 * k, 16 * (k + n))

    def tab(region, lo, hi, step=1):
        return A("tab", region + lo, region + hi, step)

    for t in range(R):
        peer = T.cores[rank ^ (1 << t)]
        qx, sx, qp, sp, ol, lp = ["%s%d" % (k, t) for k in ("qx", "sx", "qp", "sp", "ol", "lp")]
        engines = len(topo.engines(peer, core))
        for h in (1, 0):
            mm(4 + h, "qu", "su", 0, qx, sx, 128 * h, 128 * h + 128)
            for lo, n in ((0, 128), (128, 16)):
                ts(A("r1", 144 * h + lo, 144 * h + lo + n), bank(4 + h, 0, n), 0.0, OP.is_gt, cut, OP.min)
            for k in range(2):
                turn(H("r2", 2 * h + k), A("r1", 144 * h + 16 * k, 144 * h + 16 * k + 128))
                scan(H("r3", 2 * h + k), part(H("dj", 2 * h + k), "dj0", "dj80", "dj81", "dj9", "dj10"), H("r2", 2 * h + k), 0.0, OP.mult, OP.add)
            ts(A("par", 16 * h, 16 * h + 16), ind(A("r3", 256 * h, 256 * h + 256), columns), -1.0, OP.mult)
            act(H("r4", h), ind(H("r3", 2 * h), turned), scale=-1.0)
            turn(own("jr", 0, h), H("r4", h))
            for op in ops[-10:]:
                op["lead"] = LEAD * h
        send(peer, T[qp][:].bitcast(dt.uint8), T[qx][:].bitcast(dt.uint8), qx, "aq%d" % t)
        send(peer, T[sp][:], T[sx][:], sx, "aq%d" % t)
        arrive([qp, sp], "aq%d" % t, 2 * engines, 2000.0)
        ring = [0] + [1 + k % 3 for k in range(STEPS)]
        for h in range(2):
            for k in range(STEPS):
                act(own("jr", ring[k + 1], h), ind(win("jr", ring[k], h), L(max(k - 1, 0), h)))
                if k != STEPS - 2:
                    lo = 32 * (k == STEPS - 1)
                    wrap(L(k + 1, h, lo), H("hd", h, 256 * k + 256, lo), own("jr", ring[k + 1], h, lo))
            path_sums("sa", [0, 1] + [2 + k % 3 for k in range(STEPS)], h, A("af", 384 * h, 384 * h + 128))
            sweep("af", 256 * h, 128 * h + 32, 128 * h + 128)
        for a in range(32, 128, 32):
            act(own("jr", ring[-1], 1, a, a + 32), ind(win("jr", ring[-1], 1, a), L(STEPS, 1, a, a + 32)))
        wrap(L(STEPS + 1, 1), H("hd", 1, 256 * STEPS + 256), own("jr", ring[-1], 1))
        act(A("af", 128, C), ind(A("af", 0, 128), L(STEPS + 1, 1)))
        for h in range(2):
            name, lo, hi = own("jr", 0, h)[1][0]
            begin = len(ops)
            scan(A("key", 128 * h, 128 * h + 128, -1), A("jfr", 128 * h, 128 * h + 128, -1), A(name, lo, hi, -1), 1.0, OP.min, OP.add)
            keyw = A("wf", 16 + 8 * h, 24 + 8 * h)
            ts(keyw, L(0, h), ifr, OP.add)
            tt(keyw, keyw, F(64 + 8 * h, 8), OP.add)
            for k in range(8 * h, 8 * h + 8):
                act(A("junk", 128 * k, 128 * k + 128), H("key", h), AF.Sign, A("wf", 16 + k, 17 + k), -1.0, A("wf", 32 + k, 33 + k))
            ts(A("rkl", 8 * h, 8 * h + 8), A("wf", 32 + 8 * h, 40 + 8 * h), 127.0, OP.add, 0.5, OP.mult)
            scatter(H("srow", h), A("rkl", 8 * h, 8 * h + 8), A("wide", 0, 128))
            wrap(A("spl", 8 * h, 8 * h + 8), H("shd", h), H("srow", h))
            act(A("pwd", 256 * h, 256 * h + 256), ind(own("jr", 0, h), twice))
            act(H("psrt", h), ind(A("pwd", 256 * h, 256 * h + 256), A("spl", 8 * h, 8 * h + 8)))
            lo, hi = 2 + 127 * h, 128 * h + 128
            scan(A("step", lo, hi), A("psrt", lo - 1, hi - 1), A("psrt", lo, hi), 0.0, OP.max, OP.subtract)
            act(A("same", lo, hi), A("step", lo, hi), AF.Relu, 1.0)
            for op in ops[begin:]:
                op["lead"] = LEAD
        act(A("prow"), ind(A("wide"), L(0, 1)))
        wrap(A("spl", 16, 24), A("prh"), A("prow"))
        for k, lo in enumerate((0, 128, 384)):
            scan(A("seven", lo, lo + 128), A("kp7"), A("af", lo, lo + 128), 0.0, OP.mult, OP.add)
            cp(A("ai", 19 * k, 19 * k + 19), A("seven", lo + 1, lo + 128, 7))
        for h in (1, 0):
            n, lo = 38 - 18 * h, 256 * h
            for m in range(4):
                ts(A("msk", lo + n * m, lo + n * m + n), A("ai", 38 * h, 38 * h + n), 3 * m, OP.logical_shift_right, 0x7007, OP.bitwise_and)
            tt(A("hm", lo, lo + 2 * n), A("msk", lo, lo + 4 * n, 2), A("msk", lo + 1, lo + 4 * n, 2), OP.add)
            scan(A("hm", lo + 128, lo + 128 + 2 * n), A("kp10" if h else "kp19"), A("hm", lo, lo + 2 * n), 0.0 if h else whole, OP.mult, OP.add)
            both, high = A("hm", lo + 128 + n // 2 - 1, lo + 128 + 2 * n, n // 2), A("wf", 48 + 4 * h, 52 + 4 * h)
            ts(high, both, 4096 * ROUND, OP.add, 4096 * ROUND, OP.subtract)
            tt(part(A("z", lo, lo + 256, 64), "z0%d" % h), both, high, OP.subtract)
            act(part(A("z", lo + 32, lo + 256, 64), "z1%d" % h), high, scale=1.0 / 4096)
            scan(A("zb", lo, lo + 256), A("keep"), part(A("z", lo, lo + 256), "z", "z0%d" % h, "z1%d" % h), 0.0, OP.mult, OP.add)
            turn(A("zt", lo, lo + 256), A("zb", lo, lo + 256))
        size = part(A("z", 0, 512, 32), "z00", "z10", "z01", "z11")
        act(A("ssrt", 144, 272), ind(A("zt", 256, 512), A("spl", 8, 16)))
        cp(A("ssrt", 16, 144), ind(A("zt", 0, 256), A("spl", 0, 8)))
        act(A("szp"), ind(A("zt"), A("spl", 16, 24)))
        scan(H("cum", 0), A("ssrt", 15, 143), H("same", 0), -1.0, OP.add, OP.mult)
        scan(A("cum", 128, 256, -1), A("same", 129, 257, -1), A("ssrt", 144, 272, -1), 0.0, OP.mult, OP.subtract)
        ts(own("wz", 0, 0), ind(H("cum", 0), A("rkl", 0, 8)), 1.0, OP.add)
        act(own("wz", 1, 0), ind(H("cum", 0), A("rkl", 0, 8)), AF.Identity, 1.0)
        tt(own("wz", 0, 1), ind(H("cum", 1), A("rkl", 8, 16)), A("szp"), OP.add)
        act(own("wz", 1, 1), own("wz", 0, 1))
        ring = [k % 3 for k in range(STEPS + 2)]
        path_sums("wz", ring, 0, H("pf", 0))
        path_sums("wz", ring, 1, own("wz", ring[-1], 1))
        sweep("pf", 0, 32, 128)
        sweep("wz", BLOCK * ring[-1] + 128, 160, C)
        for lo, hi in ((0, 64), (64, 128), (128, C)):
            if hi == C:
                tt(A("pf", lo, hi), ind(H("pf", 0), L(STEPS + 1, 0, lo, hi)), own("wz", ring[-1], 1, lo - 128, hi - 128), OP.add)
            wrap(A("pll", lo // 16, hi // 16), A("phd", lo, hi), A("pf", lo, hi))
            scatter(A("orow"), A("pll", lo // 16, hi // 16), A("jrow", lo, hi))
        scan(A("ohd"), A("k4"), A("orow"), 0.0, OP.mult, OP.max)
        ts(A(ol), A("ohd", 3, C, 4), inv4, OP.mult, b256, OP.add)
        send(peer, T[lp][:], T[ol][:], ol, "al%d" % t)
        arrive([lp], "al%d" % t, engines)
        for b in range(4):
            mm(b, "qe", "se", b, qp, sp)
            act(A("tp", 256 * b, 256 * b + 256), bank(b))
        if t == R - 1:
            for h in range(2):
                act(H("po", h), own("jr", 0, h))
            store("y", T.op[:], T.po[0:128:16, :], A("po"))
        for k in range(2):
            ts(V(k), A("pll"), -float(k), OP.add)
            tt(V(2 + k), V(k), size, OP.add)
        ts(V(4, 4), V(0, 4), 2, OP.arith_shift_right)
        ts(V(8, 4), V(0, 4), 4, OP.arith_shift_right)
        tt(W(2, 2), V(6, 2), V(4, 2), OP.is_gt)
        tt(W(4, 2), V(10, 2), V(8, 2), OP.is_gt)
        tt(W(6), V(7), V(4), OP.subtract)
        tt(W(7), V(11), V(8), OP.subtract)
        tt(W(8, 2), W(2, 2), W(4, 2), OP.add)
        ts(W(10), W(8), float(S4 - RAW), OP.mult, float(RAW - S16), OP.add)
        ts(W(11), W(9), float(P4 - RAW), OP.mult)
        tt(W(22), W(10), V(0), OP.add)
        tt(W(23), W(11), V(3), OP.add)
        ts(W(12), W(6), 2.0, OP.is_equal)
        ts(W(18), W(7), 16.0, OP.mult, 3.0, OP.add)
        tt(W(13), W(6), W(18), OP.is_equal)
        ts(W(14), W(7), 2.0, OP.is_ge)
        ts(W(15), V(4), 4.0, OP.mult, float(S4 - MID + 4), OP.add)
        ts(W(16), V(8), 16.0, OP.mult, float(PAIR - MID), OP.add)
        ts(W(20), V(8), 16.0, OP.mult, 15.0, OP.add)
        ts(W(19), V(8), -17.0, OP.mult, 222.0, OP.add)
        tt(W(20), W(20), W(19), OP.min)
        tt(W(17), W(20), V(11), OP.add)
        tt(W(12, 3), W(12, 3), W(15, 3), OP.mult)
        tt(W(21), W(12), W(13), OP.add)
        tt(W(24), W(21), W(14), OP.add)
        cp(A("idx", 0, 32), W(22, 2))
        cp(A("idx", 32, 48), W(24))
        for h in range(2):
            for q in (2 * h, 2 * h + 1):
                (act if q % 2 else cp)(A("bt", 256 * q, 256 * q + 256), ind(A("tp"), A(lp, 16 * q, 16 * q + 16)))
            quant(H("qf", h), H("sf", h), A("bt", 512 * h, 512 * h + 512))
            for b in range(4):
                mm(4 * h + b, "qw", "sw", b, "qf", "sf", 128 * h, 128 * h + 128)
                lo = 256 * b + 128 * h
                act(tab(RAW, lo, lo + 128), bank(4 * h + b, 0, 128), scale=0.03125)
                scan(tab(S16, lo, lo + 128, -1), A("mb16", 0, 128), tab(RAW, lo, lo + 128, -1), -BIG, OP.min, OP.max)
        for b in range(4):
            mm(b, "qe", "se", b, qx, sx)
        for region, mask, step in ((S4, "mb4", -1), (P4, "mb4", 1), (P16, "mb16", 1)):
            n = 128 if region == S4 else 512
            for lo in range(0, 1024, n):
                scan(tab(region, lo, lo + n, step), A(mask, 0, n), tab(RAW, lo, lo + n, step), -BIG, OP.min, OP.max)
        tt(tab(PAIR, 0, 1024, 16), tab(S4, 4, 1024, 16), tab(S4, 8, 1024, 16), OP.max)
        for b in range(4):
            act(A("mg", 112 * b, 112 * b + 112), ind(tab(S16, 256 * b, 256 * b + 256), lines))
        for b in range(4):
            scan(tab(MID, 256 * b + 16, 256 * b + 128), A("mbm"), A("mg", 112 * b, 112 * b + 112), -BIG, OP.min, OP.max)
        for op in ops[-9:]:
            op["lead"] = LEAD / 3
        for b in range(4):
            lo, hi = 256 * b, 256 * b + 256
            act(A("m1", lo, hi), ind(A("tab", S16 + lo, RAW + hi), A("idx", 0, 16)))
            tt(A("m2", lo, hi), ind(A("tab", RAW + lo, P16 + hi), A("idx", 16, 32)), A("m1", lo, hi), OP.max)
        for h in (1, 0):
            for b in range(4):
                lo = 256 * b
                if t < R - 1:
                    tt(H("m3", h, lo), ind(A("tab", MID + lo, S4 + lo + 256), A("idx", 32 + 8 * h, 40 + 8 * h)), H("m2", h, lo), OP.max)
                elif h == 1:
                    tt(A("m3", lo, lo + 256), ind(A("tab", MID + lo, S4 + lo + 256), A("idx", 32, 48)), A("m2", lo, lo + 256), OP.max)
                tt(part(A("xn", 512 * h + b, 512 * h + 512, 4), "xn%d%d" % (h, b)), bank(b, 128 * h, 128 * h + 128), H("m3", h, lo), OP.add)
            quant(H("qx%d" % (t + 1), h), H("sx%d" % (t + 1), h), part(A("xn", 512 * h, 512 * h + 512), *["xn%d%d" % (h, b) for b in range(4)]))

    for h in range(2):
        lo, hi = 128 * h, 128 * h + 128
        mm(4 + h, "qv", "sv", 0, "qx3", "sx3", lo, hi)
        store("y", T.oc[:, 4 * lo:4 * hi], T.qx3[:, lo:hi].bitcast(dt.uint8), H("qx3", h))
        cp(H("yo", h), bank(4 + h, 0, 128))
        store("y", T.y[:, lo:hi], T.yo[:, lo:hi], H("yo", h))
    for k in range(4):
        store("s", T.osc[4 * k:4 * k + 4, :], T.sx3[32 * k:32 * k + 4, :], A("sx3"))
    emit(g, T, ops)
    g.sync.wait_ge(T.sem.stored, totals["stored"])
    g.wait_ge(T.sem.sent, totals["sent"])
